import numpy as np
import ml_dtypes


def mxq(x, axis, fmt="e4m3"):
    dtype, down = {"e4m3": (ml_dtypes.float8_e4m3fn, 7), "e5m2": (ml_dtypes.float8_e5m2, 14)}[fmt]
    v = np.moveaxis(np.asarray(x, np.float32).astype(ml_dtypes.bfloat16).astype(np.float64), axis, -1)
    blocks = v.reshape(v.shape[:-1] + (-1, 32))
    amax = np.abs(blocks).max(-1, keepdims=True)
    byte = np.maximum(np.where(amax > 0, np.frexp(amax)[1] - 1 + 127, 0) - down, 1)
    scale = np.exp2(byte - 127.0)
    codes = (blocks / scale).astype(np.float32).astype(dtype).astype(np.float64)
    return np.moveaxis((codes * scale).reshape(v.shape), -1, axis)


WIDE = False


def mx_kscale(k):
    if not WIDE:
        return np.ones(k)
    levels = np.array([10, -10, 5, -5, 0])
    if k % 512:
        return np.exp2(np.random.permutation(np.resize(levels, k // 32))).repeat(32)
    a = np.empty((k // 512, 16))
    for p in range(k // 512):
        a[p, :8] = np.random.permutation(np.resize(levels, 8))
        for g in range(8):
            far = levels[np.abs(levels - a[p, g]) >= 10]
            a[p, g + 8] = far[np.random.randint(len(far))]
    return np.exp2(a.ravel()).repeat(32)


def f64(x):
    return np.asarray(x).astype(np.float64)


def striped(idx):
    return np.tile(idx.reshape(-1, 16).T, (8, 1)).astype(np.uint16)


def unstriped(offs):
    return offs[:16].T.reshape(-1).astype(np.int64)


E2M1 = np.array([0.0, 0.5, 1.0, 1.5, 2.0, 3.0, 4.0, 6.0, -0.0, -0.5, -1.0, -1.5, -2.0, -3.0, -4.0, -6.0])


def pack_weight(w, fmt):
    k, n = w.shape
    w = f64(np.asarray(w, np.float32).astype(ml_dtypes.bfloat16)).reshape(k // 32, 32, n)
    amax = np.abs(w).max(1)
    if fmt == "e4m3":
        byte = np.frexp(amax)[1] - 1 + 127 - 7
    else:
        mant, ex = np.frexp(amax / 6.0)
        byte = np.where(mant > 0.5, ex, ex - 1) + 127
    byte = np.clip(np.where(amax > 0, byte, 1), 1, 254)
    scaled = (w * np.exp2(127.0 - byte)[:, None, :]).reshape(k, n).astype(np.float32)
    by_word = np.ascontiguousarray(scaled.reshape(k // 512, 128, 4, n).transpose(0, 1, 3, 2))
    if fmt == "e4m3":
        words = by_word.astype(ml_dtypes.float8_e4m3fn).view(np.uint8)
    else:
        c = by_word.astype(ml_dtypes.float4_e2m1fn).view(np.uint8) & 0xF
        words = (c[..., 0::2] | (c[..., 1::2] << 4)).reshape(k // 512, 128, 2 * n)
    return np.ascontiguousarray(words), np.ascontiguousarray(byte.astype(np.uint8).reshape(k // 512, 16, n))


def unpack_weight(words, scales, fmt):
    g, _, n = scales.shape
    words = np.ascontiguousarray(words).reshape(g, 128, n, -1)
    if fmt == "e4m3":
        vals = words.view(ml_dtypes.float8_e4m3fn).astype(np.float64)
    else:
        nib = np.empty((g, 128, n, 4), np.uint8)
        nib[..., 0::2] = words & 0xF
        nib[..., 1::2] = words >> 4
        vals = E2M1[nib]
    vals = vals * np.repeat(np.exp2(scales.astype(np.float64) - 127.0), 8, axis=1)[..., None]
    return vals.transpose(0, 1, 3, 2).reshape(g * 512, n)


def gelu(v):
    return 0.5 * v * (1.0 + np.tanh(np.sqrt(2.0 / np.pi) * (v + 0.044715 * v**3)))


def bf(x):
    return np.asarray(x, np.float32).astype(ml_dtypes.bfloat16)


def planes(Y):
    n, m = Y.shape
    b = f64(bf(Y)).reshape(n // 32, 32, m)
    amax = np.abs(b).max(1)
    byte = np.clip(np.where(amax > 0, np.frexp(amax)[1] - 1 + 127 - 7, 1), 1, 254)
    codes = (b * np.exp2(127.0 - byte)[:, None, :]).reshape(n, m).astype(np.float32).astype(ml_dtypes.float8_e4m3fn).view(np.uint8)
    words = codes.reshape(n // 512, 128, 4, m).transpose(0, 1, 3, 2)
    return np.ascontiguousarray(words), np.ascontiguousarray(byte.astype(np.uint8).reshape(n // 512, 16, m))


K, T, S, T2, H, N = 512, 2048, 1024, 2048, 1024, 384


def setup_inputs():
    n = np.random.standard_normal
    s = mx_kscale(K)[:, None]
    u = mx_kscale(H)[:, None]
    tab_words, tab_scales = pack_weight(n((K, T)) * s, "e4m3")
    w1 = (n((K, H)) / np.sqrt(K) * u.T / s).astype(np.float32)
    w2_words, w2_scales = pack_weight(n((K, H)) / np.sqrt(K) * u.T / s, "e2m1")
    w3 = (n((H, N)) / np.sqrt(H) / u).astype(np.float32)
    w4_words, w4_scales = pack_weight(n((H, N)) / np.sqrt(H) / u, "e4m3")
    return {
        "tab_words": tab_words, "tab_scales": tab_scales,
        "offs": striped(np.random.permutation(T)[:S]),
        "offs2": striped(np.random.permutation(T2)[:S]),
        "w1": w1, "w2_words": w2_words, "w2_scales": w2_scales,
        "page0": (n((H, T2)) * u).astype(np.float32),
        "wgs": np.exp(0.3 * n((128, S))).astype(np.float32),
        "w3": w3, "w4_words": w4_words, "w4_scales": w4_scales,
    }


def reference(tab_words, tab_scales, offs, offs2, w1, w2_words, w2_scales, page0, wgs, w3, w4_words, w4_scales):
    v = unpack_weight(tab_words, tab_scales, "e4m3")[:, unstriped(offs)]
    a = mxq(f64(w1), 0, "e4m3").T @ v
    b = unpack_weight(w2_words, w2_scales, "e2m1").T @ v
    h = np.maximum(a, b)
    page = f64(page0).copy()
    page[:, unstriped(offs2)] = np.tile(f64(wgs), (H // 128, 1)) * h
    words, scales = planes(page)
    pq = mxq(page, 0, "e4m3")
    f = mxq(f64(w3), 0, "e4m3").T @ pq
    d = unpack_weight(w4_words, w4_scales, "e4m3").T @ pq
    y = f / (1.0 + np.square(d))
    return y, page, words, scales

@@ -1,0 +1,317 @@
+from contextlib import ExitStack
+
+import concourse.mybir as mybir
+
+K, T, S, T2, H, N = 512, 2048, 1024, 2048, 1024, 384
+FLOPS = 2 * (2 * K * H * S + 2 * H * N * T2)
+
+F32 = mybir.dt.float32
+BF16 = mybir.dt.bfloat16
+I32 = mybir.dt.int32
+U32 = mybir.dt.uint32
+U16 = mybir.dt.uint16
+U8 = mybir.dt.uint8
+FP8X4 = mybir.dt.float8_e4m3fn_x4
+FP4X4 = mybir.dt.float4_e2m1fn_x4
+ALU = mybir.AluOpType
+ACT = mybir.ActivationFunctionType
+
+P = 128
+PACK = 4
+PASS = P * PACK
+BANK = 512
+GROUPS = H // PASS
+HALVES = S // BANK
+CHUNKS = T2 // BANK
+NT = N // P
+EARLY_UNITS = 4
+TAB_AT = PASS + GROUPS * N + 8 * S
+
+
+def tile_list_chart_tile_planes_kernel(
+    tc, tab_words, tab_scales, offs, offs2, w1, w2_words, w2_scales, page0, wgs, w3, w4_words, w4_scales,
+    out_0, out_1, out_2, out_3,
+):
+    nc = tc.nc
+    with ExitStack() as ctx:
+        keep = ctx.enter_context(tc.tile_pool(name="keep", bufs=1))
+        ring = ctx.enter_context(tc.tile_pool(name="ring", bufs=4))
+        placed = ctx.enter_context(tc.tile_pool(name="placed", bufs=1))
+        psum = ctx.enter_context(tc.psum_pool(name="psum", bufs=8))
+
+        def held(shape, dtype, name):
+            return keep.tile(shape, dtype, name=name, align_bytes=64)
+
+        idx = held([P, S // 16], U16, "idx")
+        idx2 = held([P, S // 16], U16, "idx2")
+        tab_w = held([P, T], U32, "tab_w")
+        tab_s = placed.tile([P, T], U8, name="tab_s", offset=TAB_AT, align_bytes=64)
+        w2_w = held([P, 2 * H], U8, "w2_w")
+        w2_s = held([P, H], U8, "w2_s")
+        w4_w = held([P, GROUPS, N], U32, "w4_w")
+        w4_s = held([P, GROUPS, N], U8, "w4_s")
+        gain = [held([P, S], F32, "gain0"), None]
+        gain_rest = held([P, PACK - 1, S], F32, "gain_rest")
+        page = [held([P, T2], F32, f"page{i}") for i in range(GROUPS * PACK)]
+        page_rows = page0.rearrange("(g p t) m -> g t p m", g=GROUPS, t=PACK)
+        out_rows = out_1.rearrange("(g p t) m -> g t p m", g=GROUPS, t=PACK)
+        wgs_rows = wgs.rearrange("(q t) j -> q t j", t=PACK)
+
+        def raw_tile(shape, dtype, name):
+            return ring.tile(shape, dtype, name=name, tag="wide", align_bytes=64)
+
+        def grouped_tile(shape, name):
+            return ring.tile(shape, BF16, name=name, tag="grouped", align_bytes=64)
+
+        warm = held([P, 1], F32, "warm")
+        warm_out = held([P, 1], F32, "warm_out")
+        nc.vector.memset(tab_s[:].bitcast(I32), 0)
+        nc.gpsimd.memset(warm[:], 1.0)
+        nc.gpsimd.memset(w2_s[:].bitcast(I32), 0)
+        nc.vector.memset(w4_s[:].rearrange("p a n -> p (a n)").bitcast(I32), 0)
+        w1_raw = []
+        for g in range(GROUPS):
+            w1_raw.append(raw_tile([P, PACK, PASS], F32, f"w1_raw{g}"))
+        w1_cols = w1.rearrange("(p j) (g c) -> g p j c", j=PACK, g=GROUPS)
+        nc.sync.dma_start(w1_raw[0][:], w1_cols[0])
+        nc.sync.dma_start(idx[:], offs)
+        for q in range(4):
+            nc.sync.dma_start(tab_s[32 * q : 32 * q + 4, :].bitcast(I32), tab_scales[0, 4 * q : 4 * q + 4, :].bitcast(I32))
+        nc.sync.dma_start(w2_w[:].bitcast(I32), w2_words[0].bitcast(I32))
+        nc.sync.dma_start(tab_w[:].bitcast(I32), tab_words[0].rearrange("p n t -> p (n t)").bitcast(I32))
+        for q in range(4):
+            nc.gpsimd.dma_start(w2_s[32 * q : 32 * q + 4, :].bitcast(I32), w2_scales[0, 4 * q : 4 * q + 4, :].bitcast(I32))
+        nc.scalar.activation(warm_out[:], warm[:], ACT.Abs_reciprocal_sqrt)
+        nc.sync.dma_start(page[0][:], page_rows[0, 0])
+        nc.sync.dma_start(idx2[:], offs2)
+        for q in range(4):
+            nc.sync.dma_start(gain[0][32 * q : 32 * q + 32, :], wgs_rows[:, 0, :])
+        nc.sync.dma_start(page[1][:], page_rows[0, 1])
+        for q in range(4):
+            nc.sync.dma_start(gain_rest[32 * q : 32 * q + 32, :, :], wgs_rows[:, 1:PACK, :])
+        nc.sync.dma_start(w1_raw[1][:], w1_cols[1])
+        nc.sync.dma_start(page[2][:], page_rows[0, 2])
+        w3_rows = w3.rearrange("(a p j) n -> a p j n", a=GROUPS, j=PACK)
+        w3_raw = []
+        for a in range(GROUPS):
+            w3_raw.append(raw_tile([P, PACK, N], F32, f"w3_raw{a}"))
+            nc.sync.dma_start(w3_raw[a][:], w3_rows[a])
+        for i in range(3, GROUPS * PACK):
+            nc.sync.dma_start(page[i][:], page_rows[i // PACK, i % PACK])
+        nc.sync.dma_start(w4_w[:].bitcast(I32), w4_words.rearrange("a p n t -> p a (n t)").bitcast(I32))
+        for q in range(4):
+            nc.sync.dma_start(
+                w4_s[32 * q : 32 * q + 4, :, :].bitcast(I32),
+                w4_scales[:, 4 * q : 4 * q + 4, :].rearrange("a r n -> r a n").bitcast(I32),
+            )
+
+        def gain_of(t):
+            return gain[0][:] if t == 0 else gain_rest[:, t - 1, :]
+
+        v_w = [held([P, BANK], U32, f"v_w{u}") for u in range(HALVES)]
+        v_s = [held([P, BANK], U8, f"v_s{u}") for u in range(HALVES)]
+        w1_c = [held([P, PASS], U32, f"w1_c{g}") for g in range(GROUPS)]
+        w1_s = [None, None]
+        w2_dw = [held([P, 2 * PASS], U8, f"w2_dw{g}") for g in range(GROUPS)]
+        w2_ds = [held([P, PASS], U8, f"w2_ds{g}") for g in range(GROUPS)]
+        cols16 = BANK // 16
+
+        def gather_scales(u):
+            nc.vector.tensor_copy(v_s[u][:], tab_s[:].indirect(idx[:, u * cols16 : (u + 1) * cols16]))
+
+        def gather_words(u):
+            nc.vector.tensor_copy(v_w[u][:], tab_w[:].indirect(idx[:, u * cols16 : (u + 1) * cols16]))
+
+        def group_w1(g):
+            grouped = grouped_tile([P, PACK, P, PACK], f"w1_g{g}")
+            nc.scalar.copy(grouped[:].rearrange("p t m j -> p m j t"), w1_raw[g][:].rearrange("p j (m t) -> p m j t", t=PACK))
+            return grouped
+
+        def quantise_w1(g, grouped):
+            nc.vector.quantize_mx(w1_c[g][:].bitcast(FP8X4), w1_s[g][:], grouped[:].rearrange("p t m j -> p (t m j)"))
+
+        def deal_w2(g):
+            nc.vector.tensor_copy(
+                w2_ds[g][:].rearrange("p (t m) -> p t m", t=PACK),
+                w2_s[:, g * PASS : (g + 1) * PASS].rearrange("p (m t) -> p t m", t=PACK),
+            )
+            nc.vector.tensor_copy(
+                w2_dw[g][:].rearrange("p (t m b) -> p t m b", t=PACK, b=2),
+                w2_w[:, 2 * g * PASS : 2 * (g + 1) * PASS].rearrange("p (m t b) -> p t m b", t=PACK, b=2),
+            )
+
+        pending = {}
+
+        def readings(i, u):
+            g, t = divmod(i, PACK)
+            cols = slice(t * P, (t + 1) * P)
+            a = psum.tile([P, BANK], F32, name="a", tag="bank")
+            b = psum.tile([P, BANK], F32, name="b", tag="bank")
+            nc.tensor.matmul_mx(
+                a[:], lhsT=w1_c[g][:, cols].bitcast(FP8X4), lhsT_scale=w1_s[g][:, cols],
+                rhs=v_w[u][:].bitcast(FP8X4), rhs_scale=v_s[u][:], start=True, stop=True,
+            )
+            nc.tensor.matmul_mx(
+                b[:], lhsT=w2_dw[g][:, 2 * t * P : 2 * (t + 1) * P].bitcast(FP4X4), lhsT_scale=w2_ds[g][:, cols],
+                rhs=v_w[u][:].bitcast(FP8X4), rhs_scale=v_s[u][:], start=True, stop=True,
+            )
+            a_sb = ring.tile([P, BANK], F32, name="a_sb", tag="a_sb", bufs=6)
+            nc.scalar.copy(a_sb[:], a[:])
+            pending[(i, u)] = (a_sb, b)
+
+        def larger(i, u, h):
+            a_sb, b = pending[(i, u)]
+            nc.vector.tensor_tensor(h[:, u * BANK : (u + 1) * BANK], b[:], a_sb[:], ALU.max)
+
+        w3_at = PASS
+        odd_at = w3_at + GROUPS * N
+        even_at = odd_at + 4 * S
+        h_at = [4 * S - 64, 0, even_at, w3_at, even_at, odd_at, even_at, odd_at]
+
+        def new_h(i):
+            return placed.tile([P, S], F32, name=f"h{i}", offset=h_at[i], align_bytes=64)
+
+        def scatter(i, h):
+            nc.vector.tensor_tensor(page[i][:].indirect(idx2[:]), h[:], gain_of(i % PACK), ALU.mult)
+
+        def store_page(i):
+            nc.sync.dma_start(out_rows[i // PACK, i % PACK], page[i][:])
+
+        p_c = [held([P, T2], U32, f"p_c{g}") for g in range(GROUPS)]
+        p_s = [held([P, T2], U8, f"p_s{g}") for g in range(GROUPS)]
+        w3_c = held([P, GROUPS * N], U32, "w3_c")
+
+        def store_words(g, cols):
+            nc.sync.dma_start(out_2[g].rearrange("p m t -> p (m t)").bitcast(I32)[:, cols], p_c[g][:, cols].bitcast(I32))
+
+        def store_scales(g):
+            for q in range(4):
+                nc.sync.dma_start(out_3[g, 4 * q : 4 * q + 4, :].bitcast(I32), p_s[g][32 * q : 32 * q + 4, :].bitcast(I32))
+
+        for u in range(HALVES):
+            gather_scales(u)
+        grouped0 = group_w1(0)
+        w1_s[0] = placed.tile([P, PASS], U8, name="w1_s0", offset=TAB_AT, align_bytes=64)
+        quantise_w1(0, grouped0)
+        deal_w2(0)
+        gather_words(0)
+        gather_words(1)
+        h = [new_h(0), new_h(1)]
+        for u in range(HALVES):
+            readings(0, u)
+        deal_w2(1)
+        for u in range(HALVES):
+            larger(0, u, h[0])
+        for u in range(HALVES):
+            readings(1, u)
+
+        half = T2 // 2
+        pairs = None
+        last = None
+        w3_s = None
+        for i in range(GROUPS * PACK):
+            g, t = divmod(i, PACK)
+            if i == 2:
+                w1_s[1] = placed.tile([P, PASS], U8, name="w1_s1", offset=0, align_bytes=64)
+                quantise_w1(1, grouped1)
+            if i == 4:
+                w3_s = placed.tile([P, GROUPS * N], U8, name="w3_s", offset=w3_at, align_bytes=64)
+                for a in range(GROUPS):
+                    flat = w3_g[a][:].rearrange("p n j -> p (n j)")
+                    for lo, hi in ((0, 256), (256, N)):
+                        nc.vector.quantize_mx(
+                            w3_c[:, a * N + lo : a * N + hi].bitcast(FP8X4), w3_s[:, a * N + lo : a * N + hi], flat[:, PACK * lo : PACK * hi]
+                        )
+            if i + 1 < GROUPS * PACK:
+                if i > 0:
+                    h.append(new_h(i + 1))
+                for u in range(HALVES):
+                    larger(i + 1, u, h[i + 1])
+            if i + 2 < GROUPS * PACK:
+                for u in range(HALVES):
+                    readings(i + 2, u)
+            scatter(i, h[i])
+            store_page(i)
+            if i == 1:
+                grouped1 = group_w1(1)
+            if i == 2:
+                w3_g = [held([P, N, PACK], BF16, f"w3_g{a}") for a in range(GROUPS)]
+                for a in range(GROUPS):
+                    nc.scalar.copy(
+                        w3_g[a][:].rearrange("p (c i) j -> p c j i", i=4), w3_raw[a][:].rearrange("p j (c i) -> p c j i", i=4)
+                    )
+            if i == PACK:
+                for x in range(2):
+                    cols = slice(x * half, (x + 1) * half)
+                    woven = raw_tile([P, half, PACK], BF16, f"woven{x}")
+                    nc.scalar.copy(
+                        woven[:].rearrange("p m t -> p (m t)").bitcast(F32).rearrange("p (m u) -> p m u", u=2),
+                        pairs[x][:].rearrange("p u m e -> p (u m e)").bitcast(F32).rearrange("p (u m) -> p m u", u=2),
+                    )
+                    nc.vector.quantize_mx(p_c[0][:, cols].bitcast(FP8X4), p_s[0][:, cols], woven[:].rearrange("p m t -> p (m t)"))
+                    store_words(0, cols)
+                store_scales(0)
+            if g == 0:
+                if t == 0:
+                    pairs = [raw_tile([P, 2, half, 2], BF16, f"pairs{x}") for x in range(2)]
+                for x in range(2):
+                    nc.scalar.copy(pairs[x][:, t // 2, :, t % 2], page[i][:, x * half : (x + 1) * half])
+            elif t < PACK - 1:
+                if t == 0:
+                    last = [grouped_tile([P, BANK, PACK], f"last{c}") for c in range(CHUNKS)]
+                for c in range(CHUNKS):
+                    src = page[i][:, c * BANK : (c + 1) * BANK]
+                    if t == 2:
+                        nc.scalar.copy(last[c][:, :, 2:4], src.unsqueeze(2).to_broadcast([P, BANK, 2]))
+                    else:
+                        nc.scalar.copy(last[c][:, :, t], src)
+
+        units = [(c, n) for c in range(CHUNKS) for n in range(NT)]
+        banks = {}
+
+        def passes(unit, g):
+            c, n = unit
+            if g == 0:
+                banks[unit] = (psum.tile([P, BANK], F32, name="d", tag="bank"), psum.tile([P, BANK], F32, name="f", tag="bank"))
+            d, f = banks[unit]
+            cols = slice(c * BANK, (c + 1) * BANK)
+            nc.tensor.matmul_mx(
+                d[:], lhsT=w4_w[:, g, n * P : (n + 1) * P].bitcast(FP8X4), lhsT_scale=w4_s[:, g, n * P : (n + 1) * P],
+                rhs=p_c[g][:, cols].bitcast(FP8X4), rhs_scale=p_s[g][:, cols], start=(g == 0), stop=(g == 1),
+            )
+            wcols = slice(g * N + n * P, g * N + (n + 1) * P)
+            nc.tensor.matmul_mx(
+                f[:], lhsT=w3_c[:, wcols].bitcast(FP8X4), lhsT_scale=w3_s[:, wcols],
+                rhs=p_c[g][:, cols].bitcast(FP8X4), rhs_scale=p_s[g][:, cols], start=(g == 0), stop=(g == 1),
+            )
+
+        def finish(k, unit):
+            c, n = unit
+            d, f = banks[unit]
+            sq = ring.tile([P, BANK], F32, name="sq", tag="a_sb", bufs=6)
+            root = ring.tile([P, BANK], F32, name="root", tag="root", bufs=4)
+            y = ring.tile([P, BANK], F32, name="y", tag="y", bufs=8)
+            nc.scalar.activation(sq[:], d[:], ACT.Square)
+            nc.scalar.activation(root[:], sq[:], ACT.Abs_reciprocal_sqrt, bias=1.0)
+            if k % 4 == 0:
+                nc.scalar.activation(sq[:], root[:], ACT.Square)
+                nc.vector.tensor_tensor(y[:], f[:], sq[:], ALU.mult)
+            else:
+                nc.vector.tensor_tensor(sq[:], f[:], root[:], ALU.mult)
+                nc.vector.tensor_tensor(y[:], sq[:], root[:], ALU.mult)
+            nc.sync.dma_start(out_0[n * P : (n + 1) * P, c * BANK : (c + 1) * BANK], y[:])
+
+        for unit in units[:EARLY_UNITS]:
+            passes(unit, 0)
+        final = GROUPS * PACK - 1
+        for c in range(CHUNKS):
+            cols = slice(c * BANK, (c + 1) * BANK)
+            nc.vector.tensor_copy(last[c][:, :, PACK - 1], page[final][:, cols])
+            nc.vector.quantize_mx(p_c[1][:, cols].bitcast(FP8X4), p_s[1][:, cols], last[c][:].rearrange("p m t -> p (m t)"))
+            store_words(1, cols)
+        store_scales(1)
+        for k, unit in enumerate(units):
+            if k >= EARLY_UNITS:
+                passes(unit, 0)
+            passes(unit, 1)
+            finish(k, unit)

@@ -24,8 +24,12 @@ GROUPS = H // PASS
 HALVES = S // BANK
 CHUNKS = T2 // BANK
 NT = N // P
-EARLY_UNITS = 4
 TAB_AT = PASS + GROUPS * N + 8 * S
+W2S_AT = TAB_AT + T
+VW_AT = TAB_AT + PASS
+TABW_AT = VW_AT + 4 * S
+D_BANKS = (6, 0, 1)
+F_BANKS = (7, 2, 3, 4, 5)
 
 
 def tile_list_chart_tile_planes_kernel(
@@ -37,17 +41,17 @@ def tile_list_chart_tile_planes_kernel(
         keep = ctx.enter_context(tc.tile_pool(name="keep", bufs=1))
         ring = ctx.enter_context(tc.tile_pool(name="ring", bufs=4))
         placed = ctx.enter_context(tc.tile_pool(name="placed", bufs=1))
-        psum = ctx.enter_context(tc.psum_pool(name="psum", bufs=8))
+        psum = ctx.enter_context(tc.psum_pool(name="psum", bufs=1))
 
         def held(shape, dtype, name):
             return keep.tile(shape, dtype, name=name, align_bytes=64)
 
         idx = held([P, S // 16], U16, "idx")
         idx2 = held([P, S // 16], U16, "idx2")
-        tab_w = held([P, T], U32, "tab_w")
+        tab_w = placed.tile([P, T], U32, name="tab_w", offset=TABW_AT, align_bytes=64)
         tab_s = placed.tile([P, T], U8, name="tab_s", offset=TAB_AT, align_bytes=64)
         w2_w = held([P, 2 * H], U8, "w2_w")
-        w2_s = held([P, H], U8, "w2_s")
+        w2_s = placed.tile([P, H], U8, name="w2_s", offset=W2S_AT, align_bytes=64)
         w4_w = held([P, GROUPS, N], U32, "w4_w")
         w4_s = held([P, GROUPS, N], U8, "w4_s")
         gain = [held([P, S], F32, "gain0"), None]
@@ -66,8 +70,8 @@ def tile_list_chart_tile_planes_kernel(
         warm = held([P, 1], F32, "warm")
         warm_out = held([P, 1], F32, "warm_out")
         nc.vector.memset(tab_s[:].bitcast(I32), 0)
-        nc.gpsimd.memset(warm[:], 1.0)
-        nc.gpsimd.memset(w2_s[:].bitcast(I32), 0)
+        nc.vector.memset(w2_s[:].bitcast(I32), 0)
+        nc.vector.memset(warm[:], 1.0)
         nc.vector.memset(w4_s[:].rearrange("p a n -> p (a n)").bitcast(I32), 0)
         w1_raw = []
         for g in range(GROUPS):
@@ -77,26 +81,25 @@ def tile_list_chart_tile_planes_kernel(
         nc.sync.dma_start(idx[:], offs)
         for q in range(4):
             nc.sync.dma_start(tab_s[32 * q : 32 * q + 4, :].bitcast(I32), tab_scales[0, 4 * q : 4 * q + 4, :].bitcast(I32))
-        nc.sync.dma_start(w2_w[:].bitcast(I32), w2_words[0].bitcast(I32))
         nc.sync.dma_start(tab_w[:].bitcast(I32), tab_words[0].rearrange("p n t -> p (n t)").bitcast(I32))
         for q in range(4):
-            nc.gpsimd.dma_start(w2_s[32 * q : 32 * q + 4, :].bitcast(I32), w2_scales[0, 4 * q : 4 * q + 4, :].bitcast(I32))
+            nc.sync.dma_start(w2_s[32 * q : 32 * q + 4, :].bitcast(I32), w2_scales[0, 4 * q : 4 * q + 4, :].bitcast(I32))
+        nc.sync.dma_start(w2_w[:].bitcast(I32), w2_words[0].bitcast(I32))
         nc.scalar.activation(warm_out[:], warm[:], ACT.Abs_reciprocal_sqrt)
         nc.sync.dma_start(page[0][:], page_rows[0, 0])
         nc.sync.dma_start(idx2[:], offs2)
         for q in range(4):
             nc.sync.dma_start(gain[0][32 * q : 32 * q + 32, :], wgs_rows[:, 0, :])
         nc.sync.dma_start(page[1][:], page_rows[0, 1])
+        nc.sync.dma_start(w1_raw[1][:], w1_cols[1])
         for q in range(4):
             nc.sync.dma_start(gain_rest[32 * q : 32 * q + 32, :, :], wgs_rows[:, 1:PACK, :])
-        nc.sync.dma_start(w1_raw[1][:], w1_cols[1])
-        nc.sync.dma_start(page[2][:], page_rows[0, 2])
         w3_rows = w3.rearrange("(a p j) n -> a p j n", a=GROUPS, j=PACK)
         w3_raw = []
         for a in range(GROUPS):
             w3_raw.append(raw_tile([P, PACK, N], F32, f"w3_raw{a}"))
             nc.sync.dma_start(w3_raw[a][:], w3_rows[a])
-        for i in range(3, GROUPS * PACK):
+        for i in range(2, GROUPS * PACK):
             nc.sync.dma_start(page[i][:], page_rows[i // PACK, i % PACK])
         nc.sync.dma_start(w4_w[:].bitcast(I32), w4_words.rearrange("a p n t -> p a (n t)").bitcast(I32))
         for q in range(4):
@@ -108,12 +111,12 @@ def tile_list_chart_tile_planes_kernel(
         def gain_of(t):
             return gain[0][:] if t == 0 else gain_rest[:, t - 1, :]
 
-        v_w = [held([P, BANK], U32, f"v_w{u}") for u in range(HALVES)]
+        v_w = []
         v_s = [held([P, BANK], U8, f"v_s{u}") for u in range(HALVES)]
         w1_c = [held([P, PASS], U32, f"w1_c{g}") for g in range(GROUPS)]
         w1_s = [None, None]
-        w2_dw = [held([P, 2 * PASS], U8, f"w2_dw{g}") for g in range(GROUPS)]
-        w2_ds = [held([P, PASS], U8, f"w2_ds{g}") for g in range(GROUPS)]
+        w2_dw = [held([P, 2 * PASS], U8, "w2_dw0"), None]
+        w2_ds = held([P, H], U8, "w2_ds")
         cols16 = BANK // 16
 
         def gather_scales(u):
@@ -130,12 +133,14 @@ def tile_list_chart_tile_planes_kernel(
         def quantise_w1(g, grouped):
             nc.vector.quantize_mx(w1_c[g][:].bitcast(FP8X4), w1_s[g][:], grouped[:].rearrange("p t m j -> p (t m j)"))
 
-        def deal_w2(g):
-            nc.vector.tensor_copy(
-                w2_ds[g][:].rearrange("p (t m) -> p t m", t=PACK),
-                w2_s[:, g * PASS : (g + 1) * PASS].rearrange("p (m t) -> p t m", t=PACK),
+        def deal_w2_scales():
+            nc.gpsimd.tensor_copy(
+                w2_ds[:].rearrange("p (g t m) -> p g t m", g=GROUPS, t=PACK),
+                w2_s[:].rearrange("p (g m t) -> p g t m", g=GROUPS, t=PACK),
             )
-            nc.vector.tensor_copy(
+
+        def deal_w2_words(g):
+            nc.gpsimd.tensor_copy(
                 w2_dw[g][:].rearrange("p (t m b) -> p t m b", t=PACK, b=2),
                 w2_w[:, 2 * g * PASS : 2 * (g + 1) * PASS].rearrange("p (m t b) -> p t m b", t=PACK, b=2),
             )
@@ -145,14 +150,14 @@ def tile_list_chart_tile_planes_kernel(
         def readings(i, u):
             g, t = divmod(i, PACK)
             cols = slice(t * P, (t + 1) * P)
-            a = psum.tile([P, BANK], F32, name="a", tag="bank")
-            b = psum.tile([P, BANK], F32, name="b", tag="bank")
+            a = psum.tile([P, BANK], F32, name="a", tag=f"bank{u}")
+            b = psum.tile([P, BANK], F32, name="b", tag=f"bank{2 + 2 * (i % 2) + u}")
             nc.tensor.matmul_mx(
                 a[:], lhsT=w1_c[g][:, cols].bitcast(FP8X4), lhsT_scale=w1_s[g][:, cols],
                 rhs=v_w[u][:].bitcast(FP8X4), rhs_scale=v_s[u][:], start=True, stop=True,
             )
             nc.tensor.matmul_mx(
-                b[:], lhsT=w2_dw[g][:, 2 * t * P : 2 * (t + 1) * P].bitcast(FP4X4), lhsT_scale=w2_ds[g][:, cols],
+                b[:], lhsT=w2_dw[g][:, 2 * t * P : 2 * (t + 1) * P].bitcast(FP4X4), lhsT_scale=w2_ds[:, i * P : (i + 1) * P],
                 rhs=v_w[u][:].bitcast(FP8X4), rhs_scale=v_s[u][:], start=True, stop=True,
             )
             a_sb = ring.tile([P, BANK], F32, name="a_sb", tag="a_sb", bufs=6)
@@ -193,13 +198,16 @@ def tile_list_chart_tile_planes_kernel(
         grouped0 = group_w1(0)
         w1_s[0] = placed.tile([P, PASS], U8, name="w1_s0", offset=TAB_AT, align_bytes=64)
         quantise_w1(0, grouped0)
-        deal_w2(0)
-        gather_words(0)
-        gather_words(1)
+        deal_w2_scales()
+        deal_w2_words(0)
+        for u in range(HALVES):
+            v_w.append(placed.tile([P, BANK], U32, name=f"v_w{u}", offset=VW_AT + 4 * BANK * u, align_bytes=64))
+            gather_words(u)
+        w2_dw[1] = placed.tile([P, 2 * PASS], U8, name="w2_dw1", offset=TABW_AT, align_bytes=64)
+        deal_w2_words(1)
         h = [new_h(0), new_h(1)]
         for u in range(HALVES):
             readings(0, u)
-        deal_w2(1)
         for u in range(HALVES):
             larger(0, u, h[0])
         for u in range(HALVES):
@@ -234,7 +242,6 @@ def tile_list_chart_tile_planes_kernel(
             store_page(i)
             if i == 1:
                 grouped1 = group_w1(1)
-            if i == 2:
                 w3_g = [held([P, N, PACK], BF16, f"w3_g{a}") for a in range(GROUPS)]
                 for a in range(GROUPS):
                     nc.scalar.copy(
@@ -267,42 +274,51 @@ def tile_list_chart_tile_planes_kernel(
                         nc.scalar.copy(last[c][:, :, t], src)
 
         units = [(c, n) for c in range(CHUNKS) for n in range(NT)]
-        banks = {}
+        staged = [raw_tile([P, T2], F32, f"staged{n}") for n in range(NT)]
+        d_of = {}
+        f_of = {}
 
-        def passes(unit, g):
-            c, n = unit
+        def d_pass(k, g):
+            c, n = units[k]
             if g == 0:
-                banks[unit] = (psum.tile([P, BANK], F32, name="d", tag="bank"), psum.tile([P, BANK], F32, name="f", tag="bank"))
-            d, f = banks[unit]
+                d_of[k] = psum.tile([P, BANK], F32, name="d", tag=f"bank{D_BANKS[k % len(D_BANKS)]}")
             cols = slice(c * BANK, (c + 1) * BANK)
             nc.tensor.matmul_mx(
-                d[:], lhsT=w4_w[:, g, n * P : (n + 1) * P].bitcast(FP8X4), lhsT_scale=w4_s[:, g, n * P : (n + 1) * P],
+                d_of[k][:], lhsT=w4_w[:, g, n * P : (n + 1) * P].bitcast(FP8X4), lhsT_scale=w4_s[:, g, n * P : (n + 1) * P],
                 rhs=p_c[g][:, cols].bitcast(FP8X4), rhs_scale=p_s[g][:, cols], start=(g == 0), stop=(g == 1),
             )
+
+        def f_pass(k, g):
+            c, n = units[k]
+            if g == 0:
+                f_of[k] = psum.tile([P, BANK], F32, name="f", tag=f"bank{F_BANKS[k % len(F_BANKS)]}")
+            cols = slice(c * BANK, (c + 1) * BANK)
             wcols = slice(g * N + n * P, g * N + (n + 1) * P)
             nc.tensor.matmul_mx(
-                f[:], lhsT=w3_c[:, wcols].bitcast(FP8X4), lhsT_scale=w3_s[:, wcols],
+                f_of[k][:], lhsT=w3_c[:, wcols].bitcast(FP8X4), lhsT_scale=w3_s[:, wcols],
                 rhs=p_c[g][:, cols].bitcast(FP8X4), rhs_scale=p_s[g][:, cols], start=(g == 0), stop=(g == 1),
             )
 
         def finish(k, unit):
             c, n = unit
-            d, f = banks[unit]
+            d, f = d_of[k], f_of[k]
             sq = ring.tile([P, BANK], F32, name="sq", tag="a_sb", bufs=6)
             root = ring.tile([P, BANK], F32, name="root", tag="root", bufs=4)
-            y = ring.tile([P, BANK], F32, name="y", tag="y", bufs=8)
+            y = staged[n][:, c * BANK : (c + 1) * BANK]
             nc.scalar.activation(sq[:], d[:], ACT.Square)
             nc.scalar.activation(root[:], sq[:], ACT.Abs_reciprocal_sqrt, bias=1.0)
-            if k % 4 == 0:
+            if k < NT:
                 nc.scalar.activation(sq[:], root[:], ACT.Square)
-                nc.vector.tensor_tensor(y[:], f[:], sq[:], ALU.mult)
+                nc.vector.tensor_tensor(y, f[:], sq[:], ALU.mult)
             else:
                 nc.vector.tensor_tensor(sq[:], f[:], root[:], ALU.mult)
-                nc.vector.tensor_tensor(y[:], sq[:], root[:], ALU.mult)
-            nc.sync.dma_start(out_0[n * P : (n + 1) * P, c * BANK : (c + 1) * BANK], y[:])
+                nc.vector.tensor_tensor(y, sq[:], root[:], ALU.mult)
+            nc.sync.dma_start(out_0[n * P : (n + 1) * P, c * BANK : (c + 1) * BANK], y)
 
-        for unit in units[:EARLY_UNITS]:
-            passes(unit, 0)
+        for k in range(len(D_BANKS)):
+            d_pass(k, 0)
+        for k in range(len(F_BANKS)):
+            f_pass(k, 0)
         final = GROUPS * PACK - 1
         for c in range(CHUNKS):
             cols = slice(c * BANK, (c + 1) * BANK)
@@ -311,7 +327,10 @@ def tile_list_chart_tile_planes_kernel(
             store_words(1, cols)
         store_scales(1)
         for k, unit in enumerate(units):
-            if k >= EARLY_UNITS:
-                passes(unit, 0)
-            passes(unit, 1)
+            if k >= len(D_BANKS):
+                d_pass(k, 0)
+            d_pass(k, 1)
+            if k >= len(F_BANKS):
+                f_pass(k, 0)
+            f_pass(k, 1)
             finish(k, unit)

@@ -82,9 +82,9 @@ def tile_list_chart_tile_planes_kernel(
         for q in range(4):
             nc.sync.dma_start(tab_s[32 * q : 32 * q + 4, :].bitcast(I32), tab_scales[0, 4 * q : 4 * q + 4, :].bitcast(I32))
         nc.sync.dma_start(tab_w[:].bitcast(I32), tab_words[0].rearrange("p n t -> p (n t)").bitcast(I32))
+        nc.sync.dma_start(w2_w[:].bitcast(I32), w2_words[0].bitcast(I32))
         for q in range(4):
             nc.sync.dma_start(w2_s[32 * q : 32 * q + 4, :].bitcast(I32), w2_scales[0, 4 * q : 4 * q + 4, :].bitcast(I32))
-        nc.sync.dma_start(w2_w[:].bitcast(I32), w2_words[0].bitcast(I32))
         nc.scalar.activation(warm_out[:], warm[:], ACT.Abs_reciprocal_sqrt)
         nc.sync.dma_start(page[0][:], page_rows[0, 0])
         nc.sync.dma_start(idx2[:], offs2)
@@ -116,7 +116,7 @@ def tile_list_chart_tile_planes_kernel(
         w1_c = [held([P, PASS], U32, f"w1_c{g}") for g in range(GROUPS)]
         w1_s = [None, None]
         w2_dw = [held([P, 2 * PASS], U8, "w2_dw0"), None]
-        w2_ds = held([P, H], U8, "w2_ds")
+        w2_ds = [held([P, PASS], U8, f"w2_ds{g}") for g in range(GROUPS)]
         cols16 = BANK // 16
 
         def gather_scales(u):
@@ -133,40 +133,45 @@ def tile_list_chart_tile_planes_kernel(
         def quantise_w1(g, grouped):
             nc.vector.quantize_mx(w1_c[g][:].bitcast(FP8X4), w1_s[g][:], grouped[:].rearrange("p t m j -> p (t m j)"))
 
-        def deal_w2_scales():
-            nc.gpsimd.tensor_copy(
-                w2_ds[:].rearrange("p (g t m) -> p g t m", g=GROUPS, t=PACK),
-                w2_s[:].rearrange("p (g m t) -> p g t m", g=GROUPS, t=PACK),
+        def deal_w2_scales(g):
+            nc.vector.tensor_copy(
+                w2_ds[g][:].rearrange("p (t m) -> p t m", t=PACK),
+                w2_s[:, g * PASS : (g + 1) * PASS].rearrange("p (m t) -> p t m", t=PACK),
             )
 
         def deal_w2_words(g):
-            nc.gpsimd.tensor_copy(
+            nc.vector.tensor_copy(
                 w2_dw[g][:].rearrange("p (t m b) -> p t m b", t=PACK, b=2),
                 w2_w[:, 2 * g * PASS : 2 * (g + 1) * PASS].rearrange("p (m t b) -> p t m b", t=PACK, b=2),
             )
 
-        pending = {}
+        first = {}
+        second = {}
 
-        def readings(i, u):
+        def first_reading(i):
             g, t = divmod(i, PACK)
             cols = slice(t * P, (t + 1) * P)
-            a = psum.tile([P, BANK], F32, name="a", tag=f"bank{u}")
-            b = psum.tile([P, BANK], F32, name="b", tag=f"bank{2 + 2 * (i % 2) + u}")
-            nc.tensor.matmul_mx(
-                a[:], lhsT=w1_c[g][:, cols].bitcast(FP8X4), lhsT_scale=w1_s[g][:, cols],
-                rhs=v_w[u][:].bitcast(FP8X4), rhs_scale=v_s[u][:], start=True, stop=True,
-            )
-            nc.tensor.matmul_mx(
-                b[:], lhsT=w2_dw[g][:, 2 * t * P : 2 * (t + 1) * P].bitcast(FP4X4), lhsT_scale=w2_ds[:, i * P : (i + 1) * P],
-                rhs=v_w[u][:].bitcast(FP8X4), rhs_scale=v_s[u][:], start=True, stop=True,
-            )
-            a_sb = ring.tile([P, BANK], F32, name="a_sb", tag="a_sb", bufs=6)
-            nc.scalar.copy(a_sb[:], a[:])
-            pending[(i, u)] = (a_sb, b)
+            for u in range(HALVES):
+                a = psum.tile([P, BANK], F32, name="a", tag=f"bank{u}")
+                nc.tensor.matmul_mx(
+                    a[:], lhsT=w1_c[g][:, cols].bitcast(FP8X4), lhsT_scale=w1_s[g][:, cols],
+                    rhs=v_w[u][:].bitcast(FP8X4), rhs_scale=v_s[u][:], start=True, stop=True,
+                )
+                first[(i, u)] = ring.tile([P, BANK], F32, name="a_sb", tag="a_sb", bufs=8)
+                nc.scalar.copy(first[(i, u)][:], a[:])
+
+        def second_reading(i):
+            g, t = divmod(i, PACK)
+            for u in range(HALVES):
+                second[(i, u)] = psum.tile([P, BANK], F32, name="b", tag=f"bank{2 + 2 * (i % 2) + u}")
+                nc.tensor.matmul_mx(
+                    second[(i, u)][:], lhsT=w2_dw[g][:, 2 * t * P : 2 * (t + 1) * P].bitcast(FP4X4),
+                    lhsT_scale=w2_ds[g][:, t * P : (t + 1) * P],
+                    rhs=v_w[u][:].bitcast(FP8X4), rhs_scale=v_s[u][:], start=True, stop=True,
+                )
 
         def larger(i, u, h):
-            a_sb, b = pending[(i, u)]
-            nc.vector.tensor_tensor(h[:, u * BANK : (u + 1) * BANK], b[:], a_sb[:], ALU.max)
+            nc.vector.tensor_tensor(h[:, u * BANK : (u + 1) * BANK], second[(i, u)][:], first[(i, u)][:], ALU.max)
 
         w3_at = PASS
         odd_at = w3_at + GROUPS * N
@@ -198,20 +203,21 @@ def tile_list_chart_tile_planes_kernel(
         grouped0 = group_w1(0)
         w1_s[0] = placed.tile([P, PASS], U8, name="w1_s0", offset=TAB_AT, align_bytes=64)
         quantise_w1(0, grouped0)
-        deal_w2_scales()
         deal_w2_words(0)
+        for g in range(GROUPS):
+            deal_w2_scales(g)
         for u in range(HALVES):
             v_w.append(placed.tile([P, BANK], U32, name=f"v_w{u}", offset=VW_AT + 4 * BANK * u, align_bytes=64))
             gather_words(u)
         w2_dw[1] = placed.tile([P, 2 * PASS], U8, name="w2_dw1", offset=TABW_AT, align_bytes=64)
         deal_w2_words(1)
         h = [new_h(0), new_h(1)]
-        for u in range(HALVES):
-            readings(0, u)
+        first_reading(0)
+        second_reading(0)
         for u in range(HALVES):
             larger(0, u, h[0])
-        for u in range(HALVES):
-            readings(1, u)
+        first_reading(1)
+        second_reading(1)
 
         half = T2 // 2
         pairs = None
@@ -235,9 +241,13 @@ def tile_list_chart_tile_planes_kernel(
                     h.append(new_h(i + 1))
                 for u in range(HALVES):
                     larger(i + 1, u, h[i + 1])
+            if i < 2:
+                first_reading(i + 2)
+            elif i < PACK:
+                first_reading(2 * i)
+                first_reading(2 * i + 1)
             if i + 2 < GROUPS * PACK:
-                for u in range(HALVES):
-                    readings(i + 2, u)
+                second_reading(i + 2)
             scatter(i, h[i])
             store_page(i)
             if i == 1:
@@ -252,17 +262,16 @@ def tile_list_chart_tile_planes_kernel(
                     cols = slice(x * half, (x + 1) * half)
                     woven = raw_tile([P, half, PACK], BF16, f"woven{x}")
                     nc.scalar.copy(
-                        woven[:].rearrange("p m t -> p (m t)").bitcast(F32).rearrange("p (m u) -> p m u", u=2),
-                        pairs[x][:].rearrange("p u m e -> p (u m e)").bitcast(F32).rearrange("p (u m) -> p m u", u=2),
+                        woven[:].rearrange("p (c i) t -> p c t i", i=4), pairs[x][:].rearrange("p t (c i) -> p c t i", i=4)
                     )
                     nc.vector.quantize_mx(p_c[0][:, cols].bitcast(FP8X4), p_s[0][:, cols], woven[:].rearrange("p m t -> p (m t)"))
                     store_words(0, cols)
                 store_scales(0)
             if g == 0:
                 if t == 0:
-                    pairs = [raw_tile([P, 2, half, 2], BF16, f"pairs{x}") for x in range(2)]
+                    pairs = [raw_tile([P, PACK, half], BF16, f"pairs{x}") for x in range(2)]
                 for x in range(2):
-                    nc.scalar.copy(pairs[x][:, t // 2, :, t % 2], page[i][:, x * half : (x + 1) * half])
+                    nc.scalar.copy(pairs[x][:, t, :], page[i][:, x * half : (x + 1) * half])
             elif t < PACK - 1:
                 if t == 0:
                     last = [grouped_tile([P, BANK, PACK], f"last{c}") for c in range(CHUNKS)]
@@ -302,7 +311,7 @@ def tile_list_chart_tile_planes_kernel(
         def finish(k, unit):
             c, n = unit
             d, f = d_of[k], f_of[k]
-            sq = ring.tile([P, BANK], F32, name="sq", tag="a_sb", bufs=6)
+            sq = ring.tile([P, BANK], F32, name="sq", tag="a_sb", bufs=8)
             root = ring.tile([P, BANK], F32, name="root", tag="root", bufs=4)
             y = staged[n][:, c * BANK : (c + 1) * BANK]
             nc.scalar.activation(sq[:], d[:], ACT.Square)

@@ -24,10 +24,6 @@ GROUPS = H // PASS
 HALVES = S // BANK
 CHUNKS = T2 // BANK
 NT = N // P
-TAB_AT = PASS + GROUPS * N + 8 * S
-W2S_AT = TAB_AT + T
-VW_AT = TAB_AT + PASS
-TABW_AT = VW_AT + 4 * S
 D_BANKS = (6, 0, 1)
 F_BANKS = (7, 2, 3, 4, 5)
 
@@ -48,10 +44,10 @@ def tile_list_chart_tile_planes_kernel(
 
         idx = held([P, S // 16], U16, "idx")
         idx2 = held([P, S // 16], U16, "idx2")
-        tab_w = placed.tile([P, T], U32, name="tab_w", offset=TABW_AT, align_bytes=64)
-        tab_s = placed.tile([P, T], U8, name="tab_s", offset=TAB_AT, align_bytes=64)
+        tab_w = held([P, T], U32, "tab_w")
+        tab_s = held([P, T], U8, "tab_s")
         w2_w = held([P, 2 * H], U8, "w2_w")
-        w2_s = placed.tile([P, H], U8, name="w2_s", offset=W2S_AT, align_bytes=64)
+        w2_s = held([P, H], U8, "w2_s")
         w4_w = held([P, GROUPS, N], U32, "w4_w")
         w4_s = held([P, GROUPS, N], U8, "w4_s")
         gain = [held([P, S], F32, "gain0"), None]
@@ -69,7 +65,7 @@ def tile_list_chart_tile_planes_kernel(
 
         warm = held([P, 1], F32, "warm")
         warm_out = held([P, 1], F32, "warm_out")
-        nc.vector.memset(tab_s[:].bitcast(I32), 0)
+        nc.gpsimd.memset(tab_s[:].bitcast(I32), 0)
         nc.vector.memset(w2_s[:].bitcast(I32), 0)
         nc.vector.memset(warm[:], 1.0)
         nc.vector.memset(w4_s[:].rearrange("p a n -> p (a n)").bitcast(I32), 0)
@@ -77,17 +73,17 @@ def tile_list_chart_tile_planes_kernel(
         for g in range(GROUPS):
             w1_raw.append(raw_tile([P, PACK, PASS], F32, f"w1_raw{g}"))
         w1_cols = w1.rearrange("(p j) (g c) -> g p j c", j=PACK, g=GROUPS)
-        nc.sync.dma_start(w1_raw[0][:], w1_cols[0])
         nc.sync.dma_start(idx[:], offs)
+        nc.sync.dma_start(idx2[:], offs2)
         for q in range(4):
             nc.sync.dma_start(tab_s[32 * q : 32 * q + 4, :].bitcast(I32), tab_scales[0, 4 * q : 4 * q + 4, :].bitcast(I32))
         nc.sync.dma_start(tab_w[:].bitcast(I32), tab_words[0].rearrange("p n t -> p (n t)").bitcast(I32))
-        nc.sync.dma_start(w2_w[:].bitcast(I32), w2_words[0].bitcast(I32))
         for q in range(4):
             nc.sync.dma_start(w2_s[32 * q : 32 * q + 4, :].bitcast(I32), w2_scales[0, 4 * q : 4 * q + 4, :].bitcast(I32))
+        nc.sync.dma_start(w2_w[:].bitcast(I32), w2_words[0].bitcast(I32))
+        nc.sync.dma_start(w1_raw[0][:], w1_cols[0])
         nc.scalar.activation(warm_out[:], warm[:], ACT.Abs_reciprocal_sqrt)
         nc.sync.dma_start(page[0][:], page_rows[0, 0])
-        nc.sync.dma_start(idx2[:], offs2)
         for q in range(4):
             nc.sync.dma_start(gain[0][32 * q : 32 * q + 32, :], wgs_rows[:, 0, :])
         nc.sync.dma_start(page[1][:], page_rows[0, 1])
@@ -111,12 +107,12 @@ def tile_list_chart_tile_planes_kernel(
         def gain_of(t):
             return gain[0][:] if t == 0 else gain_rest[:, t - 1, :]
 
-        v_w = []
+        v_w = [held([P, BANK], U32, f"v_w{u}") for u in range(HALVES)]
         v_s = [held([P, BANK], U8, f"v_s{u}") for u in range(HALVES)]
         w1_c = [held([P, PASS], U32, f"w1_c{g}") for g in range(GROUPS)]
-        w1_s = [None, None]
+        w1_s = [held([P, PASS], U8, "w1_s0"), None]
         w2_dw = [held([P, 2 * PASS], U8, "w2_dw0"), None]
-        w2_ds = [held([P, PASS], U8, f"w2_ds{g}") for g in range(GROUPS)]
+        w2_ds = [held([P, PASS], U8, "w2_ds0"), None]
         cols16 = BANK // 16
 
         def gather_scales(u):
@@ -152,7 +148,7 @@ def tile_list_chart_tile_planes_kernel(
             g, t = divmod(i, PACK)
             cols = slice(t * P, (t + 1) * P)
             for u in range(HALVES):
-                a = psum.tile([P, BANK], F32, name="a", tag=f"bank{u}")
+                a = psum.tile([P, BANK], F32, name="a", tag=f"bank{u if i else 4 + u}")
                 nc.tensor.matmul_mx(
                     a[:], lhsT=w1_c[g][:, cols].bitcast(FP8X4), lhsT_scale=w1_s[g][:, cols],
                     rhs=v_w[u][:].bitcast(FP8X4), rhs_scale=v_s[u][:], start=True, stop=True,
@@ -176,7 +172,9 @@ def tile_list_chart_tile_planes_kernel(
         w3_at = PASS
         odd_at = w3_at + GROUPS * N
         even_at = odd_at + 4 * S
-        h_at = [4 * S - 64, 0, even_at, w3_at, even_at, odd_at, even_at, odd_at]
+        front_at = even_at + 4 * S
+        woven_at = [front_at + 7 * PASS, front_at + 7 * PASS + 4 * T2]
+        h_at = [4 * S - 64, 0, even_at, w3_at, even_at, odd_at, woven_at[0], woven_at[1]]
 
         def new_h(i):
             return placed.tile([P, S], F32, name=f"h{i}", offset=h_at[i], align_bytes=64)
@@ -200,17 +198,26 @@ def tile_list_chart_tile_planes_kernel(
 
         for u in range(HALVES):
             gather_scales(u)
-        grouped0 = group_w1(0)
-        w1_s[0] = placed.tile([P, PASS], U8, name="w1_s0", offset=TAB_AT, align_bytes=64)
-        quantise_w1(0, grouped0)
-        deal_w2_words(0)
-        for g in range(GROUPS):
-            deal_w2_scales(g)
         for u in range(HALVES):
-            v_w.append(placed.tile([P, BANK], U32, name=f"v_w{u}", offset=VW_AT + 4 * BANK * u, align_bytes=64))
             gather_words(u)
-        w2_dw[1] = placed.tile([P, 2 * PASS], U8, name="w2_dw1", offset=TABW_AT, align_bytes=64)
+        deal_w2_scales(0)
+        deal_w2_words(0)
+        dealt = w1_raw[0][:].rearrange("p j (m t) -> p m j t", t=PACK)
+
+        def quantise_half(x, grouped):
+            cols = slice(2 * P * x, 2 * P * (x + 1))
+            nc.vector.quantize_mx(w1_c[0][:, cols].bitcast(FP8X4), w1_s[0][:, cols], grouped[:].rearrange("p t m j -> p (t m j)"))
+
+        front = placed.tile([P, 2, P, PACK], BF16, name="w1_front", offset=front_at, align_bytes=64)
+        nc.scalar.copy(front[:].rearrange("p t m j -> p m j t"), dealt[:, :, :, 0:2])
+        quantise_half(0, front)
+        w2_ds[1] = placed.tile([P, PASS], U8, name="w2_ds1", offset=front_at, align_bytes=64)
+        w2_dw[1] = placed.tile([P, 2 * PASS], U8, name="w2_dw1", offset=front_at + PASS, align_bytes=64)
+        back = placed.tile([P, 2, P, PACK], BF16, name="w1_back", offset=front_at + 3 * PASS, align_bytes=64)
+        nc.vector.tensor_copy(back[:].rearrange("p t m j -> p m j t"), dealt[:, :, :, 2:4])
+        deal_w2_scales(1)
         deal_w2_words(1)
+        quantise_half(1, back)
         h = [new_h(0), new_h(1)]
         first_reading(0)
         second_reading(0)
@@ -260,7 +267,7 @@ def tile_list_chart_tile_planes_kernel(
             if i == PACK:
                 for x in range(2):
                     cols = slice(x * half, (x + 1) * half)
-                    woven = raw_tile([P, half, PACK], BF16, f"woven{x}")
+                    woven = placed.tile([P, half, PACK], BF16, name=f"woven{x}", offset=woven_at[x], align_bytes=64)
                     nc.scalar.copy(
                         woven[:].rearrange("p (c i) t -> p c t i", i=4), pairs[x][:].rearrange("p t (c i) -> p c t i", i=4)
                     )
@@ -282,64 +289,73 @@ def tile_list_chart_tile_planes_kernel(
                     else:
                         nc.scalar.copy(last[c][:, :, t], src)
 
-        units = [(c, n) for c in range(CHUNKS) for n in range(NT)]
+        whole = [(slice(c * BANK, (c + 1) * BANK), n) for c in range(CHUNKS) for n in range(NT)]
+
+        def halved(unit):
+            cols, n = unit
+            middle = cols.start + BANK // 2
+            return [(slice(cols.start, middle), n), (slice(middle, cols.stop), n)]
+
+        units = halved(whole[0]) + whole[1:-1] + halved(whole[-1])
         staged = [raw_tile([P, T2], F32, f"staged{n}") for n in range(NT)]
         d_of = {}
         f_of = {}
 
         def d_pass(k, g):
-            c, n = units[k]
+            cols, n = units[k]
             if g == 0:
-                d_of[k] = psum.tile([P, BANK], F32, name="d", tag=f"bank{D_BANKS[k % len(D_BANKS)]}")
-            cols = slice(c * BANK, (c + 1) * BANK)
+                d_of[k] = psum.tile([P, cols.stop - cols.start], F32, name="d", tag=f"bank{D_BANKS[k % len(D_BANKS)]}")
             nc.tensor.matmul_mx(
                 d_of[k][:], lhsT=w4_w[:, g, n * P : (n + 1) * P].bitcast(FP8X4), lhsT_scale=w4_s[:, g, n * P : (n + 1) * P],
                 rhs=p_c[g][:, cols].bitcast(FP8X4), rhs_scale=p_s[g][:, cols], start=(g == 0), stop=(g == 1),
             )
 
         def f_pass(k, g):
-            c, n = units[k]
+            cols, n = units[k]
             if g == 0:
-                f_of[k] = psum.tile([P, BANK], F32, name="f", tag=f"bank{F_BANKS[k % len(F_BANKS)]}")
-            cols = slice(c * BANK, (c + 1) * BANK)
+                f_of[k] = psum.tile([P, cols.stop - cols.start], F32, name="f", tag=f"bank{F_BANKS[k % len(F_BANKS)]}")
             wcols = slice(g * N + n * P, g * N + (n + 1) * P)
             nc.tensor.matmul_mx(
                 f_of[k][:], lhsT=w3_c[:, wcols].bitcast(FP8X4), lhsT_scale=w3_s[:, wcols],
                 rhs=p_c[g][:, cols].bitcast(FP8X4), rhs_scale=p_s[g][:, cols], start=(g == 0), stop=(g == 1),
             )
 
-        def finish(k, unit):
-            c, n = unit
+        def finish(k):
+            cols, n = units[k]
+            width = cols.stop - cols.start
             d, f = d_of[k], f_of[k]
-            sq = ring.tile([P, BANK], F32, name="sq", tag="a_sb", bufs=8)
-            root = ring.tile([P, BANK], F32, name="root", tag="root", bufs=4)
-            y = staged[n][:, c * BANK : (c + 1) * BANK]
+            sq = ring.tile([P, width], F32, name="sq", tag="a_sb", bufs=8)
+            root = ring.tile([P, width], F32, name="root", tag="root", bufs=4)
+            y = staged[n][:, cols]
             nc.scalar.activation(sq[:], d[:], ACT.Square)
             nc.scalar.activation(root[:], sq[:], ACT.Abs_reciprocal_sqrt, bias=1.0)
-            if k < NT:
+            if cols.stop <= BANK or width < BANK:
                 nc.scalar.activation(sq[:], root[:], ACT.Square)
                 nc.vector.tensor_tensor(y, f[:], sq[:], ALU.mult)
             else:
                 nc.vector.tensor_tensor(sq[:], f[:], root[:], ALU.mult)
                 nc.vector.tensor_tensor(y, sq[:], root[:], ALU.mult)
-            nc.sync.dma_start(out_0[n * P : (n + 1) * P, c * BANK : (c + 1) * BANK], y)
+            nc.sync.dma_start(out_0[n * P : (n + 1) * P, cols], y)
 
         for k in range(len(D_BANKS)):
             d_pass(k, 0)
         for k in range(len(F_BANKS)):
             f_pass(k, 0)
         final = GROUPS * PACK - 1
-        for c in range(CHUNKS):
-            cols = slice(c * BANK, (c + 1) * BANK)
-            nc.vector.tensor_copy(last[c][:, :, PACK - 1], page[final][:, cols])
-            nc.vector.quantize_mx(p_c[1][:, cols].bitcast(FP8X4), p_s[1][:, cols], last[c][:].rearrange("p m t -> p (m t)"))
-            store_words(1, cols)
+        pieces = [cols for cols, n in halved(whole[0])] + [cols for cols, n in whole[NT::NT]]
+        for cols in pieces:
+            c, lo = divmod(cols.start, BANK)
+            part = last[c][:, lo : lo + cols.stop - cols.start, :]
+            nc.vector.tensor_copy(part[:, :, PACK - 1], page[final][:, cols])
+            nc.vector.quantize_mx(p_c[1][:, cols].bitcast(FP8X4), p_s[1][:, cols], part.rearrange("p m t -> p (m t)"))
+            if cols.stop % BANK == 0:
+                store_words(1, slice(c * BANK, cols.stop))
         store_scales(1)
-        for k, unit in enumerate(units):
+        for k in range(len(units)):
             if k >= len(D_BANKS):
                 d_pass(k, 0)
             d_pass(k, 1)
             if k >= len(F_BANKS):
                 f_pass(k, 0)
             f_pass(k, 1)
-            finish(k, unit)
+            finish(k)

@@ -24,7 +24,9 @@ GROUPS = H // PASS
 HALVES = S // BANK
 CHUNKS = T2 // BANK
 NT = N // P
-D_BANKS = (6, 0, 1)
+A_BANKS = (0, 1, 6, 7)
+B_BANKS = (2, 3, 4, 5)
+D_BANKS = (0, 1, 6)
 F_BANKS = (7, 2, 3, 4, 5)
 
 
@@ -35,68 +37,81 @@ def tile_list_chart_tile_planes_kernel(
     nc = tc.nc
     with ExitStack() as ctx:
         keep = ctx.enter_context(tc.tile_pool(name="keep", bufs=1))
-        ring = ctx.enter_context(tc.tile_pool(name="ring", bufs=4))
         placed = ctx.enter_context(tc.tile_pool(name="placed", bufs=1))
         psum = ctx.enter_context(tc.psum_pool(name="psum", bufs=1))
 
         def held(shape, dtype, name):
             return keep.tile(shape, dtype, name=name, align_bytes=64)
 
+        def at(offset, shape, dtype, name):
+            return placed.tile(shape, dtype, name=name, offset=offset, align_bytes=64)
+
+        half = T2 // 2
+        row = 4 * S
+        tab_at = 0
+        scale_at = tab_at + 4 * T
+        h_at = scale_at + T
+        woven0_at = h_at + 2 * row
+        woven1_at = woven0_at + 8 * T2
+        raw_at = woven1_at + 8 * T2
+        copies_at = raw_at + 8 * row
+        h_places = [
+            woven0_at - row // 2, woven0_at - row - PASS, woven0_at, woven0_at + row, h_at, h_at + row, tab_at, woven0_at + 3 * T2,
+        ]
+
         idx = held([P, S // 16], U16, "idx")
         idx2 = held([P, S // 16], U16, "idx2")
-        tab_w = held([P, T], U32, "tab_w")
-        tab_s = held([P, T], U8, "tab_s")
+        tab_w = at(tab_at, [P, T], U32, "tab_w")
+        tab_s = at(scale_at, [P, T], U8, "tab_s")
         w2_w = held([P, 2 * H], U8, "w2_w")
         w2_s = held([P, H], U8, "w2_s")
         w4_w = held([P, GROUPS, N], U32, "w4_w")
         w4_s = held([P, GROUPS, N], U8, "w4_s")
-        gain = [held([P, S], F32, "gain0"), None]
-        gain_rest = held([P, PACK - 1, S], F32, "gain_rest")
+        gain = [held([P, S], F32, f"gain{t}") for t in range(PACK)]
         page = [held([P, T2], F32, f"page{i}") for i in range(GROUPS * PACK)]
         page_rows = page0.rearrange("(g p t) m -> g t p m", g=GROUPS, t=PACK)
         out_rows = out_1.rearrange("(g p t) m -> g t p m", g=GROUPS, t=PACK)
         wgs_rows = wgs.rearrange("(q t) j -> q t j", t=PACK)
 
-        def raw_tile(shape, dtype, name):
-            return ring.tile(shape, dtype, name=name, tag="wide", align_bytes=64)
-
-        def grouped_tile(shape, name):
-            return ring.tile(shape, BF16, name=name, tag="grouped", align_bytes=64)
-
         warm = held([P, 1], F32, "warm")
         warm_out = held([P, 1], F32, "warm_out")
-        nc.gpsimd.memset(tab_s[:].bitcast(I32), 0)
+        nc.vector.memset(tab_s[:].bitcast(I32), 0)
         nc.vector.memset(w2_s[:].bitcast(I32), 0)
         nc.vector.memset(warm[:], 1.0)
         nc.vector.memset(w4_s[:].rearrange("p a n -> p (a n)").bitcast(I32), 0)
-        w1_raw = []
-        for g in range(GROUPS):
-            w1_raw.append(raw_tile([P, PACK, PASS], F32, f"w1_raw{g}"))
+        w1_raw = [at(raw_at + g * 4 * PACK * PASS, [P, PACK, PASS], F32, f"w1_raw{g}") for g in range(GROUPS)]
+        w3_raw = [at(raw_at + 5 * row + a * 4 * PACK * N, [P, PACK, N], F32, f"w3_raw{a}") for a in range(GROUPS)]
         w1_cols = w1.rearrange("(p j) (g c) -> g p j c", j=PACK, g=GROUPS)
+        w3_rows = w3.rearrange("(a p j) n -> a p j n", a=GROUPS, j=PACK)
+
+        def load_page(i):
+            nc.sync.dma_start(page[i][:], page_rows[i // PACK, i % PACK])
+
+        def load_gain(t):
+            for q in range(4):
+                nc.sync.dma_start(gain[t][32 * q : 32 * q + 32, :], wgs_rows[:, t, :])
+
         nc.sync.dma_start(idx[:], offs)
-        nc.sync.dma_start(idx2[:], offs2)
-        for q in range(4):
-            nc.sync.dma_start(tab_s[32 * q : 32 * q + 4, :].bitcast(I32), tab_scales[0, 4 * q : 4 * q + 4, :].bitcast(I32))
         nc.sync.dma_start(tab_w[:].bitcast(I32), tab_words[0].rearrange("p n t -> p (n t)").bitcast(I32))
         for q in range(4):
-            nc.sync.dma_start(w2_s[32 * q : 32 * q + 4, :].bitcast(I32), w2_scales[0, 4 * q : 4 * q + 4, :].bitcast(I32))
+            nc.sync.dma_start(tab_s[32 * q : 32 * q + 4, :].bitcast(I32), tab_scales[0, 4 * q : 4 * q + 4, :].bitcast(I32))
         nc.sync.dma_start(w2_w[:].bitcast(I32), w2_words[0].bitcast(I32))
         nc.sync.dma_start(w1_raw[0][:], w1_cols[0])
+        for q in range(4):
+            nc.sync.dma_start(w2_s[32 * q : 32 * q + 4, :].bitcast(I32), w2_scales[0, 4 * q : 4 * q + 4, :].bitcast(I32))
         nc.scalar.activation(warm_out[:], warm[:], ACT.Abs_reciprocal_sqrt)
-        nc.sync.dma_start(page[0][:], page_rows[0, 0])
-        for q in range(4):
-            nc.sync.dma_start(gain[0][32 * q : 32 * q + 32, :], wgs_rows[:, 0, :])
-        nc.sync.dma_start(page[1][:], page_rows[0, 1])
+        nc.sync.dma_start(idx2[:], offs2)
+        load_page(0)
+        load_gain(0)
         nc.sync.dma_start(w1_raw[1][:], w1_cols[1])
-        for q in range(4):
-            nc.sync.dma_start(gain_rest[32 * q : 32 * q + 32, :, :], wgs_rows[:, 1:PACK, :])
-        w3_rows = w3.rearrange("(a p j) n -> a p j n", a=GROUPS, j=PACK)
-        w3_raw = []
+        for t in (1, 2):
+            load_gain(t)
+            load_page(t)
         for a in range(GROUPS):
-            w3_raw.append(raw_tile([P, PACK, N], F32, f"w3_raw{a}"))
             nc.sync.dma_start(w3_raw[a][:], w3_rows[a])
-        for i in range(2, GROUPS * PACK):
-            nc.sync.dma_start(page[i][:], page_rows[i // PACK, i % PACK])
+        load_gain(3)
+        for i in range(3, GROUPS * PACK):
+            load_page(i)
         nc.sync.dma_start(w4_w[:].bitcast(I32), w4_words.rearrange("a p n t -> p a (n t)").bitcast(I32))
         for q in range(4):
             nc.sync.dma_start(
@@ -104,86 +119,76 @@ def tile_list_chart_tile_planes_kernel(
                 w4_scales[:, 4 * q : 4 * q + 4, :].rearrange("a r n -> r a n").bitcast(I32),
             )
 
-        def gain_of(t):
-            return gain[0][:] if t == 0 else gain_rest[:, t - 1, :]
-
-        v_w = [held([P, BANK], U32, f"v_w{u}") for u in range(HALVES)]
-        v_s = [held([P, BANK], U8, f"v_s{u}") for u in range(HALVES)]
+        v_s = held([P, S], U8, "v_s")
         w1_c = [held([P, PASS], U32, f"w1_c{g}") for g in range(GROUPS)]
-        w1_s = [held([P, PASS], U8, "w1_s0"), None]
-        w2_dw = [held([P, 2 * PASS], U8, "w2_dw0"), None]
-        w2_ds = [held([P, PASS], U8, "w2_ds0"), None]
-        cols16 = BANK // 16
 
-        def gather_scales(u):
-            nc.vector.tensor_copy(v_s[u][:], tab_s[:].indirect(idx[:, u * cols16 : (u + 1) * cols16]))
+        nc.vector.tensor_copy(v_s[:], tab_s[:].indirect(idx[:]))
+        w1_s = {}
 
-        def gather_words(u):
-            nc.vector.tensor_copy(v_w[u][:], tab_w[:].indirect(idx[:, u * cols16 : (u + 1) * cols16]))
-
-        def group_w1(g):
-            grouped = grouped_tile([P, PACK, P, PACK], f"w1_g{g}")
-            nc.scalar.copy(grouped[:].rearrange("p t m j -> p m j t"), w1_raw[g][:].rearrange("p j (m t) -> p m j t", t=PACK))
+        def group_w1(g, lo, hi, offset):
+            grouped = at(offset, [P, hi - lo, P, PACK], BF16, f"w1_g{g}_{lo}")
+            dealt = w1_raw[g][:].rearrange("p j (m t) -> p m j t", t=PACK)
+            nc.scalar.copy(grouped[:].rearrange("p t m j -> p m j t"), dealt[:, :, :, lo:hi])
             return grouped
 
-        def quantise_w1(g, grouped):
-            nc.vector.quantize_mx(w1_c[g][:].bitcast(FP8X4), w1_s[g][:], grouped[:].rearrange("p t m j -> p (t m j)"))
-
-        def deal_w2_scales(g):
-            nc.vector.tensor_copy(
-                w2_ds[g][:].rearrange("p (t m) -> p t m", t=PACK),
-                w2_s[:, g * PASS : (g + 1) * PASS].rearrange("p (m t) -> p t m", t=PACK),
-            )
-
-        def deal_w2_words(g):
-            nc.vector.tensor_copy(
-                w2_dw[g][:].rearrange("p (t m b) -> p t m b", t=PACK, b=2),
-                w2_w[:, 2 * g * PASS : 2 * (g + 1) * PASS].rearrange("p (m t b) -> p t m b", t=PACK, b=2),
-            )
+        def quantise_w1(g, lo, hi, grouped, offset):
+            scales = at(offset, [P, (hi - lo) * P], U8, f"w1_s{g}_{lo}")
+            nc.vector.quantize_mx(w1_c[g][:, lo * P : hi * P].bitcast(FP8X4), scales[:], grouped[:].rearrange("p t m j -> p (t m j)"))
+            for t in range(lo, hi):
+                w1_s[PACK * g + t] = scales[:, (t - lo) * P : (t - lo + 1) * P]
 
         first = {}
         second = {}
+        h = {}
 
-        def first_reading(i):
+        def first_reading(i, halves=range(HALVES)):
             g, t = divmod(i, PACK)
             cols = slice(t * P, (t + 1) * P)
-            for u in range(HALVES):
-                a = psum.tile([P, BANK], F32, name="a", tag=f"bank{u if i else 4 + u}")
+            for u in halves:
+                picked = slice(u * BANK, (u + 1) * BANK)
+                a = psum.tile([P, BANK], F32, name="a", tag=f"bank{B_BANKS[u] if i == 1 else A_BANKS[2 * (i % 2) + u]}")
                 nc.tensor.matmul_mx(
-                    a[:], lhsT=w1_c[g][:, cols].bitcast(FP8X4), lhsT_scale=w1_s[g][:, cols],
-                    rhs=v_w[u][:].bitcast(FP8X4), rhs_scale=v_s[u][:], start=True, stop=True,
+                    a[:], lhsT=w1_c[g][:, cols].bitcast(FP8X4), lhsT_scale=w1_s[i],
+                    rhs=v_w[:, picked].bitcast(FP8X4), rhs_scale=v_s[:, picked], start=True, stop=True,
                 )
-                first[(i, u)] = ring.tile([P, BANK], F32, name="a_sb", tag="a_sb", bufs=8)
+                first[(i, u)] = at(copies_at + 4 * BANK * ((2 * i + u) % 8), [P, BANK], F32, f"a_sb{i}_{u}")
                 nc.scalar.copy(first[(i, u)][:], a[:])
 
-        def second_reading(i):
+        def second_reading(i, halves=range(HALVES)):
             g, t = divmod(i, PACK)
-            for u in range(HALVES):
-                second[(i, u)] = psum.tile([P, BANK], F32, name="b", tag=f"bank{2 + 2 * (i % 2) + u}")
+            for u in halves:
+                picked = slice(u * BANK, (u + 1) * BANK)
+                second[(i, u)] = psum.tile([P, BANK], F32, name="b", tag=f"bank{B_BANKS[2 * (i % 2) + u]}")
                 nc.tensor.matmul_mx(
-                    second[(i, u)][:], lhsT=w2_dw[g][:, 2 * t * P : 2 * (t + 1) * P].bitcast(FP4X4),
+                    second[(i, u)][:], lhsT=w2_dw[:, 2 * i * P : 2 * (i + 1) * P].bitcast(FP4X4),
                     lhsT_scale=w2_ds[g][:, t * P : (t + 1) * P],
-                    rhs=v_w[u][:].bitcast(FP8X4), rhs_scale=v_s[u][:], start=True, stop=True,
+                    rhs=v_w[:, picked].bitcast(FP8X4), rhs_scale=v_s[:, picked], start=True, stop=True,
                 )
 
-        def larger(i, u, h):
-            nc.vector.tensor_tensor(h[:, u * BANK : (u + 1) * BANK], second[(i, u)][:], first[(i, u)][:], ALU.max)
+        def larger(i):
+            h[i] = at(h_places[i], [P, S], F32, f"h{i}")
+            for u in range(HALVES):
+                nc.vector.tensor_tensor(h[i][:, u * BANK : (u + 1) * BANK], second[(i, u)][:], first[(i, u)][:], ALU.max)
 
-        w3_at = PASS
-        odd_at = w3_at + GROUPS * N
-        even_at = odd_at + 4 * S
-        front_at = even_at + 4 * S
-        woven_at = [front_at + 7 * PASS, front_at + 7 * PASS + 4 * T2]
-        h_at = [4 * S - 64, 0, even_at, w3_at, even_at, odd_at, woven_at[0], woven_at[1]]
+        pairs = []
 
-        def new_h(i):
-            return placed.tile([P, S], F32, name=f"h{i}", offset=h_at[i], align_bytes=64)
+        def scatter(i):
+            t = i % PACK
+            nc.vector.tensor_tensor(page[i][:].indirect(idx2[:]), h[i][:], gain[t][:], ALU.mult)
+            nc.sync.dma_start(out_rows[i // PACK, t], page[i][:])
+            if i + 1 < GROUPS * PACK:
+                for x in range(2):
+                    nc.scalar.copy(pairs[x][:, t // 2, :, t % 2], page[i][:, x * half : (x + 1) * half])
 
-        def scatter(i, h):
-            nc.vector.tensor_tensor(page[i][:].indirect(idx2[:]), h[:], gain_of(i % PACK), ALU.mult)
-
-        def store_page(i):
-            nc.sync.dma_start(out_rows[i // PACK, i % PACK], page[i][:])
+        def weave(cols, offset, name):
+            x, lo = divmod(cols.start, half)
+            width = cols.stop - cols.start
+            woven = at(offset, [P, width, PACK], BF16, name)
+            words = pairs[x][:].rearrange("p u m b -> p (u m b)").bitcast(U32).rearrange("p (u m) -> p m u", u=2)
+            nc.scalar.copy(
+                woven[:].rearrange("p m t -> p (m t)").bitcast(U32).rearrange("p (m u) -> p m u", u=2), words[:, lo : lo + width, :]
+            )
+            return woven
 
         p_c = [held([P, T2], U32, f"p_c{g}") for g in range(GROUPS)]
         p_s = [held([P, T2], U8, f"p_s{g}") for g in range(GROUPS)]
@@ -196,98 +201,66 @@ def tile_list_chart_tile_planes_kernel(
             for q in range(4):
                 nc.sync.dma_start(out_3[g, 4 * q : 4 * q + 4, :].bitcast(I32), p_s[g][32 * q : 32 * q + 4, :].bitcast(I32))
 
+        front = group_w1(0, 0, 2, woven1_at + 6 * PASS)
+        quantise_w1(0, 0, 2, front, scale_at)
+        back = group_w1(0, 2, PACK, woven1_at + 12 * PASS)
+        v_w = held([P, S], U32, "v_w")
         for u in range(HALVES):
-            gather_scales(u)
+            nc.vector.tensor_copy(v_w[:, u * BANK : (u + 1) * BANK], tab_w[:].indirect(idx[:, u * BANK // 16 : (u + 1) * BANK // 16]))
+        w2_dw = held([P, 2 * H], U8, "w2_dw")
+        nc.vector.tensor_copy(
+            w2_dw[:].bitcast(U16).rearrange("p (g t m) -> p g t m", g=GROUPS, t=PACK),
+            w2_w[:].bitcast(U16).rearrange("p (g m t) -> p g t m", g=GROUPS, t=PACK),
+        )
+        w2_ds = [held([P, PASS], U8, "w2_ds0"), at(tab_at + row, [P, PASS], U8, "w2_ds1")]
+        for g in range(GROUPS):
+            nc.vector.tensor_copy(
+                w2_ds[g][:].rearrange("p (t m) -> p t m", t=PACK),
+                w2_s[:, g * PASS : (g + 1) * PASS].rearrange("p (m t) -> p t m", t=PACK),
+            )
         for u in range(HALVES):
-            gather_words(u)
-        deal_w2_scales(0)
-        deal_w2_words(0)
-        dealt = w1_raw[0][:].rearrange("p j (m t) -> p m j t", t=PACK)
-
-        def quantise_half(x, grouped):
-            cols = slice(2 * P * x, 2 * P * (x + 1))
-            nc.vector.quantize_mx(w1_c[0][:, cols].bitcast(FP8X4), w1_s[0][:, cols], grouped[:].rearrange("p t m j -> p (t m j)"))
-
-        front = placed.tile([P, 2, P, PACK], BF16, name="w1_front", offset=front_at, align_bytes=64)
-        nc.scalar.copy(front[:].rearrange("p t m j -> p m j t"), dealt[:, :, :, 0:2])
-        quantise_half(0, front)
-        w2_ds[1] = placed.tile([P, PASS], U8, name="w2_ds1", offset=front_at, align_bytes=64)
-        w2_dw[1] = placed.tile([P, 2 * PASS], U8, name="w2_dw1", offset=front_at + PASS, align_bytes=64)
-        back = placed.tile([P, 2, P, PACK], BF16, name="w1_back", offset=front_at + 3 * PASS, align_bytes=64)
-        nc.vector.tensor_copy(back[:].rearrange("p t m j -> p m j t"), dealt[:, :, :, 2:4])
-        deal_w2_scales(1)
-        deal_w2_words(1)
-        quantise_half(1, back)
-        h = [new_h(0), new_h(1)]
-        first_reading(0)
-        second_reading(0)
-        for u in range(HALVES):
-            larger(0, u, h[0])
-        first_reading(1)
-        second_reading(1)
-
-        half = T2 // 2
-        pairs = None
-        last = None
-        w3_s = None
-        for i in range(GROUPS * PACK):
-            g, t = divmod(i, PACK)
-            if i == 2:
-                w1_s[1] = placed.tile([P, PASS], U8, name="w1_s1", offset=0, align_bytes=64)
-                quantise_w1(1, grouped1)
-            if i == 4:
-                w3_s = placed.tile([P, GROUPS * N], U8, name="w3_s", offset=w3_at, align_bytes=64)
-                for a in range(GROUPS):
-                    flat = w3_g[a][:].rearrange("p n j -> p (n j)")
-                    for lo, hi in ((0, 256), (256, N)):
-                        nc.vector.quantize_mx(
-                            w3_c[:, a * N + lo : a * N + hi].bitcast(FP8X4), w3_s[:, a * N + lo : a * N + hi], flat[:, PACK * lo : PACK * hi]
-                        )
-            if i + 1 < GROUPS * PACK:
-                if i > 0:
-                    h.append(new_h(i + 1))
-                for u in range(HALVES):
-                    larger(i + 1, u, h[i + 1])
-            if i < 2:
-                first_reading(i + 2)
-            elif i < PACK:
-                first_reading(2 * i)
-                first_reading(2 * i + 1)
-            if i + 2 < GROUPS * PACK:
-                second_reading(i + 2)
-            scatter(i, h[i])
-            store_page(i)
-            if i == 1:
-                grouped1 = group_w1(1)
-                w3_g = [held([P, N, PACK], BF16, f"w3_g{a}") for a in range(GROUPS)]
-                for a in range(GROUPS):
-                    nc.scalar.copy(
-                        w3_g[a][:].rearrange("p (c i) j -> p c j i", i=4), w3_raw[a][:].rearrange("p j (c i) -> p c j i", i=4)
-                    )
-            if i == PACK:
-                for x in range(2):
-                    cols = slice(x * half, (x + 1) * half)
-                    woven = placed.tile([P, half, PACK], BF16, name=f"woven{x}", offset=woven_at[x], align_bytes=64)
-                    nc.scalar.copy(
-                        woven[:].rearrange("p (c i) t -> p c t i", i=4), pairs[x][:].rearrange("p t (c i) -> p c t i", i=4)
-                    )
-                    nc.vector.quantize_mx(p_c[0][:, cols].bitcast(FP8X4), p_s[0][:, cols], woven[:].rearrange("p m t -> p (m t)"))
-                    store_words(0, cols)
-                store_scales(0)
-            if g == 0:
-                if t == 0:
-                    pairs = [raw_tile([P, PACK, half], BF16, f"pairs{x}") for x in range(2)]
-                for x in range(2):
-                    nc.scalar.copy(pairs[x][:, t, :], page[i][:, x * half : (x + 1) * half])
-            elif t < PACK - 1:
-                if t == 0:
-                    last = [grouped_tile([P, BANK, PACK], f"last{c}") for c in range(CHUNKS)]
-                for c in range(CHUNKS):
-                    src = page[i][:, c * BANK : (c + 1) * BANK]
-                    if t == 2:
-                        nc.scalar.copy(last[c][:, :, 2:4], src.unsqueeze(2).to_broadcast([P, BANK, 2]))
-                    else:
-                        nc.scalar.copy(last[c][:, :, t], src)
+            first_reading(0, [u])
+            second_reading(0, [u])
+        larger(0)
+        quantise_w1(0, 2, PACK, back, copies_at)
+        for i in range(1, PACK):
+            first_reading(i)
+        grouped1 = group_w1(1, 0, PACK, copies_at)
+        pairs.extend(at(raw_at + (1 + 2 * x) * row, [P, 2, half, 2], BF16, f"pairs{x}") for x in range(2))
+        scatter(0)
+        for i in range(1, PACK):
+            second_reading(i)
+            larger(i)
+        quantise_w1(1, 0, PACK, grouped1, woven0_at - PASS)
+        for i in range(PACK, GROUPS * PACK):
+            first_reading(i)
+        scatter(1)
+        for i in range(PACK, GROUPS * PACK - 1):
+            second_reading(i)
+            larger(i)
+        second_reading(GROUPS * PACK - 1)
+        scatter(2)
+        w3_g = [at(woven1_at + 16 * PASS + a * 2 * PACK * N, [P, N, PACK], BF16, f"w3_g{a}") for a in range(GROUPS)]
+        for a in range(GROUPS):
+            nc.scalar.copy(w3_g[a][:].rearrange("p (c i) j -> p c j i", i=4), w3_raw[a][:].rearrange("p j (c i) -> p c j i", i=4))
+        scatter(3)
+        woven0 = [weave(slice(x * half, (x + 1) * half), woven0_at + x * 8 * half, f"woven0_{x}") for x in range(2)]
+        scatter(4)
+        w3_s = at(h_at, [P, GROUPS * N], U8, "w3_s")
+        for a in range(GROUPS):
+            flat = w3_g[a][:].rearrange("p n j -> p (n j)")
+            for lo, hi in ((0, 256), (256, N)):
+                nc.vector.quantize_mx(
+                    w3_c[:, a * N + lo : a * N + hi].bitcast(FP8X4), w3_s[:, a * N + lo : a * N + hi], flat[:, PACK * lo : PACK * hi]
+                )
+        scatter(5)
+        scatter(6)
+        for x in range(2):
+            cols = slice(x * half, (x + 1) * half)
+            nc.vector.quantize_mx(p_c[0][:, cols].bitcast(FP8X4), p_s[0][:, cols], woven0[x][:].rearrange("p m t -> p (m t)"))
+            store_words(0, cols)
+        store_scales(0)
+        larger(GROUPS * PACK - 1)
 
         whole = [(slice(c * BANK, (c + 1) * BANK), n) for c in range(CHUNKS) for n in range(NT)]
 
@@ -297,7 +270,10 @@ def tile_list_chart_tile_planes_kernel(
             return [(slice(cols.start, middle), n), (slice(middle, cols.stop), n)]
 
         units = halved(whole[0]) + whole[1:-1] + halved(whole[-1])
-        staged = [raw_tile([P, T2], F32, f"staged{n}") for n in range(NT)]
+        pieces = [cols for cols, n in halved(whole[0])] + [cols for cols, n in whole[NT::NT]]
+        woven1 = [weave(cols, woven1_at + 8 * cols.start, f"woven1_{cols.start}") for cols in pieces]
+        scatter(GROUPS * PACK - 1)
+        staged = [at(raw_at + n * 4 * T2, [P, T2], F32, f"staged{n}") for n in range(NT)]
         d_of = {}
         f_of = {}
 
@@ -324,8 +300,8 @@ def tile_list_chart_tile_planes_kernel(
             cols, n = units[k]
             width = cols.stop - cols.start
             d, f = d_of[k], f_of[k]
-            sq = ring.tile([P, width], F32, name="sq", tag="a_sb", bufs=8)
-            root = ring.tile([P, width], F32, name="root", tag="root", bufs=4)
+            sq = at(copies_at + 4 * BANK * (k % 8), [P, width], F32, f"sq{k}")
+            root = at(tab_at + 4 * BANK * (k % 4), [P, width], F32, f"root{k}")
             y = staged[n][:, cols]
             nc.scalar.activation(sq[:], d[:], ACT.Square)
             nc.scalar.activation(root[:], sq[:], ACT.Abs_reciprocal_sqrt, bias=1.0)
@@ -342,14 +318,11 @@ def tile_list_chart_tile_planes_kernel(
         for k in range(len(F_BANKS)):
             f_pass(k, 0)
         final = GROUPS * PACK - 1
-        pieces = [cols for cols, n in halved(whole[0])] + [cols for cols, n in whole[NT::NT]]
-        for cols in pieces:
-            c, lo = divmod(cols.start, BANK)
-            part = last[c][:, lo : lo + cols.stop - cols.start, :]
+        for cols, part in zip(pieces, woven1):
             nc.vector.tensor_copy(part[:, :, PACK - 1], page[final][:, cols])
-            nc.vector.quantize_mx(p_c[1][:, cols].bitcast(FP8X4), p_s[1][:, cols], part.rearrange("p m t -> p (m t)"))
+            nc.vector.quantize_mx(p_c[1][:, cols].bitcast(FP8X4), p_s[1][:, cols], part[:].rearrange("p m t -> p (m t)"))
             if cols.stop % BANK == 0:
-                store_words(1, slice(c * BANK, cols.stop))
+                store_words(1, slice(cols.stop - BANK, cols.stop))
         store_scales(1)
         for k in range(len(units)):
             if k >= len(D_BANKS):

@@ -24,10 +24,10 @@ GROUPS = H // PASS
 HALVES = S // BANK
 CHUNKS = T2 // BANK
 NT = N // P
-A_BANKS = (0, 1, 6, 7)
-B_BANKS = (2, 3, 4, 5)
-D_BANKS = (0, 1, 6)
-F_BANKS = (7, 2, 3, 4, 5)
+A_BANKS = (4, 5, 6, 7)
+B_BANKS = (2, 3, 0, 1)
+D_BANKS = (4, 5, 6)
+F_BANKS = (7, 2, 3, 0, 1)
 
 
 def tile_list_chart_tile_planes_kernel(
@@ -50,7 +50,7 @@ def tile_list_chart_tile_planes_kernel(
         row = 4 * S
         tab_at = 0
         scale_at = tab_at + 4 * T
-        h_at = scale_at + T
+        h_at = scale_at + H
         woven0_at = h_at + 2 * row
         woven1_at = woven0_at + 8 * T2
         raw_at = woven1_at + 8 * T2
@@ -62,9 +62,9 @@ def tile_list_chart_tile_planes_kernel(
         idx = held([P, S // 16], U16, "idx")
         idx2 = held([P, S // 16], U16, "idx2")
         tab_w = at(tab_at, [P, T], U32, "tab_w")
-        tab_s = at(scale_at, [P, T], U8, "tab_s")
+        tab_s = held([P, T], U8, "tab_s")
         w2_w = held([P, 2 * H], U8, "w2_w")
-        w2_s = held([P, H], U8, "w2_s")
+        w2_s = at(scale_at, [P, H], U8, "w2_s")
         w4_w = held([P, GROUPS, N], U32, "w4_w")
         w4_s = held([P, GROUPS, N], U8, "w4_s")
         gain = [held([P, S], F32, f"gain{t}") for t in range(PACK)]
@@ -88,19 +88,19 @@ def tile_list_chart_tile_planes_kernel(
             nc.sync.dma_start(page[i][:], page_rows[i // PACK, i % PACK])
 
         def load_gain(t):
-            for q in range(4):
+            for q in (0, 2, 1, 3):
                 nc.sync.dma_start(gain[t][32 * q : 32 * q + 32, :], wgs_rows[:, t, :])
 
         nc.sync.dma_start(idx[:], offs)
-        nc.sync.dma_start(tab_w[:].bitcast(I32), tab_words[0].rearrange("p n t -> p (n t)").bitcast(I32))
+        nc.sync.dma_start(idx2[:], offs2)
         for q in range(4):
             nc.sync.dma_start(tab_s[32 * q : 32 * q + 4, :].bitcast(I32), tab_scales[0, 4 * q : 4 * q + 4, :].bitcast(I32))
+        nc.sync.dma_start(tab_w[:].bitcast(I32), tab_words[0].rearrange("p n t -> p (n t)").bitcast(I32))
         nc.sync.dma_start(w2_w[:].bitcast(I32), w2_words[0].bitcast(I32))
-        nc.sync.dma_start(w1_raw[0][:], w1_cols[0])
         for q in range(4):
             nc.sync.dma_start(w2_s[32 * q : 32 * q + 4, :].bitcast(I32), w2_scales[0, 4 * q : 4 * q + 4, :].bitcast(I32))
+        nc.sync.dma_start(w1_raw[0][:], w1_cols[0])
         nc.scalar.activation(warm_out[:], warm[:], ACT.Abs_reciprocal_sqrt)
-        nc.sync.dma_start(idx2[:], offs2)
         load_page(0)
         load_gain(0)
         nc.sync.dma_start(w1_raw[1][:], w1_cols[1])
@@ -146,7 +146,7 @@ def tile_list_chart_tile_planes_kernel(
             cols = slice(t * P, (t + 1) * P)
             for u in halves:
                 picked = slice(u * BANK, (u + 1) * BANK)
-                a = psum.tile([P, BANK], F32, name="a", tag=f"bank{B_BANKS[u] if i == 1 else A_BANKS[2 * (i % 2) + u]}")
+                a = psum.tile([P, BANK], F32, name="a", tag=f"bank{B_BANKS[2 * (1 - i) + u] if i < 2 else A_BANKS[2 * (i % 2) + u]}")
                 nc.tensor.matmul_mx(
                     a[:], lhsT=w1_c[g][:, cols].bitcast(FP8X4), lhsT_scale=w1_s[i],
                     rhs=v_w[:, picked].bitcast(FP8X4), rhs_scale=v_s[:, picked], start=True, stop=True,
@@ -202,12 +202,11 @@ def tile_list_chart_tile_planes_kernel(
                 nc.sync.dma_start(out_3[g, 4 * q : 4 * q + 4, :].bitcast(I32), p_s[g][32 * q : 32 * q + 4, :].bitcast(I32))
 
         front = group_w1(0, 0, 2, woven1_at + 6 * PASS)
-        quantise_w1(0, 0, 2, front, scale_at)
         back = group_w1(0, 2, PACK, woven1_at + 12 * PASS)
         v_w = held([P, S], U32, "v_w")
         for u in range(HALVES):
             nc.vector.tensor_copy(v_w[:, u * BANK : (u + 1) * BANK], tab_w[:].indirect(idx[:, u * BANK // 16 : (u + 1) * BANK // 16]))
-        w2_dw = held([P, 2 * H], U8, "w2_dw")
+        w2_dw = at(tab_at + row + PASS, [P, 2 * H], U8, "w2_dw")
         nc.vector.tensor_copy(
             w2_dw[:].bitcast(U16).rearrange("p (g t m) -> p g t m", g=GROUPS, t=PACK),
             w2_w[:].bitcast(U16).rearrange("p (g m t) -> p g t m", g=GROUPS, t=PACK),
@@ -218,9 +217,9 @@ def tile_list_chart_tile_planes_kernel(
                 w2_ds[g][:].rearrange("p (t m) -> p t m", t=PACK),
                 w2_s[:, g * PASS : (g + 1) * PASS].rearrange("p (m t) -> p t m", t=PACK),
             )
-        for u in range(HALVES):
-            first_reading(0, [u])
-            second_reading(0, [u])
+        quantise_w1(0, 0, 2, front, scale_at)
+        second_reading(0)
+        first_reading(0)
         larger(0)
         quantise_w1(0, 2, PACK, back, copies_at)
         for i in range(1, PACK):
@@ -296,33 +295,55 @@ def tile_list_chart_tile_planes_kernel(
                 rhs=p_c[g][:, cols].bitcast(FP8X4), rhs_scale=p_s[g][:, cols], start=(g == 0), stop=(g == 1),
             )
 
-        def finish(k):
+        root_of = {}
+        part_of = {}
+
+        def damping(k):
             cols, n = units[k]
             width = cols.stop - cols.start
-            d, f = d_of[k], f_of[k]
             sq = at(copies_at + 4 * BANK * (k % 8), [P, width], F32, f"sq{k}")
             root = at(tab_at + 4 * BANK * (k % 4), [P, width], F32, f"root{k}")
-            y = staged[n][:, cols]
-            nc.scalar.activation(sq[:], d[:], ACT.Square)
+            nc.scalar.activation(sq[:], d_of[k][:], ACT.Square)
             nc.scalar.activation(root[:], sq[:], ACT.Abs_reciprocal_sqrt, bias=1.0)
             if cols.stop <= BANK or width < BANK:
                 nc.scalar.activation(sq[:], root[:], ACT.Square)
-                nc.vector.tensor_tensor(y, f[:], sq[:], ALU.mult)
+                nc.vector.tensor_tensor(staged[n][:, cols], f_of[k][:], sq[:], ALU.mult)
+                nc.sync.dma_start(out_0[n * P : (n + 1) * P, cols], staged[n][:, cols])
             else:
-                nc.vector.tensor_tensor(sq[:], f[:], root[:], ALU.mult)
-                nc.vector.tensor_tensor(y, sq[:], root[:], ALU.mult)
-            nc.sync.dma_start(out_0[n * P : (n + 1) * P, cols], y)
+                nc.vector.tensor_tensor(sq[:], f_of[k][:], root[:], ALU.mult)
+                root_of[k] = root
+                part_of[k] = sq
+
+        def finish(k):
+            cols, n = units[k]
+            nc.vector.tensor_tensor(staged[n][:, cols], part_of[k][:], root_of[k][:], ALU.mult)
+            nc.sync.dma_start(out_0[n * P : (n + 1) * P, cols], staged[n][:, cols])
 
         for k in range(len(D_BANKS)):
             d_pass(k, 0)
         for k in range(len(F_BANKS)):
             f_pass(k, 0)
         final = GROUPS * PACK - 1
-        for cols, part in zip(pieces, woven1):
-            nc.vector.tensor_copy(part[:, :, PACK - 1], page[final][:, cols])
-            nc.vector.quantize_mx(p_c[1][:, cols].bitcast(FP8X4), p_s[1][:, cols], part[:].rearrange("p m t -> p (m t)"))
+
+        def fill(j):
+            copy = nc.scalar.copy if j == 2 else nc.vector.tensor_copy
+            copy(woven1[j][:, :, PACK - 1], page[final][:, pieces[j]])
+
+        def quantise_piece(j):
+            cols = pieces[j]
+            nc.vector.quantize_mx(p_c[1][:, cols].bitcast(FP8X4), p_s[1][:, cols], woven1[j][:].rearrange("p m t -> p (m t)"))
             if cols.stop % BANK == 0:
                 store_words(1, slice(cols.stop - BANK, cols.stop))
+
+        for j in range(3):
+            fill(j)
+        quantise_piece(0)
+        fill(3)
+        quantise_piece(1)
+        quantise_piece(2)
+        fill(4)
+        quantise_piece(3)
+        quantise_piece(4)
         store_scales(1)
         for k in range(len(units)):
             if k >= len(D_BANKS):
@@ -331,4 +352,6 @@ def tile_list_chart_tile_planes_kernel(
             if k >= len(F_BANKS):
                 f_pass(k, 0)
             f_pass(k, 1)
-            finish(k)
+            damping(k)
+            if k - 1 in part_of:
+                finish(k - 1)

@@ -56,7 +56,7 @@ def tile_list_chart_tile_planes_kernel(
         raw_at = woven1_at + 8 * T2
         copies_at = raw_at + 8 * row
         h_places = [
-            woven0_at - row // 2, woven0_at - row - PASS, woven0_at, woven0_at + row, h_at, h_at + row, tab_at, woven0_at + 3 * T2,
+            woven0_at - row // 2, woven0_at - row - PASS, woven0_at, woven0_at + row, h_at, h_at + row, tab_at, woven0_at,
         ]
 
         idx = held([P, S // 16], U16, "idx")
@@ -253,13 +253,17 @@ def tile_list_chart_tile_planes_kernel(
                     w3_c[:, a * N + lo : a * N + hi].bitcast(FP8X4), w3_s[:, a * N + lo : a * N + hi], flat[:, PACK * lo : PACK * hi]
                 )
         scatter(5)
-        scatter(6)
-        for x in range(2):
+
+        def quantise_half(x):
             cols = slice(x * half, (x + 1) * half)
             nc.vector.quantize_mx(p_c[0][:, cols].bitcast(FP8X4), p_s[0][:, cols], woven0[x][:].rearrange("p m t -> p (m t)"))
             store_words(0, cols)
-        store_scales(0)
+
+        quantise_half(0)
         larger(GROUPS * PACK - 1)
+        scatter(6)
+        quantise_half(1)
+        store_scales(0)
 
         whole = [(slice(c * BANK, (c + 1) * BANK), n) for c in range(CHUNKS) for n in range(NT)]
 
@@ -305,7 +309,7 @@ def tile_list_chart_tile_planes_kernel(
             root = at(tab_at + 4 * BANK * (k % 4), [P, width], F32, f"root{k}")
             nc.scalar.activation(sq[:], d_of[k][:], ACT.Square)
             nc.scalar.activation(root[:], sq[:], ACT.Abs_reciprocal_sqrt, bias=1.0)
-            if cols.stop <= BANK or width < BANK:
+            if width < BANK:
                 nc.scalar.activation(sq[:], root[:], ACT.Square)
                 nc.vector.tensor_tensor(staged[n][:, cols], f_of[k][:], sq[:], ALU.mult)
                 nc.sync.dma_start(out_0[n * P : (n + 1) * P, cols], staged[n][:, cols])

@@ -50,7 +50,7 @@ def tile_list_chart_tile_planes_kernel(
         row = 4 * S
         tab_at = 0
         scale_at = tab_at + 4 * T
-        h_at = scale_at + H
+        h_at = scale_at + 5 * PASS
         woven0_at = h_at + 2 * row
         woven1_at = woven0_at + 8 * T2
         raw_at = woven1_at + 8 * T2
@@ -149,20 +149,21 @@ def tile_list_chart_tile_planes_kernel(
                 a = psum.tile([P, BANK], F32, name="a", tag=f"bank{B_BANKS[2 * (1 - i) + u] if i < 2 else A_BANKS[2 * (i % 2) + u]}")
                 nc.tensor.matmul_mx(
                     a[:], lhsT=w1_c[g][:, cols].bitcast(FP8X4), lhsT_scale=w1_s[i],
-                    rhs=v_w[:, picked].bitcast(FP8X4), rhs_scale=v_s[:, picked], start=True, stop=True,
+                    rhs=v_w[u][:].bitcast(FP8X4), rhs_scale=v_s[:, picked], start=True, stop=True,
                 )
-                first[(i, u)] = at(copies_at + 4 * BANK * ((2 * i + u) % 8), [P, BANK], F32, f"a_sb{i}_{u}")
-                nc.scalar.copy(first[(i, u)][:], a[:])
+                first[(i, u)] = a
+                if i > 0:
+                    first[(i, u)] = at(copies_at + 4 * BANK * ((2 * i + u) % 8), [P, BANK], F32, f"a_sb{i}_{u}")
+                    nc.scalar.copy(first[(i, u)][:], a[:])
 
         def second_reading(i, halves=range(HALVES)):
-            g, t = divmod(i, PACK)
             for u in halves:
                 picked = slice(u * BANK, (u + 1) * BANK)
                 second[(i, u)] = psum.tile([P, BANK], F32, name="b", tag=f"bank{B_BANKS[2 * (i % 2) + u]}")
                 nc.tensor.matmul_mx(
                     second[(i, u)][:], lhsT=w2_dw[:, 2 * i * P : 2 * (i + 1) * P].bitcast(FP4X4),
-                    lhsT_scale=w2_ds[g][:, t * P : (t + 1) * P],
-                    rhs=v_w[:, picked].bitcast(FP8X4), rhs_scale=v_s[:, picked], start=True, stop=True,
+                    lhsT_scale=w2_ds[:, i * P : (i + 1) * P],
+                    rhs=v_w[u][:].bitcast(FP8X4), rhs_scale=v_s[:, picked], start=True, stop=True,
                 )
 
         def larger(i):
@@ -201,30 +202,39 @@ def tile_list_chart_tile_planes_kernel(
             for q in range(4):
                 nc.sync.dma_start(out_3[g, 4 * q : 4 * q + 4, :].bitcast(I32), p_s[g][32 * q : 32 * q + 4, :].bitcast(I32))
 
-        front = group_w1(0, 0, 2, woven1_at + 6 * PASS)
+        front = at(woven1_at + 2 * PASS, [P, 2, P, PACK], BF16, "w1_front")
+        front_view = front[:].rearrange("p t m j -> p m j t")
+        front_raw = w1_raw[0][:].rearrange("p j (m t) -> p m j t", t=PACK)
+        nc.scalar.copy(front_view[:, : P // 2], front_raw[:, : P // 2, :, 0:2])
         back = group_w1(0, 2, PACK, woven1_at + 12 * PASS)
-        v_w = held([P, S], U32, "v_w")
-        for u in range(HALVES):
-            nc.vector.tensor_copy(v_w[:, u * BANK : (u + 1) * BANK], tab_w[:].indirect(idx[:, u * BANK // 16 : (u + 1) * BANK // 16]))
-        w2_dw = at(tab_at + row + PASS, [P, 2 * H], U8, "w2_dw")
+        v_w = [held([P, BANK], U32, "v_w0")]
+        nc.vector.tensor_copy(v_w[0][:], tab_w[:].indirect(idx[:, : BANK // 16]))
+        w2_dw = held([P, 2 * H], U8, "w2_dw")
         nc.vector.tensor_copy(
             w2_dw[:].bitcast(U16).rearrange("p (g t m) -> p g t m", g=GROUPS, t=PACK),
             w2_w[:].bitcast(U16).rearrange("p (g m t) -> p g t m", g=GROUPS, t=PACK),
         )
-        w2_ds = [held([P, PASS], U8, "w2_ds0"), at(tab_at + row, [P, PASS], U8, "w2_ds1")]
-        for g in range(GROUPS):
-            nc.vector.tensor_copy(
-                w2_ds[g][:].rearrange("p (t m) -> p t m", t=PACK),
-                w2_s[:, g * PASS : (g + 1) * PASS].rearrange("p (m t) -> p t m", t=PACK),
-            )
+        w2_ds = held([P, H], U8, "w2_ds")
+        nc.vector.tensor_copy(
+            w2_ds[:].rearrange("p (g t m) -> p g t m", g=GROUPS, t=PACK),
+            w2_s[:].rearrange("p (g m t) -> p g t m", g=GROUPS, t=PACK),
+        )
+        v_w.append(at(scale_at + PASS, [P, BANK], U32, "v_w1"))
+        nc.vector.tensor_copy(v_w[1][:], tab_w[:].indirect(idx[:, BANK // 16 :]))
+        nc.vector.tensor_copy(front_view[:, P // 2 :], front_raw[:, P // 2 :, :, 0:2])
         quantise_w1(0, 0, 2, front, scale_at)
         second_reading(0)
         first_reading(0)
+        quantise_w1(0, 2, PACK, back, woven1_at + 10 * PASS)
+        for u in range(HALVES):
+            copied = at(woven1_at + 4 * u * PASS, [P, BANK], F32, f"b_sb{u}")
+            nc.scalar.copy(copied[:], second[(0, u)][:])
+            second[(0, u)] = first[(0, u)]
+            first[(0, u)] = copied
         larger(0)
-        quantise_w1(0, 2, PACK, back, copies_at)
         for i in range(1, PACK):
             first_reading(i)
-        grouped1 = group_w1(1, 0, PACK, copies_at)
+        grouped1 = group_w1(1, 0, PACK, woven1_at)
         pairs.extend(at(raw_at + (1 + 2 * x) * row, [P, 2, half, 2], BF16, f"pairs{x}") for x in range(2))
         scatter(0)
         for i in range(1, PACK):
@@ -239,19 +249,15 @@ def tile_list_chart_tile_planes_kernel(
             larger(i)
         second_reading(GROUPS * PACK - 1)
         scatter(2)
-        w3_g = [at(woven1_at + 16 * PASS + a * 2 * PACK * N, [P, N, PACK], BF16, f"w3_g{a}") for a in range(GROUPS)]
+        w3_g = at(woven1_at + 16 * PASS, [P, GROUPS * N, PACK], BF16, "w3_g")
         for a in range(GROUPS):
-            nc.scalar.copy(w3_g[a][:].rearrange("p (c i) j -> p c j i", i=4), w3_raw[a][:].rearrange("p j (c i) -> p c j i", i=4))
+            nc.scalar.copy(w3_g[:, a * N : (a + 1) * N, :].rearrange("p (c i) j -> p c j i", i=4), w3_raw[a][:].rearrange("p j (c i) -> p c j i", i=4))
         scatter(3)
         woven0 = [weave(slice(x * half, (x + 1) * half), woven0_at + x * 8 * half, f"woven0_{x}") for x in range(2)]
         scatter(4)
         w3_s = at(h_at, [P, GROUPS * N], U8, "w3_s")
-        for a in range(GROUPS):
-            flat = w3_g[a][:].rearrange("p n j -> p (n j)")
-            for lo, hi in ((0, 256), (256, N)):
-                nc.vector.quantize_mx(
-                    w3_c[:, a * N + lo : a * N + hi].bitcast(FP8X4), w3_s[:, a * N + lo : a * N + hi], flat[:, PACK * lo : PACK * hi]
-                )
+        for cols in (slice(0, BANK), slice(BANK, GROUPS * N)):
+            nc.vector.quantize_mx(w3_c[:, cols].bitcast(FP8X4), w3_s[:, cols], w3_g[:, cols, :].rearrange("p n j -> p (n j)"))
         scatter(5)
 
         def quantise_half(x):

@@ -21,13 +21,20 @@ PACK = 4
 PASS = P * PACK
 BANK = 512
 GROUPS = H // PASS
+TILES = GROUPS * PACK
+LAST = TILES - 1
 HALVES = S // BANK
 CHUNKS = T2 // BANK
 NT = N // P
-A_BANKS = (4, 5, 6, 7)
-B_BANKS = (2, 3, 0, 1)
+KIB = 1024
+QUADRANTS = 4
+
+W1_BANKS = (4, 5, 6, 7)
+W2_BANKS = (2, 3, 0, 1)
 D_BANKS = (4, 5, 6)
 F_BANKS = (7, 2, 3, 0, 1)
+COPY_BUFFERS = 8
+ROOT_BUFFERS = 4
 
 
 def tile_list_chart_tile_planes_kernel(
@@ -47,16 +54,17 @@ def tile_list_chart_tile_planes_kernel(
             return placed.tile(shape, dtype, name=name, offset=offset, align_bytes=64)
 
         half = T2 // 2
-        row = 4 * S
         tab_at = 0
-        scale_at = tab_at + 4 * T
-        h_at = scale_at + 5 * PASS
-        woven0_at = h_at + 2 * row
-        woven1_at = woven0_at + 8 * T2
-        raw_at = woven1_at + 8 * T2
-        copies_at = raw_at + 8 * row
+        scale_at = tab_at + 8 * KIB
+        h_at = scale_at + 5 * KIB // 2
+        woven0_at = h_at + 8 * KIB
+        woven1_at = woven0_at + 16 * KIB
+        raw_at = woven1_at + 16 * KIB
+        copies_at = raw_at + 32 * KIB
+        w1_late_scales_at = woven0_at - KIB // 2
         h_places = [
-            woven0_at - row // 2, woven0_at - row - PASS, woven0_at, woven0_at + row, h_at, h_at + row, tab_at, woven0_at,
+            woven0_at - 2 * KIB, w1_late_scales_at - 4 * KIB, woven0_at, woven0_at + 4 * KIB,
+            h_at, h_at + 4 * KIB, tab_at, woven0_at,
         ]
 
         idx = held([P, S // 16], U16, "idx")
@@ -68,7 +76,7 @@ def tile_list_chart_tile_planes_kernel(
         w4_w = held([P, GROUPS, N], U32, "w4_w")
         w4_s = held([P, GROUPS, N], U8, "w4_s")
         gain = [held([P, S], F32, f"gain{t}") for t in range(PACK)]
-        page = [held([P, T2], F32, f"page{i}") for i in range(GROUPS * PACK)]
+        page = [held([P, T2], F32, f"page{i}") for i in range(TILES)]
         page_rows = page0.rearrange("(g p t) m -> g t p m", g=GROUPS, t=PACK)
         out_rows = out_1.rearrange("(g p t) m -> g t p m", g=GROUPS, t=PACK)
         wgs_rows = wgs.rearrange("(q t) j -> q t j", t=PACK)
@@ -79,10 +87,10 @@ def tile_list_chart_tile_planes_kernel(
         nc.vector.memset(w2_s[:].bitcast(I32), 0)
         nc.vector.memset(warm[:], 1.0)
         nc.vector.memset(w4_s[:].rearrange("p a n -> p (a n)").bitcast(I32), 0)
-        w1_raw = [at(raw_at + g * 4 * PACK * PASS, [P, PACK, PASS], F32, f"w1_raw{g}") for g in range(GROUPS)]
-        w3_raw = [at(raw_at + 5 * row + a * 4 * PACK * N, [P, PACK, N], F32, f"w3_raw{a}") for a in range(GROUPS)]
+        w1_raw = [at(raw_at + g * 8 * KIB, [P, PACK, PASS], F32, f"w1_raw{g}") for g in range(GROUPS)]
+        w3_raw = [at(raw_at + (20 + 6 * g) * KIB, [P, PACK, N], F32, f"w3_raw{g}") for g in range(GROUPS)]
         w1_cols = w1.rearrange("(p j) (g c) -> g p j c", j=PACK, g=GROUPS)
-        w3_rows = w3.rearrange("(a p j) n -> a p j n", a=GROUPS, j=PACK)
+        w3_rows = w3.rearrange("(g p j) n -> g p j n", g=GROUPS, j=PACK)
 
         def load_page(i):
             nc.sync.dma_start(page[i][:], page_rows[i // PACK, i % PACK])
@@ -93,11 +101,11 @@ def tile_list_chart_tile_planes_kernel(
 
         nc.sync.dma_start(idx[:], offs)
         nc.sync.dma_start(idx2[:], offs2)
-        for q in range(4):
+        for q in range(QUADRANTS):
             nc.sync.dma_start(tab_s[32 * q : 32 * q + 4, :].bitcast(I32), tab_scales[0, 4 * q : 4 * q + 4, :].bitcast(I32))
         nc.sync.dma_start(tab_w[:].bitcast(I32), tab_words[0].rearrange("p n t -> p (n t)").bitcast(I32))
         nc.sync.dma_start(w2_w[:].bitcast(I32), w2_words[0].bitcast(I32))
-        for q in range(4):
+        for q in range(QUADRANTS):
             nc.sync.dma_start(w2_s[32 * q : 32 * q + 4, :].bitcast(I32), w2_scales[0, 4 * q : 4 * q + 4, :].bitcast(I32))
         nc.sync.dma_start(w1_raw[0][:], w1_cols[0])
         nc.scalar.activation(warm_out[:], warm[:], ACT.Abs_reciprocal_sqrt)
@@ -107,13 +115,13 @@ def tile_list_chart_tile_planes_kernel(
         for t in (1, 2):
             load_gain(t)
             load_page(t)
-        for a in range(GROUPS):
-            nc.sync.dma_start(w3_raw[a][:], w3_rows[a])
-        load_gain(3)
-        for i in range(3, GROUPS * PACK):
+        for g in range(GROUPS):
+            nc.sync.dma_start(w3_raw[g][:], w3_rows[g])
+        load_gain(PACK - 1)
+        for i in range(PACK - 1, TILES):
             load_page(i)
         nc.sync.dma_start(w4_w[:].bitcast(I32), w4_words.rearrange("a p n t -> p a (n t)").bitcast(I32))
-        for q in range(4):
+        for q in range(QUADRANTS):
             nc.sync.dma_start(
                 w4_s[32 * q : 32 * q + 4, :, :].bitcast(I32),
                 w4_scales[:, 4 * q : 4 * q + 4, :].rearrange("a r n -> r a n").bitcast(I32),
@@ -121,65 +129,71 @@ def tile_list_chart_tile_planes_kernel(
 
         v_s = held([P, S], U8, "v_s")
         w1_c = [held([P, PASS], U32, f"w1_c{g}") for g in range(GROUPS)]
-
         nc.vector.tensor_copy(v_s[:], tab_s[:].indirect(idx[:]))
         w1_s = {}
 
-        def group_w1(g, lo, hi, offset):
-            grouped = at(offset, [P, hi - lo, P, PACK], BF16, f"w1_g{g}_{lo}")
-            dealt = w1_raw[g][:].rearrange("p j (m t) -> p m j t", t=PACK)
-            nc.scalar.copy(grouped[:].rearrange("p t m j -> p m j t"), dealt[:, :, :, lo:hi])
-            return grouped
+        def dealt_w1(g):
+            return w1_raw[g][:].rearrange("p j (m t) -> p m j t", t=PACK)
 
-        def quantise_w1(g, lo, hi, grouped, offset):
+        def round_w1(g, lo, hi, offset):
+            rounded = at(offset, [P, hi - lo, P, PACK], BF16, f"w1_rounded{g}_{lo}")
+            nc.scalar.copy(rounded[:].rearrange("p t m j -> p m j t"), dealt_w1(g)[:, :, :, lo:hi])
+            return rounded
+
+        def quantise_w1(g, lo, hi, rounded, offset):
             scales = at(offset, [P, (hi - lo) * P], U8, f"w1_s{g}_{lo}")
-            nc.vector.quantize_mx(w1_c[g][:, lo * P : hi * P].bitcast(FP8X4), scales[:], grouped[:].rearrange("p t m j -> p (t m j)"))
+            nc.vector.quantize_mx(w1_c[g][:, lo * P : hi * P].bitcast(FP8X4), scales[:], rounded[:].rearrange("p t m j -> p (t m j)"))
             for t in range(lo, hi):
                 w1_s[PACK * g + t] = scales[:, (t - lo) * P : (t - lo + 1) * P]
 
-        first = {}
-        second = {}
+        def w1_product(i, u, bank):
+            g, t = divmod(i, PACK)
+            product = psum.tile([P, BANK], F32, name="w1_product", tag=f"bank{bank}")
+            nc.tensor.matmul_mx(
+                product[:], lhsT=w1_c[g][:, t * P : (t + 1) * P].bitcast(FP8X4), lhsT_scale=w1_s[i],
+                rhs=v_w[u][:].bitcast(FP8X4), rhs_scale=v_s[:, u * BANK : (u + 1) * BANK], start=True, stop=True,
+            )
+            return product
+
+        def w2_products(i):
+            products = []
+            for u in range(HALVES):
+                products.append(psum.tile([P, BANK], F32, name="w2_product", tag=f"bank{W2_BANKS[2 * (i % 2) + u]}"))
+                nc.tensor.matmul_mx(
+                    products[u][:], lhsT=w2_dw[:, 2 * i * P : 2 * (i + 1) * P].bitcast(FP4X4),
+                    lhsT_scale=w2_ds[:, i * P : (i + 1) * P],
+                    rhs=v_w[u][:].bitcast(FP8X4), rhs_scale=v_s[:, u * BANK : (u + 1) * BANK], start=True, stop=True,
+                )
+            return products
+
+        in_sbuf = {}
         h = {}
 
-        def first_reading(i, halves=range(HALVES)):
-            g, t = divmod(i, PACK)
-            cols = slice(t * P, (t + 1) * P)
-            for u in halves:
-                picked = slice(u * BANK, (u + 1) * BANK)
-                a = psum.tile([P, BANK], F32, name="a", tag=f"bank{B_BANKS[2 * (1 - i) + u] if i < 2 else A_BANKS[2 * (i % 2) + u]}")
-                nc.tensor.matmul_mx(
-                    a[:], lhsT=w1_c[g][:, cols].bitcast(FP8X4), lhsT_scale=w1_s[i],
-                    rhs=v_w[u][:].bitcast(FP8X4), rhs_scale=v_s[:, picked], start=True, stop=True,
-                )
-                first[(i, u)] = a
-                if i > 0:
-                    first[(i, u)] = at(copies_at + 4 * BANK * ((2 * i + u) % 8), [P, BANK], F32, f"a_sb{i}_{u}")
-                    nc.scalar.copy(first[(i, u)][:], a[:])
+        def copied_w1_products(i, banks):
+            in_sbuf[i] = []
+            for u in range(HALVES):
+                product = w1_product(i, u, banks[u])
+                buffer = (HALVES * i + u) % COPY_BUFFERS
+                in_sbuf[i].append(at(copies_at + 2 * KIB * buffer, [P, BANK], F32, f"w1_copy{i}_{u}"))
+                nc.scalar.copy(in_sbuf[i][u][:], product[:])
 
-        def second_reading(i, halves=range(HALVES)):
-            for u in halves:
-                picked = slice(u * BANK, (u + 1) * BANK)
-                second[(i, u)] = psum.tile([P, BANK], F32, name="b", tag=f"bank{B_BANKS[2 * (i % 2) + u]}")
-                nc.tensor.matmul_mx(
-                    second[(i, u)][:], lhsT=w2_dw[:, 2 * i * P : 2 * (i + 1) * P].bitcast(FP4X4),
-                    lhsT_scale=w2_ds[:, i * P : (i + 1) * P],
-                    rhs=v_w[u][:].bitcast(FP8X4), rhs_scale=v_s[:, picked], start=True, stop=True,
-                )
+        def w1_banks(i):
+            return W1_BANKS[2 * (i % 2) : 2 * (i % 2) + 2]
 
-        def larger(i):
+        def larger(i, in_psum):
             h[i] = at(h_places[i], [P, S], F32, f"h{i}")
             for u in range(HALVES):
-                nc.vector.tensor_tensor(h[i][:, u * BANK : (u + 1) * BANK], second[(i, u)][:], first[(i, u)][:], ALU.max)
-
-        pairs = []
+                nc.vector.tensor_tensor(h[i][:, u * BANK : (u + 1) * BANK], in_psum[u][:], in_sbuf[i][u][:], ALU.max)
 
         def scatter(i):
+            nc.vector.tensor_tensor(page[i][:].indirect(idx2[:]), h[i][:], gain[i % PACK][:], ALU.mult)
+            nc.sync.dma_start(out_rows[i // PACK, i % PACK], page[i][:])
+
+        def scatter_and_round(i):
+            scatter(i)
             t = i % PACK
-            nc.vector.tensor_tensor(page[i][:].indirect(idx2[:]), h[i][:], gain[t][:], ALU.mult)
-            nc.sync.dma_start(out_rows[i // PACK, t], page[i][:])
-            if i + 1 < GROUPS * PACK:
-                for x in range(2):
-                    nc.scalar.copy(pairs[x][:, t // 2, :, t % 2], page[i][:, x * half : (x + 1) * half])
+            for x in range(2):
+                nc.scalar.copy(pairs[x][:, t // 2, :, t % 2], page[i][:, x * half : (x + 1) * half])
 
         def weave(cols, offset, name):
             x, lo = divmod(cols.start, half)
@@ -195,18 +209,20 @@ def tile_list_chart_tile_planes_kernel(
         p_s = [held([P, T2], U8, f"p_s{g}") for g in range(GROUPS)]
         w3_c = held([P, GROUPS * N], U32, "w3_c")
 
+        def quantise_page(g, cols, woven):
+            nc.vector.quantize_mx(p_c[g][:, cols].bitcast(FP8X4), p_s[g][:, cols], woven[:].rearrange("p m t -> p (m t)"))
+
         def store_words(g, cols):
             nc.sync.dma_start(out_2[g].rearrange("p m t -> p (m t)").bitcast(I32)[:, cols], p_c[g][:, cols].bitcast(I32))
 
         def store_scales(g):
-            for q in range(4):
+            for q in range(QUADRANTS):
                 nc.sync.dma_start(out_3[g, 4 * q : 4 * q + 4, :].bitcast(I32), p_s[g][32 * q : 32 * q + 4, :].bitcast(I32))
 
-        front = at(woven1_at + 2 * PASS, [P, 2, P, PACK], BF16, "w1_front")
+        front = at(woven1_at + KIB, [P, 2, P, PACK], BF16, "w1_front")
         front_view = front[:].rearrange("p t m j -> p m j t")
-        front_raw = w1_raw[0][:].rearrange("p j (m t) -> p m j t", t=PACK)
-        nc.scalar.copy(front_view[:, : P // 2], front_raw[:, : P // 2, :, 0:2])
-        back = group_w1(0, 2, PACK, woven1_at + 12 * PASS)
+        nc.scalar.copy(front_view[:, : P // 2], dealt_w1(0)[:, : P // 2, :, 0:2])
+        back = round_w1(0, 2, PACK, woven1_at + 6 * KIB)
         v_w = [held([P, BANK], U32, "v_w0")]
         nc.vector.tensor_copy(v_w[0][:], tab_w[:].indirect(idx[:, : BANK // 16]))
         w2_dw = held([P, 2 * H], U8, "w2_dw")
@@ -219,70 +235,67 @@ def tile_list_chart_tile_planes_kernel(
             w2_ds[:].rearrange("p (g t m) -> p g t m", g=GROUPS, t=PACK),
             w2_s[:].rearrange("p (g m t) -> p g t m", g=GROUPS, t=PACK),
         )
-        v_w.append(at(scale_at + PASS, [P, BANK], U32, "v_w1"))
+        v_w.append(at(scale_at + KIB // 2, [P, BANK], U32, "v_w1"))
         nc.vector.tensor_copy(v_w[1][:], tab_w[:].indirect(idx[:, BANK // 16 :]))
-        nc.vector.tensor_copy(front_view[:, P // 2 :], front_raw[:, P // 2 :, :, 0:2])
+        nc.vector.tensor_copy(front_view[:, P // 2 :], dealt_w1(0)[:, P // 2 :, :, 0:2])
         quantise_w1(0, 0, 2, front, scale_at)
-        second_reading(0)
-        first_reading(0)
-        quantise_w1(0, 2, PACK, back, woven1_at + 10 * PASS)
+        early = w2_products(0)
+        late = [w1_product(0, u, W2_BANKS[2 + u]) for u in range(HALVES)]
+        quantise_w1(0, 2, PACK, back, woven1_at + 5 * KIB)
+        in_sbuf[0] = []
         for u in range(HALVES):
-            copied = at(woven1_at + 4 * u * PASS, [P, BANK], F32, f"b_sb{u}")
-            nc.scalar.copy(copied[:], second[(0, u)][:])
-            second[(0, u)] = first[(0, u)]
-            first[(0, u)] = copied
-        larger(0)
+            in_sbuf[0].append(at(woven1_at + 2 * KIB * u, [P, BANK], F32, f"w2_copy{u}"))
+            nc.scalar.copy(in_sbuf[0][u][:], early[u][:])
+        larger(0, late)
+        copied_w1_products(1, W2_BANKS[0:2])
+        for i in range(2, PACK):
+            copied_w1_products(i, w1_banks(i))
+        rounded1 = round_w1(1, 0, PACK, woven1_at)
+        pairs = [at(raw_at + (4 + 8 * x) * KIB, [P, 2, half, 2], BF16, f"pairs{x}") for x in range(2)]
+
+        scatter_and_round(0)
         for i in range(1, PACK):
-            first_reading(i)
-        grouped1 = group_w1(1, 0, PACK, woven1_at)
-        pairs.extend(at(raw_at + (1 + 2 * x) * row, [P, 2, half, 2], BF16, f"pairs{x}") for x in range(2))
-        scatter(0)
-        for i in range(1, PACK):
-            second_reading(i)
-            larger(i)
-        quantise_w1(1, 0, PACK, grouped1, woven0_at - PASS)
-        for i in range(PACK, GROUPS * PACK):
-            first_reading(i)
-        scatter(1)
-        for i in range(PACK, GROUPS * PACK - 1):
-            second_reading(i)
-            larger(i)
-        second_reading(GROUPS * PACK - 1)
-        scatter(2)
-        w3_g = at(woven1_at + 16 * PASS, [P, GROUPS * N, PACK], BF16, "w3_g")
-        for a in range(GROUPS):
-            nc.scalar.copy(w3_g[:, a * N : (a + 1) * N, :].rearrange("p (c i) j -> p c j i", i=4), w3_raw[a][:].rearrange("p j (c i) -> p c j i", i=4))
-        scatter(3)
-        woven0 = [weave(slice(x * half, (x + 1) * half), woven0_at + x * 8 * half, f"woven0_{x}") for x in range(2)]
-        scatter(4)
+            larger(i, w2_products(i))
+        quantise_w1(1, 0, PACK, rounded1, w1_late_scales_at)
+        for i in range(PACK, TILES):
+            copied_w1_products(i, w1_banks(i))
+        scatter_and_round(1)
+        for i in range(PACK, LAST):
+            larger(i, w2_products(i))
+        last_products = w2_products(LAST)
+        scatter_and_round(2)
+        w3_rounded = at(woven1_at + 8 * KIB, [P, GROUPS * N, PACK], BF16, "w3_rounded")
+        for g in range(GROUPS):
+            nc.scalar.copy(
+                w3_rounded[:, g * N : (g + 1) * N, :].rearrange("p (c i) j -> p c j i", i=4),
+                w3_raw[g][:].rearrange("p j (c i) -> p c j i", i=4),
+            )
+        scatter_and_round(3)
+        page_halves = [slice(x * half, (x + 1) * half) for x in range(2)]
+        woven0 = [weave(cols, woven0_at + 8 * cols.start, f"woven0_{cols.start}") for cols in page_halves]
+        scatter_and_round(4)
         w3_s = at(h_at, [P, GROUPS * N], U8, "w3_s")
         for cols in (slice(0, BANK), slice(BANK, GROUPS * N)):
-            nc.vector.quantize_mx(w3_c[:, cols].bitcast(FP8X4), w3_s[:, cols], w3_g[:, cols, :].rearrange("p n j -> p (n j)"))
-        scatter(5)
-
-        def quantise_half(x):
-            cols = slice(x * half, (x + 1) * half)
-            nc.vector.quantize_mx(p_c[0][:, cols].bitcast(FP8X4), p_s[0][:, cols], woven0[x][:].rearrange("p m t -> p (m t)"))
-            store_words(0, cols)
-
-        quantise_half(0)
-        larger(GROUPS * PACK - 1)
-        scatter(6)
-        quantise_half(1)
+            nc.vector.quantize_mx(w3_c[:, cols].bitcast(FP8X4), w3_s[:, cols], w3_rounded[:, cols, :].rearrange("p n j -> p (n j)"))
+        scatter_and_round(5)
+        quantise_page(0, page_halves[0], woven0[0])
+        store_words(0, page_halves[0])
+        larger(LAST, last_products)
+        scatter_and_round(6)
+        quantise_page(0, page_halves[1], woven0[1])
+        store_words(0, page_halves[1])
         store_scales(0)
 
-        whole = [(slice(c * BANK, (c + 1) * BANK), n) for c in range(CHUNKS) for n in range(NT)]
+        def halved(cols):
+            middle = (cols.start + cols.stop) // 2
+            return [slice(cols.start, middle), slice(middle, cols.stop)]
 
-        def halved(unit):
-            cols, n = unit
-            middle = cols.start + BANK // 2
-            return [(slice(cols.start, middle), n), (slice(middle, cols.stop), n)]
-
-        units = halved(whole[0]) + whole[1:-1] + halved(whole[-1])
-        pieces = [cols for cols, n in halved(whole[0])] + [cols for cols, n in whole[NT::NT]]
+        chunks = [slice(c * BANK, (c + 1) * BANK) for c in range(CHUNKS)]
+        units = [(cols, n) for cols in chunks for n in range(NT)][:-1] + [(cols, NT - 1) for cols in halved(chunks[-1])]
+        pieces = halved(chunks[0]) + chunks[1:]
         woven1 = [weave(cols, woven1_at + 8 * cols.start, f"woven1_{cols.start}") for cols in pieces]
-        scatter(GROUPS * PACK - 1)
-        staged = [at(raw_at + n * 4 * T2, [P, T2], F32, f"staged{n}") for n in range(NT)]
+        scatter(LAST)
+        staged = [at(raw_at + n * 8 * KIB, [P, T2], F32, f"staged{n}") for n in range(NT)]
         d_of = {}
         f_of = {}
 
@@ -292,7 +305,7 @@ def tile_list_chart_tile_planes_kernel(
                 d_of[k] = psum.tile([P, cols.stop - cols.start], F32, name="d", tag=f"bank{D_BANKS[k % len(D_BANKS)]}")
             nc.tensor.matmul_mx(
                 d_of[k][:], lhsT=w4_w[:, g, n * P : (n + 1) * P].bitcast(FP8X4), lhsT_scale=w4_s[:, g, n * P : (n + 1) * P],
-                rhs=p_c[g][:, cols].bitcast(FP8X4), rhs_scale=p_s[g][:, cols], start=(g == 0), stop=(g == 1),
+                rhs=p_c[g][:, cols].bitcast(FP8X4), rhs_scale=p_s[g][:, cols], start=(g == 0), stop=(g == GROUPS - 1),
             )
 
         def f_pass(k, g):
@@ -302,59 +315,53 @@ def tile_list_chart_tile_planes_kernel(
             wcols = slice(g * N + n * P, g * N + (n + 1) * P)
             nc.tensor.matmul_mx(
                 f_of[k][:], lhsT=w3_c[:, wcols].bitcast(FP8X4), lhsT_scale=w3_s[:, wcols],
-                rhs=p_c[g][:, cols].bitcast(FP8X4), rhs_scale=p_s[g][:, cols], start=(g == 0), stop=(g == 1),
+                rhs=p_c[g][:, cols].bitcast(FP8X4), rhs_scale=p_s[g][:, cols], start=(g == 0), stop=(g == GROUPS - 1),
             )
 
-        root_of = {}
-        part_of = {}
+        def store_unit(k, left, right):
+            cols, n = units[k]
+            nc.vector.tensor_tensor(staged[n][:, cols], left[:], right[:], ALU.mult)
+            nc.sync.dma_start(out_0[n * P : (n + 1) * P, cols], staged[n][:, cols])
 
-        def damping(k):
+        def damp(k):
             cols, n = units[k]
             width = cols.stop - cols.start
-            sq = at(copies_at + 4 * BANK * (k % 8), [P, width], F32, f"sq{k}")
-            root = at(tab_at + 4 * BANK * (k % 4), [P, width], F32, f"root{k}")
-            nc.scalar.activation(sq[:], d_of[k][:], ACT.Square)
-            nc.scalar.activation(root[:], sq[:], ACT.Abs_reciprocal_sqrt, bias=1.0)
+            scratch = at(copies_at + 2 * KIB * (k % COPY_BUFFERS), [P, width], F32, f"scratch{k}")
+            root = at(tab_at + 2 * KIB * (k % ROOT_BUFFERS), [P, width], F32, f"root{k}")
+            nc.scalar.activation(scratch[:], d_of[k][:], ACT.Square)
+            nc.scalar.activation(root[:], scratch[:], ACT.Abs_reciprocal_sqrt, bias=1.0)
             if width < BANK:
-                nc.scalar.activation(sq[:], root[:], ACT.Square)
-                nc.vector.tensor_tensor(staged[n][:, cols], f_of[k][:], sq[:], ALU.mult)
-                nc.sync.dma_start(out_0[n * P : (n + 1) * P, cols], staged[n][:, cols])
-            else:
-                nc.vector.tensor_tensor(sq[:], f_of[k][:], root[:], ALU.mult)
-                root_of[k] = root
-                part_of[k] = sq
+                nc.scalar.activation(scratch[:], root[:], ACT.Square)
+                store_unit(k, f_of[k], scratch)
+                return []
+            nc.vector.tensor_tensor(scratch[:], f_of[k][:], root[:], ALU.mult)
+            return [(k, scratch, root)]
 
-        def finish(k):
-            cols, n = units[k]
-            nc.vector.tensor_tensor(staged[n][:, cols], part_of[k][:], root_of[k][:], ALU.mult)
-            nc.sync.dma_start(out_0[n * P : (n + 1) * P, cols], staged[n][:, cols])
+        def fill(j, copy):
+            copy(woven1[j][:, :, PACK - 1], page[LAST][:, pieces[j]])
+
+        def quantise_piece(j):
+            cols = pieces[j]
+            quantise_page(1, cols, woven1[j])
+            if cols.stop % BANK == 0:
+                store_words(1, slice(cols.stop - BANK, cols.stop))
 
         for k in range(len(D_BANKS)):
             d_pass(k, 0)
         for k in range(len(F_BANKS)):
             f_pass(k, 0)
-        final = GROUPS * PACK - 1
-
-        def fill(j):
-            copy = nc.scalar.copy if j == 2 else nc.vector.tensor_copy
-            copy(woven1[j][:, :, PACK - 1], page[final][:, pieces[j]])
-
-        def quantise_piece(j):
-            cols = pieces[j]
-            nc.vector.quantize_mx(p_c[1][:, cols].bitcast(FP8X4), p_s[1][:, cols], woven1[j][:].rearrange("p m t -> p (m t)"))
-            if cols.stop % BANK == 0:
-                store_words(1, slice(cols.stop - BANK, cols.stop))
-
-        for j in range(3):
-            fill(j)
+        fill(0, nc.vector.tensor_copy)
+        fill(1, nc.vector.tensor_copy)
+        fill(2, nc.scalar.copy)
         quantise_piece(0)
-        fill(3)
+        fill(3, nc.vector.tensor_copy)
         quantise_piece(1)
         quantise_piece(2)
-        fill(4)
+        fill(4, nc.vector.tensor_copy)
         quantise_piece(3)
         quantise_piece(4)
         store_scales(1)
+        waiting = []
         for k in range(len(units)):
             if k >= len(D_BANKS):
                 d_pass(k, 0)
@@ -362,6 +369,7 @@ def tile_list_chart_tile_planes_kernel(
             if k >= len(F_BANKS):
                 f_pass(k, 0)
             f_pass(k, 1)
-            damping(k)
-            if k - 1 in part_of:
-                finish(k - 1)
+            following = damp(k)
+            for earlier, part, root in waiting:
+                store_unit(earlier, part, root)
+            waiting = following

@@ -31,8 +31,8 @@ QUADRANTS = 4
 
 W1_BANKS = (4, 5, 6, 7)
 W2_BANKS = (2, 3, 0, 1)
-D_BANKS = (4, 5, 6)
-F_BANKS = (7, 2, 3, 0, 1)
+BANKS = (4, 5, 6, 7, 2, 3, 0, 1)
+D_LEAD = 3
 COPY_BUFFERS = 8
 ROOT_BUFFERS = 4
 
@@ -55,24 +55,26 @@ def tile_list_chart_tile_planes_kernel(
 
         half = T2 // 2
         tab_at = 0
-        scale_at = tab_at + 8 * KIB
-        h_at = scale_at + 5 * KIB // 2
+        words_at = tab_at + 8 * KIB
+        head_at = words_at + 2 * KIB
+        h_at = head_at + 15 * KIB // 2
         woven0_at = h_at + 8 * KIB
         woven1_at = woven0_at + 16 * KIB
         raw_at = woven1_at + 16 * KIB
         copies_at = raw_at + 32 * KIB
+        late_at = copies_at + 16 * KIB
         w1_late_scales_at = woven0_at - KIB // 2
         h_places = [
             woven0_at - 2 * KIB, w1_late_scales_at - 4 * KIB, woven0_at, woven0_at + 4 * KIB,
-            h_at, h_at + 4 * KIB, tab_at, woven0_at,
+            h_at, h_at + 4 * KIB, late_at, woven0_at,
         ]
 
         idx = held([P, S // 16], U16, "idx")
         idx2 = held([P, S // 16], U16, "idx2")
         tab_w = at(tab_at, [P, T], U32, "tab_w")
         tab_s = held([P, T], U8, "tab_s")
-        w2_w = held([P, 2 * H], U8, "w2_w")
-        w2_s = at(scale_at, [P, H], U8, "w2_s")
+        w2_w = [at(words_at, [P, 2 * PASS], U8, "w2_w0"), held([P, 2 * PASS], U8, "w2_w1")]
+        w2_s = held([P, H], U8, "w2_s")
         w4_w = held([P, GROUPS, N], U32, "w4_w")
         w4_s = held([P, GROUPS, N], U8, "w4_s")
         gain = [held([P, S], F32, f"gain{t}") for t in range(PACK)]
@@ -104,10 +106,11 @@ def tile_list_chart_tile_planes_kernel(
         for q in range(QUADRANTS):
             nc.sync.dma_start(tab_s[32 * q : 32 * q + 4, :].bitcast(I32), tab_scales[0, 4 * q : 4 * q + 4, :].bitcast(I32))
         nc.sync.dma_start(tab_w[:].bitcast(I32), tab_words[0].rearrange("p n t -> p (n t)").bitcast(I32))
-        nc.sync.dma_start(w2_w[:].bitcast(I32), w2_words[0].bitcast(I32))
         for q in range(QUADRANTS):
             nc.sync.dma_start(w2_s[32 * q : 32 * q + 4, :].bitcast(I32), w2_scales[0, 4 * q : 4 * q + 4, :].bitcast(I32))
+        nc.sync.dma_start(w2_w[0][:].bitcast(I32), w2_words[0, :, : 2 * PASS].bitcast(I32))
         nc.sync.dma_start(w1_raw[0][:], w1_cols[0])
+        nc.sync.dma_start(w2_w[1][:].bitcast(I32), w2_words[0, :, 2 * PASS :].bitcast(I32))
         nc.scalar.activation(warm_out[:], warm[:], ACT.Abs_reciprocal_sqrt)
         load_page(0)
         load_gain(0)
@@ -156,12 +159,13 @@ def tile_list_chart_tile_planes_kernel(
             return product
 
         def w2_products(i):
+            g, t = divmod(i, PACK)
             products = []
             for u in range(HALVES):
                 products.append(psum.tile([P, BANK], F32, name="w2_product", tag=f"bank{W2_BANKS[2 * (i % 2) + u]}"))
                 nc.tensor.matmul_mx(
-                    products[u][:], lhsT=w2_dw[:, 2 * i * P : 2 * (i + 1) * P].bitcast(FP4X4),
-                    lhsT_scale=w2_ds[:, i * P : (i + 1) * P],
+                    products[u][:], lhsT=w2_dw[g][:, 2 * t * P : 2 * (t + 1) * P].bitcast(FP4X4),
+                    lhsT_scale=w2_ds[g][:, t * P : (t + 1) * P],
                     rhs=v_w[u][:].bitcast(FP8X4), rhs_scale=v_s[:, u * BANK : (u + 1) * BANK], start=True, stop=True,
                 )
             return products
@@ -192,25 +196,20 @@ def tile_list_chart_tile_planes_kernel(
         def scatter_and_round(i):
             scatter(i)
             t = i % PACK
-            for x in range(2):
-                nc.scalar.copy(pairs[x][:, t // 2, :, t % 2], page[i][:, x * half : (x + 1) * half])
+            nc.scalar.copy(pairs[:, t // 2, :, t % 2], page[i][:])
 
         def weave(cols, offset, name):
-            x, lo = divmod(cols.start, half)
-            width = cols.stop - cols.start
-            woven = at(offset, [P, width, PACK], BF16, name)
-            words = pairs[x][:].rearrange("p u m b -> p (u m b)").bitcast(U32).rearrange("p (u m) -> p m u", u=2)
-            nc.scalar.copy(
-                woven[:].rearrange("p m t -> p (m t)").bitcast(U32).rearrange("p (m u) -> p m u", u=2), words[:, lo : lo + width, :]
-            )
+            woven = at(offset, [P, (cols.stop - cols.start) * PACK], BF16, name)
+            words = pairs[:].rearrange("p u m b -> p (u m b)").bitcast(U32).rearrange("p (u m) -> p m u", u=2)
+            nc.scalar.copy(woven[:].bitcast(U32).rearrange("p (m u) -> p m u", u=2), words[:, cols, :])
             return woven
 
         p_c = [held([P, T2], U32, f"p_c{g}") for g in range(GROUPS)]
-        p_s = [held([P, T2], U8, f"p_s{g}") for g in range(GROUPS)]
+        p_s = {1: held([P, T2], U8, "p_s1")}
         w3_c = held([P, GROUPS * N], U32, "w3_c")
 
         def quantise_page(g, cols, woven):
-            nc.vector.quantize_mx(p_c[g][:, cols].bitcast(FP8X4), p_s[g][:, cols], woven[:].rearrange("p m t -> p (m t)"))
+            nc.vector.quantize_mx(p_c[g][:, cols].bitcast(FP8X4), p_s[g][:, cols], woven)
 
         def store_words(g, cols):
             nc.sync.dma_start(out_2[g].rearrange("p m t -> p (m t)").bitcast(I32)[:, cols], p_c[g][:, cols].bitcast(I32))
@@ -219,39 +218,43 @@ def tile_list_chart_tile_planes_kernel(
             for q in range(QUADRANTS):
                 nc.sync.dma_start(out_3[g, 4 * q : 4 * q + 4, :].bitcast(I32), p_s[g][32 * q : 32 * q + 4, :].bitcast(I32))
 
-        front = at(woven1_at + KIB, [P, 2, P, PACK], BF16, "w1_front")
-        front_view = front[:].rearrange("p t m j -> p m j t")
-        nc.scalar.copy(front_view[:, : P // 2], dealt_w1(0)[:, : P // 2, :, 0:2])
-        back = round_w1(0, 2, PACK, woven1_at + 6 * KIB)
+        front = round_w1(0, 0, 2, head_at + 7 * KIB // 4)
+        back = round_w1(0, 2, PACK, head_at + 11 * KIB // 2)
         v_w = [held([P, BANK], U32, "v_w0")]
         nc.vector.tensor_copy(v_w[0][:], tab_w[:].indirect(idx[:, : BANK // 16]))
-        w2_dw = held([P, 2 * H], U8, "w2_dw")
-        nc.vector.tensor_copy(
-            w2_dw[:].bitcast(U16).rearrange("p (g t m) -> p g t m", g=GROUPS, t=PACK),
-            w2_w[:].bitcast(U16).rearrange("p (g m t) -> p g t m", g=GROUPS, t=PACK),
-        )
-        w2_ds = held([P, H], U8, "w2_ds")
-        nc.vector.tensor_copy(
-            w2_ds[:].rearrange("p (g t m) -> p g t m", g=GROUPS, t=PACK),
-            w2_s[:].rearrange("p (g m t) -> p g t m", g=GROUPS, t=PACK),
-        )
-        v_w.append(at(scale_at + KIB // 2, [P, BANK], U32, "v_w1"))
+
+        def deal_w2(g, words, scales):
+            nc.vector.tensor_copy(
+                scales[:].rearrange("p (t m) -> p t m", t=PACK),
+                w2_s[:, g * PASS : (g + 1) * PASS].rearrange("p (m t) -> p t m", t=PACK),
+            )
+            nc.vector.tensor_copy(
+                words[:].bitcast(U16).rearrange("p (t m) -> p t m", t=PACK),
+                w2_w[g][:].bitcast(U16).rearrange("p (m t) -> p t m", t=PACK),
+            )
+
+        w2_dw = [held([P, 2 * PASS], U8, "w2_dw0")]
+        w2_ds = [held([P, PASS], U8, "w2_ds0")]
+        deal_w2(0, w2_dw[0], w2_ds[0])
+        v_w.append(at(words_at, [P, BANK], U32, "v_w1"))
         nc.vector.tensor_copy(v_w[1][:], tab_w[:].indirect(idx[:, BANK // 16 :]))
-        nc.vector.tensor_copy(front_view[:, P // 2 :], dealt_w1(0)[:, P // 2 :, :, 0:2])
-        quantise_w1(0, 0, 2, front, scale_at)
+        quantise_w1(0, 0, 2, front, tab_at)
+        w2_dw.append(at(head_at + 5 * KIB // 2, [P, 2 * PASS], U8, "w2_dw1"))
+        w2_ds.append(at(head_at + 2 * KIB, [P, PASS], U8, "w2_ds1"))
+        deal_w2(1, w2_dw[1], w2_ds[1])
         early = w2_products(0)
         late = [w1_product(0, u, W2_BANKS[2 + u]) for u in range(HALVES)]
-        quantise_w1(0, 2, PACK, back, woven1_at + 5 * KIB)
+        quantise_w1(0, 2, PACK, back, tab_at + KIB)
         in_sbuf[0] = []
         for u in range(HALVES):
-            in_sbuf[0].append(at(woven1_at + 2 * KIB * u, [P, BANK], F32, f"w2_copy{u}"))
+            in_sbuf[0].append(at(head_at + 7 * KIB // 2 * u, [P, BANK], F32, f"w2_copy{u}"))
             nc.scalar.copy(in_sbuf[0][u][:], early[u][:])
         larger(0, late)
         copied_w1_products(1, W2_BANKS[0:2])
         for i in range(2, PACK):
             copied_w1_products(i, w1_banks(i))
-        rounded1 = round_w1(1, 0, PACK, woven1_at)
-        pairs = [at(raw_at + (4 + 8 * x) * KIB, [P, 2, half, 2], BF16, f"pairs{x}") for x in range(2)]
+        rounded1 = round_w1(1, 0, PACK, head_at + 7 * KIB // 2)
+        pairs = at(raw_at + 4 * KIB, [P, 2, T2, 2], BF16, "pairs")
 
         scatter_and_round(0)
         for i in range(1, PACK):
@@ -273,16 +276,16 @@ def tile_list_chart_tile_planes_kernel(
         scatter_and_round(3)
         page_halves = [slice(x * half, (x + 1) * half) for x in range(2)]
         woven0 = [weave(cols, woven0_at + 8 * cols.start, f"woven0_{cols.start}") for cols in page_halves]
-        scatter_and_round(4)
-        w3_s = at(h_at, [P, GROUPS * N], U8, "w3_s")
+        for i in range(PACK, LAST):
+            scatter_and_round(i)
+        w3_s = at(late_at, [P, GROUPS * N], U8, "w3_s")
+        p_s[0] = at(late_at + KIB, [P, T2], U8, "p_s0")
         for cols in (slice(0, BANK), slice(BANK, GROUPS * N)):
             nc.vector.quantize_mx(w3_c[:, cols].bitcast(FP8X4), w3_s[:, cols], w3_rounded[:, cols, :].rearrange("p n j -> p (n j)"))
-        scatter_and_round(5)
-        quantise_page(0, page_halves[0], woven0[0])
+        quantise_page(0, page_halves[0], woven0[0][:])
         store_words(0, page_halves[0])
         larger(LAST, last_products)
-        scatter_and_round(6)
-        quantise_page(0, page_halves[1], woven0[1])
+        quantise_page(0, page_halves[1], woven0[1][:])
         store_words(0, page_halves[1])
         store_scales(0)
 
@@ -293,7 +296,13 @@ def tile_list_chart_tile_planes_kernel(
         chunks = [slice(c * BANK, (c + 1) * BANK) for c in range(CHUNKS)]
         units = [(cols, n) for cols in chunks for n in range(NT)][:-1] + [(cols, NT - 1) for cols in halved(chunks[-1])]
         pieces = halved(chunks[0]) + chunks[1:]
-        woven1 = [weave(cols, woven1_at + 8 * cols.start, f"woven1_{cols.start}") for cols in pieces]
+        spans = [chunks[0], chunks[-1], slice(BANK, 3 * BANK)]
+        woven1 = [weave(cols, woven1_at + 8 * cols.start, f"woven1_{cols.start}") for cols in spans]
+
+        def woven_part(cols):
+            j = [span.start <= cols.start < span.stop for span in spans].index(True)
+            return woven1[j][:, PACK * (cols.start - spans[j].start) : PACK * (cols.stop - spans[j].start)]
+
         scatter(LAST)
         staged = [at(raw_at + n * 8 * KIB, [P, T2], F32, f"staged{n}") for n in range(NT)]
         d_of = {}
@@ -302,7 +311,7 @@ def tile_list_chart_tile_planes_kernel(
         def d_pass(k, g):
             cols, n = units[k]
             if g == 0:
-                d_of[k] = psum.tile([P, cols.stop - cols.start], F32, name="d", tag=f"bank{D_BANKS[k % len(D_BANKS)]}")
+                d_of[k] = psum.tile([P, cols.stop - cols.start], F32, name="d", tag=f"bank{BANKS[sums.index((d_pass, k)) % len(BANKS)]}")
             nc.tensor.matmul_mx(
                 d_of[k][:], lhsT=w4_w[:, g, n * P : (n + 1) * P].bitcast(FP8X4), lhsT_scale=w4_s[:, g, n * P : (n + 1) * P],
                 rhs=p_c[g][:, cols].bitcast(FP8X4), rhs_scale=p_s[g][:, cols], start=(g == 0), stop=(g == GROUPS - 1),
@@ -311,7 +320,7 @@ def tile_list_chart_tile_planes_kernel(
         def f_pass(k, g):
             cols, n = units[k]
             if g == 0:
-                f_of[k] = psum.tile([P, cols.stop - cols.start], F32, name="f", tag=f"bank{F_BANKS[k % len(F_BANKS)]}")
+                f_of[k] = psum.tile([P, cols.stop - cols.start], F32, name="f", tag=f"bank{BANKS[sums.index((f_pass, k)) % len(BANKS)]}")
             wcols = slice(g * N + n * P, g * N + (n + 1) * P)
             nc.tensor.matmul_mx(
                 f_of[k][:], lhsT=w3_c[:, wcols].bitcast(FP8X4), lhsT_scale=w3_s[:, wcols],
@@ -330,7 +339,7 @@ def tile_list_chart_tile_planes_kernel(
             root = at(tab_at + 2 * KIB * (k % ROOT_BUFFERS), [P, width], F32, f"root{k}")
             nc.scalar.activation(scratch[:], d_of[k][:], ACT.Square)
             nc.scalar.activation(root[:], scratch[:], ACT.Abs_reciprocal_sqrt, bias=1.0)
-            if width < BANK:
+            if k >= len(units) - 3:
                 nc.scalar.activation(scratch[:], root[:], ACT.Square)
                 store_unit(k, f_of[k], scratch)
                 return []
@@ -338,37 +347,39 @@ def tile_list_chart_tile_planes_kernel(
             return [(k, scratch, root)]
 
         def fill(j, copy):
-            copy(woven1[j][:, :, PACK - 1], page[LAST][:, pieces[j]])
+            copy(woven_part(pieces[j]).rearrange("p (m t) -> p m t", t=PACK)[:, :, PACK - 1], page[LAST][:, pieces[j]])
 
         def quantise_piece(j):
             cols = pieces[j]
-            quantise_page(1, cols, woven1[j])
+            quantise_page(1, cols, woven_part(cols))
             if cols.stop % BANK == 0:
                 store_words(1, slice(cols.stop - BANK, cols.stop))
 
-        for k in range(len(D_BANKS)):
-            d_pass(k, 0)
-        for k in range(len(F_BANKS)):
-            f_pass(k, 0)
+        sums = [(d_pass, k) for k in range(D_LEAD)]
+        for k in range(len(units)):
+            sums.append((f_pass, k))
+            if k + D_LEAD < len(units):
+                sums.append((d_pass, k + D_LEAD))
+        for one_pass, k in sums[: len(BANKS)]:
+            one_pass(k, 0)
         fill(0, nc.vector.tensor_copy)
         fill(1, nc.vector.tensor_copy)
-        fill(2, nc.scalar.copy)
+        fill(4, nc.scalar.copy)
         quantise_piece(0)
-        fill(3, nc.vector.tensor_copy)
         quantise_piece(1)
+        fill(2, nc.vector.tensor_copy)
+        fill(3, nc.vector.tensor_copy)
         quantise_piece(2)
-        fill(4, nc.vector.tensor_copy)
         quantise_piece(3)
         quantise_piece(4)
         store_scales(1)
         waiting = []
-        for k in range(len(units)):
-            if k >= len(D_BANKS):
-                d_pass(k, 0)
-            d_pass(k, 1)
-            if k >= len(F_BANKS):
-                f_pass(k, 0)
-            f_pass(k, 1)
+        for place, (one_pass, k) in enumerate(sums):
+            if place >= len(BANKS):
+                one_pass(k, 0)
+            one_pass(k, 1)
+            if one_pass != f_pass:
+                continue
             following = damp(k)
             for earlier, part, root in waiting:
                 store_unit(earlier, part, root)

@@ -218,7 +218,9 @@ def tile_list_chart_tile_planes_kernel(
             for q in range(QUADRANTS):
                 nc.sync.dma_start(out_3[g, 4 * q : 4 * q + 4, :].bitcast(I32), p_s[g][32 * q : 32 * q + 4, :].bitcast(I32))
 
-        front = round_w1(0, 0, 2, head_at + 7 * KIB // 4)
+        front = at(head_at + 7 * KIB // 4, [P, 2, P, PACK], BF16, "w1_front")
+        front_view = front[:].rearrange("p t m j -> p m j t")
+        nc.scalar.copy(front_view[:, : P // 2], dealt_w1(0)[:, : P // 2, :, 0:2])
         back = round_w1(0, 2, PACK, head_at + 11 * KIB // 2)
         v_w = [held([P, BANK], U32, "v_w0")]
         nc.vector.tensor_copy(v_w[0][:], tab_w[:].indirect(idx[:, : BANK // 16]))
@@ -238,6 +240,7 @@ def tile_list_chart_tile_planes_kernel(
         deal_w2(0, w2_dw[0], w2_ds[0])
         v_w.append(at(words_at, [P, BANK], U32, "v_w1"))
         nc.vector.tensor_copy(v_w[1][:], tab_w[:].indirect(idx[:, BANK // 16 :]))
+        nc.vector.tensor_copy(front_view[:, P // 2 :], dealt_w1(0)[:, P // 2 :, :, 0:2])
         quantise_w1(0, 0, 2, front, tab_at)
         w2_dw.append(at(head_at + 5 * KIB // 2, [P, 2 * PASS], U8, "w2_dw1"))
         w2_ds.append(at(head_at + 2 * KIB, [P, PASS], U8, "w2_ds1"))

@@ -66,7 +66,7 @@ def tile_list_chart_tile_planes_kernel(
         w1_late_scales_at = woven0_at - KIB // 2
         h_places = [
             woven0_at - 2 * KIB, w1_late_scales_at - 4 * KIB, woven0_at, woven0_at + 4 * KIB,
-            h_at, h_at + 4 * KIB, late_at, woven0_at,
+            h_at, h_at + 4 * KIB, late_at + 2 * KIB,
         ]
 
         idx = held([P, S // 16], U16, "idx")
@@ -281,15 +281,24 @@ def tile_list_chart_tile_planes_kernel(
         woven0 = [weave(cols, woven0_at + 8 * cols.start, f"woven0_{cols.start}") for cols in page_halves]
         for i in range(PACK, LAST):
             scatter_and_round(i)
-        w3_s = at(late_at, [P, GROUPS * N], U8, "w3_s")
-        p_s[0] = at(late_at + KIB, [P, T2], U8, "p_s0")
+        w3_s = at(late_at + 3 * KIB, [P, GROUPS * N], U8, "w3_s")
         for cols in (slice(0, BANK), slice(BANK, GROUPS * N)):
             nc.vector.quantize_mx(w3_c[:, cols].bitcast(FP8X4), w3_s[:, cols], w3_rounded[:, cols, :].rearrange("p n j -> p (n j)"))
-        quantise_page(0, page_halves[0], woven0[0][:])
-        store_words(0, page_halves[0])
-        larger(LAST, last_products)
-        quantise_page(0, page_halves[1], woven0[1][:])
-        store_words(0, page_halves[1])
+        last_h = [at(late_at + KIB // 4 + u * 11 * KIB // 2, [P, BANK], F32, f"h{LAST}_{u}") for u in range(HALVES)]
+        for u in range(HALVES):
+            nc.vector.tensor_tensor(last_h[u][:], last_products[u][:], in_sbuf[LAST][u][:], ALU.max)
+
+        def scatter_half(u):
+            nc.vector.tensor_tensor(
+                page[LAST][:].indirect(idx2[:, u * BANK // 16 : (u + 1) * BANK // 16]), last_h[u][:],
+                gain[PACK - 1][:, u * BANK : (u + 1) * BANK], ALU.mult,
+            )
+
+        scatter_half(0)
+        p_s[0] = at(late_at + KIB // 4, [P, T2], U8, "p_s0")
+        for x in (1, 0):
+            quantise_page(0, page_halves[x], woven0[x][:])
+            store_words(0, page_halves[x])
         store_scales(0)
 
         def halved(cols):
@@ -306,7 +315,8 @@ def tile_list_chart_tile_planes_kernel(
             j = [span.start <= cols.start < span.stop for span in spans].index(True)
             return woven1[j][:, PACK * (cols.start - spans[j].start) : PACK * (cols.stop - spans[j].start)]
 
-        scatter(LAST)
+        scatter_half(1)
+        nc.sync.dma_start(out_rows[GROUPS - 1, PACK - 1], page[LAST][:])
         staged = [at(raw_at + n * 8 * KIB, [P, T2], F32, f"staged{n}") for n in range(NT)]
         d_of = {}
         f_of = {}

@@ -1,6 +1,7 @@
 from contextlib import ExitStack
 
 import concourse.mybir as mybir
+from concourse.masks import make_identity
 
 K, T, S, T2, H, N = 512, 2048, 1024, 2048, 1024, 384
 FLOPS = 2 * (2 * K * H * S + 2 * H * N * T2)
@@ -29,7 +30,8 @@ NT = N // P
 KIB = 1024
 QUADRANTS = 4
 
-W1_BANKS = (4, 5, 6, 7)
+W1_BANKS = (4, 5)
+TURN_BANKS = (6, 7)
 W2_BANKS = (2, 3, 0, 1)
 BANKS = (4, 5, 6, 7, 2, 3, 0, 1)
 D_LEAD = 3
@@ -55,32 +57,40 @@ def tile_list_chart_tile_planes_kernel(
 
         half = T2 // 2
         tab_at = 0
-        words_at = tab_at + 8 * KIB
-        head_at = words_at + 2 * KIB
+        head_at = tab_at + 8 * KIB
         h_at = head_at + 15 * KIB // 2
         woven0_at = h_at + 8 * KIB
         woven1_at = woven0_at + 16 * KIB
         raw_at = woven1_at + 16 * KIB
         copies_at = raw_at + 32 * KIB
         late_at = copies_at + 16 * KIB
-        w1_late_scales_at = woven0_at - KIB // 2
+        h1_at = h_at + 4 * KIB
+        w1_back_scales_at = h1_at + 9 * KIB // 2
+        w1_late_scales_at = w1_back_scales_at + KIB // 4
         h_places = [
-            woven0_at - 2 * KIB, w1_late_scales_at - 4 * KIB, woven0_at, woven0_at + 4 * KIB,
-            h_at, h_at + 4 * KIB, late_at + 2 * KIB,
+            h1_at + 15 * KIB // 4, h1_at, h1_at - 15 * KIB // 4, h1_at + KIB // 4,
+            tab_at + 4 * KIB, tab_at, late_at + 2 * KIB,
         ]
 
         idx = held([P, S // 16], U16, "idx")
         idx2 = held([P, S // 16], U16, "idx2")
         tab_w = at(tab_at, [P, T], U32, "tab_w")
         tab_s = held([P, T], U8, "tab_s")
-        w2_w = [at(words_at, [P, 2 * PASS], U8, "w2_w0"), held([P, 2 * PASS], U8, "w2_w1")]
+        w2_w = [held([P, 2 * PASS], U8, f"w2_w{g}") for g in range(GROUPS)]
         w2_s = held([P, H], U8, "w2_s")
         w4_w = held([P, GROUPS, N], U32, "w4_w")
         w4_s = held([P, GROUPS, N], U8, "w4_s")
         gain = [held([P, S], F32, f"gain{t}") for t in range(PACK)]
+        plain_gain = held([P, S], F32, "plain_gain")
+        identity = held([P, P], F32, "identity")
+        make_identity(nc, identity[:])
         page = [held([P, T2], F32, f"page{i}") for i in range(TILES)]
-        page_rows = page0.rearrange("(g p t) m -> g t p m", g=GROUPS, t=PACK)
-        out_rows = out_1.rearrange("(g p t) m -> g t p m", g=GROUPS, t=PACK)
+
+        def tile_rows(matrix, i):
+            if i < PACK:
+                return matrix[i * P : (i + 1) * P, :]
+            return matrix[PASS:, :].rearrange("(p t) m -> t p m", t=PACK)[i - PACK]
+
         wgs_rows = wgs.rearrange("(q t) j -> q t j", t=PACK)
 
         warm = held([P, 1], F32, "warm")
@@ -89,13 +99,14 @@ def tile_list_chart_tile_planes_kernel(
         nc.vector.memset(w2_s[:].bitcast(I32), 0)
         nc.vector.memset(warm[:], 1.0)
         nc.vector.memset(w4_s[:].rearrange("p a n -> p (a n)").bitcast(I32), 0)
-        w1_raw = [at(raw_at + g * 8 * KIB, [P, PACK, PASS], F32, f"w1_raw{g}") for g in range(GROUPS)]
+        w1_front, w1_back = [at(raw_at + x * 4 * KIB, [P, PACK, 2 * P], F32, f"w1_raw0_{x}") for x in range(2)]
+        w1_late = at(woven1_at, [P, PACK, PASS], F32, "w1_raw1")
         w3_raw = [at(raw_at + (20 + 6 * g) * KIB, [P, PACK, N], F32, f"w3_raw{g}") for g in range(GROUPS)]
-        w1_cols = w1.rearrange("(p j) (g c) -> g p j c", j=PACK, g=GROUPS)
+        w1_rows = w1.rearrange("(p j) c -> p j c", j=PACK)
         w3_rows = w3.rearrange("(g p j) n -> g p j n", g=GROUPS, j=PACK)
 
         def load_page(i):
-            nc.sync.dma_start(page[i][:], page_rows[i // PACK, i % PACK])
+            nc.sync.dma_start(page[i][:], tile_rows(page0, i))
 
         def load_gain(t):
             for q in (0, 2, 1, 3):
@@ -109,20 +120,20 @@ def tile_list_chart_tile_planes_kernel(
         for q in range(QUADRANTS):
             nc.sync.dma_start(w2_s[32 * q : 32 * q + 4, :].bitcast(I32), w2_scales[0, 4 * q : 4 * q + 4, :].bitcast(I32))
         nc.sync.dma_start(w2_w[0][:].bitcast(I32), w2_words[0, :, : 2 * PASS].bitcast(I32))
-        nc.sync.dma_start(w1_raw[0][:], w1_cols[0])
+        nc.sync.dma_start(w1_front[:], w1_rows[:, :, : 2 * P])
         nc.sync.dma_start(w2_w[1][:].bitcast(I32), w2_words[0, :, 2 * PASS :].bitcast(I32))
         nc.scalar.activation(warm_out[:], warm[:], ACT.Abs_reciprocal_sqrt)
         load_page(0)
-        load_gain(0)
-        nc.sync.dma_start(w1_raw[1][:], w1_cols[1])
-        for t in (1, 2):
-            load_gain(t)
-            load_page(t)
+        nc.sync.dma_start(plain_gain[:], wgs)
+        nc.sync.dma_start(w1_back[:], w1_rows[:, :, 2 * P : PASS])
+        nc.sync.dma_start(w1_late[:], w1_rows[:, :, PASS:])
+        for i in range(1, PACK):
+            load_page(i)
         for g in range(GROUPS):
             nc.sync.dma_start(w3_raw[g][:], w3_rows[g])
-        load_gain(PACK - 1)
-        for i in range(PACK - 1, TILES):
-            load_page(i)
+        for t in range(PACK):
+            load_gain(t)
+            load_page(PACK + t)
         nc.sync.dma_start(w4_w[:].bitcast(I32), w4_words.rearrange("a p n t -> p a (n t)").bitcast(I32))
         for q in range(QUADRANTS):
             nc.sync.dma_start(
@@ -135,17 +146,12 @@ def tile_list_chart_tile_planes_kernel(
         nc.vector.tensor_copy(v_s[:], tab_s[:].indirect(idx[:]))
         w1_s = {}
 
-        def dealt_w1(g):
-            return w1_raw[g][:].rearrange("p j (m t) -> p m j t", t=PACK)
-
-        def round_w1(g, lo, hi, offset):
-            rounded = at(offset, [P, hi - lo, P, PACK], BF16, f"w1_rounded{g}_{lo}")
-            nc.scalar.copy(rounded[:].rearrange("p t m j -> p m j t"), dealt_w1(g)[:, :, :, lo:hi])
-            return rounded
+        def round_plain(rounded, raw):
+            nc.scalar.copy(rounded.rearrange("p (c i) j -> p c j i", i=4), raw.rearrange("p j (c i) -> p c j i", i=4))
 
         def quantise_w1(g, lo, hi, rounded, offset):
             scales = at(offset, [P, (hi - lo) * P], U8, f"w1_s{g}_{lo}")
-            nc.vector.quantize_mx(w1_c[g][:, lo * P : hi * P].bitcast(FP8X4), scales[:], rounded[:].rearrange("p t m j -> p (t m j)"))
+            nc.vector.quantize_mx(w1_c[g][:, lo * P : hi * P].bitcast(FP8X4), scales[:], rounded[:].rearrange("p c j -> p (c j)"))
             for t in range(lo, hi):
                 w1_s[PACK * g + t] = scales[:, (t - lo) * P : (t - lo + 1) * P]
 
@@ -164,8 +170,8 @@ def tile_list_chart_tile_planes_kernel(
             for u in range(HALVES):
                 products.append(psum.tile([P, BANK], F32, name="w2_product", tag=f"bank{W2_BANKS[2 * (i % 2) + u]}"))
                 nc.tensor.matmul_mx(
-                    products[u][:], lhsT=w2_dw[g][:, 2 * t * P : 2 * (t + 1) * P].bitcast(FP4X4),
-                    lhsT_scale=w2_ds[g][:, t * P : (t + 1) * P],
+                    products[u][:], lhsT=w2_used[g][:, 2 * t * P : 2 * (t + 1) * P].bitcast(FP4X4),
+                    lhsT_scale=w2_scales_used[g][:, t * P : (t + 1) * P],
                     rhs=v_w[u][:].bitcast(FP8X4), rhs_scale=v_s[:, u * BANK : (u + 1) * BANK], start=True, stop=True,
                 )
             return products
@@ -178,11 +184,9 @@ def tile_list_chart_tile_planes_kernel(
             for u in range(HALVES):
                 product = w1_product(i, u, banks[u])
                 buffer = (HALVES * i + u) % COPY_BUFFERS
-                in_sbuf[i].append(at(copies_at + 2 * KIB * buffer, [P, BANK], F32, f"w1_copy{i}_{u}"))
+                place = woven1_at if (i, u) == (2, 0) else copies_at + 2 * KIB * buffer
+                in_sbuf[i].append(at(place, [P, BANK], F32, f"w1_copy{i}_{u}"))
                 nc.scalar.copy(in_sbuf[i][u][:], product[:])
-
-        def w1_banks(i):
-            return W1_BANKS[2 * (i % 2) : 2 * (i % 2) + 2]
 
         def larger(i, in_psum):
             h[i] = at(h_places[i], [P, S], F32, f"h{i}")
@@ -190,8 +194,31 @@ def tile_list_chart_tile_planes_kernel(
                 nc.vector.tensor_tensor(h[i][:, u * BANK : (u + 1) * BANK], in_psum[u][:], in_sbuf[i][u][:], ALU.max)
 
         def scatter(i):
-            nc.vector.tensor_tensor(page[i][:].indirect(idx2[:]), h[i][:], gain[i % PACK][:], ALU.mult)
-            nc.sync.dma_start(out_rows[i // PACK, i % PACK], page[i][:])
+            factor = plain_gain if i < PACK else gain[i - PACK]
+            nc.vector.tensor_tensor(page[i][:].indirect(idx2[:]), h[i][:], factor[:], ALU.mult)
+            nc.sync.dma_start(tile_rows(out_1, i), page[i][:])
+
+        def turn(i, banks):
+            for q in range(CHUNKS):
+                bank = psum.tile([P, PACK, P], F32, name="turned", tag=f"bank{banks[q % len(banks)]}")
+                for c in range(PACK):
+                    lo = q * BANK + c * P
+                    nc.tensor.transpose(bank[:, c, :], page[i][:, lo : lo + P], identity[:])
+                nc.scalar.copy(turned[:, PACK * q : PACK * (q + 1), i * P : (i + 1) * P], bank[:])
+
+        def turn_back(x):
+            woven = at(woven0_at + 8 * KIB * x, [P, half * PACK], BF16, f"woven0_{x}")
+            words = turned[:].rearrange("p c r -> p (c r)").bitcast(F32).rearrange("p (c w u) -> p c u w", u=2, w=P)
+            for q in range(half // (2 * P)):
+                bank = psum.tile([P, 2, 2, P], F32, name="turned_back", tag=f"bank{(W1_BANKS + TURN_BANKS)[q]}")
+                for c in range(2):
+                    for u in range(2):
+                        nc.tensor.transpose(bank[:, c, u, :], words[:, 8 * x + 2 * q + c, u, :], identity[:])
+                nc.scalar.copy(
+                    woven[:].bitcast(F32)[:, q * BANK : (q + 1) * BANK].rearrange("p (c m u) -> p c m u", c=2, u=2),
+                    bank[:].rearrange("p c u m -> p c m u"),
+                )
+            return woven
 
         def scatter_and_round(i):
             scatter(i)
@@ -218,67 +245,66 @@ def tile_list_chart_tile_planes_kernel(
             for q in range(QUADRANTS):
                 nc.sync.dma_start(out_3[g, 4 * q : 4 * q + 4, :].bitcast(I32), p_s[g][32 * q : 32 * q + 4, :].bitcast(I32))
 
-        front = at(head_at + 7 * KIB // 4, [P, 2, P, PACK], BF16, "w1_front")
-        front_view = front[:].rearrange("p t m j -> p m j t")
-        nc.scalar.copy(front_view[:, : P // 2], dealt_w1(0)[:, : P // 2, :, 0:2])
-        back = round_w1(0, 2, PACK, head_at + 11 * KIB // 2)
-        v_w = [held([P, BANK], U32, "v_w0")]
-        nc.vector.tensor_copy(v_w[0][:], tab_w[:].indirect(idx[:, : BANK // 16]))
-
-        def deal_w2(g, words, scales):
-            nc.vector.tensor_copy(
-                scales[:].rearrange("p (t m) -> p t m", t=PACK),
-                w2_s[:, g * PASS : (g + 1) * PASS].rearrange("p (m t) -> p t m", t=PACK),
-            )
-            nc.vector.tensor_copy(
-                words[:].bitcast(U16).rearrange("p (t m) -> p t m", t=PACK),
-                w2_w[g][:].bitcast(U16).rearrange("p (m t) -> p t m", t=PACK),
-            )
-
-        w2_dw = [held([P, 2 * PASS], U8, "w2_dw0")]
-        w2_ds = [held([P, PASS], U8, "w2_ds0")]
-        deal_w2(0, w2_dw[0], w2_ds[0])
-        v_w.append(at(words_at, [P, BANK], U32, "v_w1"))
-        nc.vector.tensor_copy(v_w[1][:], tab_w[:].indirect(idx[:, BANK // 16 :]))
-        nc.vector.tensor_copy(front_view[:, P // 2 :], dealt_w1(0)[:, P // 2 :, :, 0:2])
+        front = at(head_at + 7 * KIB // 4, [P, 2 * P, PACK], BF16, "w1_rounded0")
+        round_plain(front[:], w1_front[:])
+        v_w = [held([P, BANK], U32, f"v_w{u}") for u in range(HALVES)]
+        for u in range(HALVES):
+            nc.vector.tensor_copy(v_w[u][:], tab_w[:].indirect(idx[:, u * BANK // 16 : (u + 1) * BANK // 16]))
         quantise_w1(0, 0, 2, front, tab_at)
-        w2_dw.append(at(head_at + 5 * KIB // 2, [P, 2 * PASS], U8, "w2_dw1"))
-        w2_ds.append(at(head_at + 2 * KIB, [P, PASS], U8, "w2_ds1"))
-        deal_w2(1, w2_dw[1], w2_ds[1])
+        w2_dw = at(head_at + 5 * KIB // 2, [P, 2 * PASS], U8, "w2_dw")
+        w2_ds = at(head_at + 2 * KIB, [P, PASS], U8, "w2_ds")
+        nc.vector.tensor_copy(w2_ds[:].rearrange("p (t m) -> p t m", t=PACK), w2_s[:, PASS:].rearrange("p (m t) -> p t m", t=PACK))
+        nc.vector.tensor_copy(
+            w2_dw[:].bitcast(U16).rearrange("p (t m) -> p t m", t=PACK),
+            w2_w[1][:].bitcast(U16).rearrange("p (m t) -> p t m", t=PACK),
+        )
+        w2_used = [w2_w[0], w2_dw]
+        w2_scales_used = [w2_s, w2_ds]
         early = w2_products(0)
         late = [w1_product(0, u, W2_BANKS[2 + u]) for u in range(HALVES)]
-        quantise_w1(0, 2, PACK, back, tab_at + KIB)
         in_sbuf[0] = []
         for u in range(HALVES):
             in_sbuf[0].append(at(head_at + 7 * KIB // 2 * u, [P, BANK], F32, f"w2_copy{u}"))
             nc.scalar.copy(in_sbuf[0][u][:], early[u][:])
         larger(0, late)
         copied_w1_products(1, W2_BANKS[0:2])
-        for i in range(2, PACK):
-            copied_w1_products(i, w1_banks(i))
-        rounded1 = round_w1(1, 0, PACK, head_at + 7 * KIB // 2)
-        pairs = at(raw_at + 4 * KIB, [P, 2, T2, 2], BF16, "pairs")
+        back = at(head_at, [P, 2 * P, PACK], BF16, "w1_rounded1")
+        round_plain(back[:], w1_back[:])
+        rounded1 = at(head_at + 7 * KIB // 2, [P, PASS, PACK], BF16, "w1_rounded2")
+        nc.scalar.copy(
+            rounded1[:].rearrange("p (t m) j -> p m j t", t=PACK), w1_late[:].rearrange("p j (m t) -> p m j t", t=PACK)
+        )
 
-        scatter_and_round(0)
-        for i in range(1, PACK):
-            larger(i, w2_products(i))
+        scatter(0)
+        larger(1, w2_products(1))
+        quantise_w1(0, 2, PACK, back, w1_back_scales_at)
         quantise_w1(1, 0, PACK, rounded1, w1_late_scales_at)
-        for i in range(PACK, TILES):
-            copied_w1_products(i, w1_banks(i))
-        scatter_and_round(1)
+        copied_w1_products(2, W1_BANKS)
+        copied_w1_products(3, TURN_BANKS)
+        for i in (4, 5):
+            copied_w1_products(i, W1_BANKS)
+        turned = at(raw_at + 4 * KIB, [P, T2 // P, PASS], BF16, "turned")
+        turn(0, TURN_BANKS)
+        scatter(1)
+        for i in range(2, PACK):
+            larger(i, w2_products(i))
+        for i in (6, 7):
+            copied_w1_products(i, W1_BANKS)
         for i in range(PACK, LAST):
             larger(i, w2_products(i))
         last_products = w2_products(LAST)
-        scatter_and_round(2)
-        w3_rounded = at(woven1_at + 8 * KIB, [P, GROUPS * N, PACK], BF16, "w3_rounded")
+        turn(1, TURN_BANKS)
+        scatter(2)
+        turn(2, TURN_BANKS + W1_BANKS)
+        w3_rounded = at(head_at, [P, GROUPS * N, PACK], BF16, "w3_rounded")
         for g in range(GROUPS):
-            nc.scalar.copy(
-                w3_rounded[:, g * N : (g + 1) * N, :].rearrange("p (c i) j -> p c j i", i=4),
-                w3_raw[g][:].rearrange("p j (c i) -> p c j i", i=4),
-            )
-        scatter_and_round(3)
+            round_plain(w3_rounded[:, g * N : (g + 1) * N, :], w3_raw[g][:])
+        scatter(3)
+        turn(3, TURN_BANKS + W1_BANKS)
         page_halves = [slice(x * half, (x + 1) * half) for x in range(2)]
-        woven0 = [weave(cols, woven0_at + 8 * cols.start, f"woven0_{cols.start}") for cols in page_halves]
+        woven0 = [turn_back(x) for x in range(2)]
+        pairs = at(raw_at + 4 * KIB, [P, 2, T2, 2], BF16, "pairs")
+        nc.gpsimd.memset(pairs[:, 1, :, :].rearrange("p m b -> p (m b)").bitcast(I32), 0)
         for i in range(PACK, LAST):
             scatter_and_round(i)
         w3_s = at(late_at + 3 * KIB, [P, GROUPS * N], U8, "w3_s")
@@ -316,7 +342,7 @@ def tile_list_chart_tile_planes_kernel(
             return woven1[j][:, PACK * (cols.start - spans[j].start) : PACK * (cols.stop - spans[j].start)]
 
         scatter_half(1)
-        nc.sync.dma_start(out_rows[GROUPS - 1, PACK - 1], page[LAST][:])
+        nc.sync.dma_start(tile_rows(out_1, LAST), page[LAST][:])
         staged = [at(raw_at + n * 8 * KIB, [P, T2], F32, f"staged{n}") for n in range(NT)]
         d_of = {}
         f_of = {}

@@ -69,7 +69,7 @@ def tile_list_chart_tile_planes_kernel(
         w1_late_scales_at = w1_back_scales_at + KIB // 4
         h_places = [
             h1_at + 15 * KIB // 4, h1_at, h1_at - 15 * KIB // 4, h1_at + KIB // 4,
-            tab_at + 4 * KIB, tab_at, late_at + 2 * KIB,
+            tab_at + 4 * KIB, tab_at, late_at,
         ]
 
         idx = held([P, S // 16], U16, "idx")
@@ -293,6 +293,9 @@ def tile_list_chart_tile_planes_kernel(
         for i in range(PACK, LAST):
             larger(i, w2_products(i))
         last_products = w2_products(LAST)
+        last_h = [at(late_at + (4 + 2 * u) * KIB, [P, BANK], F32, f"h{LAST}_{u}") for u in range(HALVES)]
+        for u in range(HALVES):
+            nc.vector.tensor_tensor(last_h[u][:], last_products[u][:], in_sbuf[LAST][u][:], ALU.max)
         turn(1, TURN_BANKS)
         scatter(2)
         turn(2, TURN_BANKS + W1_BANKS)
@@ -307,12 +310,6 @@ def tile_list_chart_tile_planes_kernel(
         nc.gpsimd.memset(pairs[:, 1, :, :].rearrange("p m b -> p (m b)").bitcast(I32), 0)
         for i in range(PACK, LAST):
             scatter_and_round(i)
-        w3_s = at(late_at + 3 * KIB, [P, GROUPS * N], U8, "w3_s")
-        for cols in (slice(0, BANK), slice(BANK, GROUPS * N)):
-            nc.vector.quantize_mx(w3_c[:, cols].bitcast(FP8X4), w3_s[:, cols], w3_rounded[:, cols, :].rearrange("p n j -> p (n j)"))
-        last_h = [at(late_at + KIB // 4 + u * 11 * KIB // 2, [P, BANK], F32, f"h{LAST}_{u}") for u in range(HALVES)]
-        for u in range(HALVES):
-            nc.vector.tensor_tensor(last_h[u][:], last_products[u][:], in_sbuf[LAST][u][:], ALU.max)
 
         def scatter_half(u):
             nc.vector.tensor_tensor(
@@ -321,8 +318,11 @@ def tile_list_chart_tile_planes_kernel(
             )
 
         scatter_half(0)
-        p_s[0] = at(late_at + KIB // 4, [P, T2], U8, "p_s0")
-        for x in (1, 0):
+        w3_s = at(late_at + 5 * KIB, [P, GROUPS * N], U8, "w3_s")
+        for cols in (slice(0, BANK), slice(BANK, GROUPS * N)):
+            nc.vector.quantize_mx(w3_c[:, cols].bitcast(FP8X4), w3_s[:, cols], w3_rounded[:, cols, :].rearrange("p n j -> p (n j)"))
+        p_s[0] = at(late_at + 5 * KIB // 2, [P, T2], U8, "p_s0")
+        for x in range(2):
             quantise_page(0, page_halves[x], woven0[x][:])
             store_words(0, page_halves[x])
         store_scales(0)
@@ -335,7 +335,8 @@ def tile_list_chart_tile_planes_kernel(
         units = [(cols, n) for cols in chunks for n in range(NT)][:-1] + [(cols, NT - 1) for cols in halved(chunks[-1])]
         pieces = halved(chunks[0]) + chunks[1:]
         spans = [chunks[0], chunks[-1], slice(BANK, 3 * BANK)]
-        woven1 = [weave(cols, woven1_at + 8 * cols.start, f"woven1_{cols.start}") for cols in spans]
+        places = [woven1_at, woven1_at + 4 * KIB, woven0_at + 8 * KIB]
+        woven1 = [weave(cols, place, f"woven1_{cols.start}") for cols, place in zip(spans, places)]
 
         def woven_part(cols):
             j = [span.start <= cols.start < span.stop for span in spans].index(True)

@@ -36,7 +36,7 @@ W2_BANKS = (2, 3, 0, 1)
 BANKS = (4, 5, 6, 7, 2, 3, 0, 1)
 D_LEAD = 3
 COPY_BUFFERS = 8
-ROOT_BUFFERS = 4
+ROOT_BUFFERS = 8
 
 
 def tile_list_chart_tile_planes_kernel(
@@ -99,7 +99,9 @@ def tile_list_chart_tile_planes_kernel(
         nc.vector.memset(w2_s[:].bitcast(I32), 0)
         nc.vector.memset(warm[:], 1.0)
         nc.vector.memset(w4_s[:].rearrange("p a n -> p (a n)").bitcast(I32), 0)
-        w1_front, w1_back = [at(raw_at + x * 4 * KIB, [P, PACK, 2 * P], F32, f"w1_raw0_{x}") for x in range(2)]
+        front_at = woven1_at + 8 * KIB
+        w1_front = at(front_at, [P, PACK, 2 * P], F32, "w1_front")
+        w1_back = at(raw_at, [P, PACK, 2 * P], F32, "w1_back")
         w1_late = at(woven1_at, [P, PACK, PASS], F32, "w1_raw1")
         w3_raw = [at(raw_at + (20 + 6 * g) * KIB, [P, PACK, N], F32, f"w3_raw{g}") for g in range(GROUPS)]
         w1_rows = w1.rearrange("(p j) c -> p j c", j=PACK)
@@ -264,13 +266,13 @@ def tile_list_chart_tile_planes_kernel(
         late = [w1_product(0, u, W2_BANKS[2 + u]) for u in range(HALVES)]
         in_sbuf[0] = []
         for u in range(HALVES):
-            in_sbuf[0].append(at(head_at + 7 * KIB // 2 * u, [P, BANK], F32, f"w2_copy{u}"))
+            in_sbuf[0].append(at(front_at + 2 * KIB * u, [P, BANK], F32, f"w2_copy{u}"))
             nc.scalar.copy(in_sbuf[0][u][:], early[u][:])
         larger(0, late)
         copied_w1_products(1, W2_BANKS[0:2])
-        back = at(head_at, [P, 2 * P, PACK], BF16, "w1_rounded1")
+        back = at(front_at, [P, 2 * P, PACK], BF16, "w1_rounded1")
         round_plain(back[:], w1_back[:])
-        rounded1 = at(head_at + 7 * KIB // 2, [P, PASS, PACK], BF16, "w1_rounded2")
+        rounded1 = at(front_at + 2 * KIB, [P, PASS, PACK], BF16, "w1_rounded2")
         nc.scalar.copy(
             rounded1[:].rearrange("p (t m) j -> p m j t", t=PACK), w1_late[:].rearrange("p j (m t) -> p m j t", t=PACK)
         )
@@ -322,7 +324,7 @@ def tile_list_chart_tile_planes_kernel(
         for cols in (slice(0, BANK), slice(BANK, GROUPS * N)):
             nc.vector.quantize_mx(w3_c[:, cols].bitcast(FP8X4), w3_s[:, cols], w3_rounded[:, cols, :].rearrange("p n j -> p (n j)"))
         p_s[0] = at(late_at + 5 * KIB // 2, [P, T2], U8, "p_s0")
-        for x in range(2):
+        for x in (1, 0):
             quantise_page(0, page_halves[x], woven0[x][:])
             store_words(0, page_halves[x])
         store_scales(0)
@@ -335,7 +337,7 @@ def tile_list_chart_tile_planes_kernel(
         units = [(cols, n) for cols in chunks for n in range(NT)][:-1] + [(cols, NT - 1) for cols in halved(chunks[-1])]
         pieces = halved(chunks[0]) + chunks[1:]
         spans = [chunks[0], chunks[-1], slice(BANK, 3 * BANK)]
-        places = [woven1_at, woven1_at + 4 * KIB, woven0_at + 8 * KIB]
+        places = [woven1_at, woven1_at + 4 * KIB, woven0_at]
         woven1 = [weave(cols, place, f"woven1_{cols.start}") for cols, place in zip(spans, places)]
 
         def woven_part(cols):
@@ -345,6 +347,7 @@ def tile_list_chart_tile_planes_kernel(
         scatter_half(1)
         nc.sync.dma_start(tile_rows(out_1, LAST), page[LAST][:])
         staged = [at(raw_at + n * 8 * KIB, [P, T2], F32, f"staged{n}") for n in range(NT)]
+        root_places = [region + 2 * KIB * j for region in (tab_at, h_at) for j in range(ROOT_BUFFERS // 2)]
         d_of = {}
         f_of = {}
 
@@ -376,7 +379,7 @@ def tile_list_chart_tile_planes_kernel(
             cols, n = units[k]
             width = cols.stop - cols.start
             scratch = at(copies_at + 2 * KIB * (k % COPY_BUFFERS), [P, width], F32, f"scratch{k}")
-            root = at(tab_at + 2 * KIB * (k % ROOT_BUFFERS), [P, width], F32, f"root{k}")
+            root = at(root_places[k % ROOT_BUFFERS], [P, width], F32, f"root{k}")
             nc.scalar.activation(scratch[:], d_of[k][:], ACT.Square)
             nc.scalar.activation(root[:], scratch[:], ACT.Abs_reciprocal_sqrt, bias=1.0)
             if k >= len(units) - 3:
@@ -386,8 +389,8 @@ def tile_list_chart_tile_planes_kernel(
             nc.vector.tensor_tensor(scratch[:], f_of[k][:], root[:], ALU.mult)
             return [(k, scratch, root)]
 
-        def fill(j, copy):
-            copy(woven_part(pieces[j]).rearrange("p (m t) -> p m t", t=PACK)[:, :, PACK - 1], page[LAST][:, pieces[j]])
+        def fill(cols, copy):
+            copy(woven_part(cols).rearrange("p (m t) -> p m t", t=PACK)[:, :, PACK - 1], page[LAST][:, cols])
 
         def quantise_piece(j):
             cols = pieces[j]
@@ -402,13 +405,15 @@ def tile_list_chart_tile_planes_kernel(
                 sums.append((d_pass, k + D_LEAD))
         for one_pass, k in sums[: len(BANKS)]:
             one_pass(k, 0)
-        fill(0, nc.vector.tensor_copy)
-        fill(1, nc.vector.tensor_copy)
-        fill(4, nc.scalar.copy)
+        shared = 3 * BANK - P
+        fill(pieces[0], nc.vector.tensor_copy)
+        fill(pieces[1], nc.vector.tensor_copy)
+        fill(pieces[4], nc.scalar.copy)
+        fill(slice(shared, 3 * BANK), nc.scalar.copy)
         quantise_piece(0)
         quantise_piece(1)
-        fill(2, nc.vector.tensor_copy)
-        fill(3, nc.vector.tensor_copy)
+        fill(pieces[2], nc.vector.tensor_copy)
+        fill(slice(2 * BANK, shared), nc.vector.tensor_copy)
         quantise_piece(2)
         quantise_piece(3)
         quantise_piece(4)

@@ -59,7 +59,7 @@ def tile_list_chart_tile_planes_kernel(
         tab_at = 0
         head_at = tab_at + 8 * KIB
         h_at = head_at + 15 * KIB // 2
-        woven0_at = h_at + 8 * KIB
+        woven0_at = h_at + 33 * KIB // 4
         woven1_at = woven0_at + 16 * KIB
         raw_at = woven1_at + 16 * KIB
         copies_at = raw_at + 32 * KIB
@@ -180,6 +180,7 @@ def tile_list_chart_tile_planes_kernel(
 
         in_sbuf = {}
         h = {}
+        scaled = {}
 
         def copied_w1_products(i, banks):
             in_sbuf[i] = []
@@ -195,9 +196,14 @@ def tile_list_chart_tile_planes_kernel(
             for u in range(HALVES):
                 nc.vector.tensor_tensor(h[i][:, u * BANK : (u + 1) * BANK], in_psum[u][:], in_sbuf[i][u][:], ALU.max)
 
+        def factor(i):
+            return plain_gain if i < PACK else gain[i - PACK]
+
         def scatter(i):
-            factor = plain_gain if i < PACK else gain[i - PACK]
-            nc.vector.tensor_tensor(page[i][:].indirect(idx2[:]), h[i][:], factor[:], ALU.mult)
+            if i in scaled:
+                nc.vector.tensor_copy(page[i][:].indirect(idx2[:]), scaled[i][:])
+            else:
+                nc.vector.tensor_tensor(page[i][:].indirect(idx2[:]), h[i][:], factor(i)[:], ALU.mult)
             nc.sync.dma_start(tile_rows(out_1, i), page[i][:])
 
         def turn(i, banks):
@@ -225,7 +231,10 @@ def tile_list_chart_tile_planes_kernel(
         def scatter_and_round(i):
             scatter(i)
             t = i % PACK
-            nc.scalar.copy(pairs[:, t // 2, :, t % 2], page[i][:])
+            if i == LAST - 1:
+                nc.scalar.copy(pairs[:, 1, :, :], page[i][:].unsqueeze(2).to_broadcast([P, T2, 2]))
+            else:
+                nc.scalar.copy(pairs[:, 0, :, t], page[i][:])
 
         def weave(cols, offset, name):
             woven = at(offset, [P, (cols.stop - cols.start) * PACK], BF16, name)
@@ -290,16 +299,36 @@ def tile_list_chart_tile_planes_kernel(
         scatter(1)
         for i in range(2, PACK):
             larger(i, w2_products(i))
-        for i in (6, 7):
-            copied_w1_products(i, W1_BANKS)
+        copied_w1_products(6, W1_BANKS)
         for i in range(PACK, LAST):
             larger(i, w2_products(i))
+        first_last = at(copies_at + 12 * KIB, [P, S], F32, "w1_copy_last")
+        second_last = at(front_at, [P, S], F32, "w2_copy_last")
         last_products = w2_products(LAST)
-        last_h = [at(late_at + (4 + 2 * u) * KIB, [P, BANK], F32, f"h{LAST}_{u}") for u in range(HALVES)]
         for u in range(HALVES):
-            nc.vector.tensor_tensor(last_h[u][:], last_products[u][:], in_sbuf[LAST][u][:], ALU.max)
+            cols = slice(u * BANK, (u + 1) * BANK)
+            nc.scalar.copy(first_last[:, cols], w1_product(LAST, u, W1_BANKS[u])[:])
+            nc.scalar.copy(second_last[:, cols], last_products[u][:])
         turn(1, TURN_BANKS)
         scatter(2)
+        scaled[3] = at(h_places[2], [P, S], F32, "scaled3")
+        nc.gpsimd.tensor_tensor(scaled[3][:], h[3][:], factor(3)[:], ALU.mult)
+        for i in range(PACK, LAST):
+            scaled[i] = h[i] if i < LAST - 1 else at(h_places[3], [P, S], F32, "scaled6")
+            nc.gpsimd.tensor_tensor(scaled[i][:], h[i][:], factor(i)[:], ALU.mult)
+        take_second = at(h_places[LAST - 1], [P, S], F32, "take_second")
+        take_first = at(front_at + 4 * KIB, [P, S], F32, "take_first")
+        nc.gpsimd.tensor_tensor(take_second[:], second_last[:], first_last[:], ALU.subtract)
+        nc.gpsimd.tensor_scalar(take_second[:], take_second[:], 1.0, 0.0, ALU.min, ALU.max)
+        nc.gpsimd.tensor_scalar(take_second[:], take_second[:], 2.0**63, 2.0**63, ALU.mult, ALU.mult)
+        nc.gpsimd.tensor_scalar(take_second[:], take_second[:], 1.0, 0.0, ALU.min, ALU.max)
+        nc.gpsimd.tensor_scalar(take_first[:], take_second[:], -1.0, 1.0, ALU.mult, ALU.add)
+        nc.gpsimd.tensor_tensor(second_last[:], second_last[:], take_second[:], ALU.mult)
+        nc.gpsimd.tensor_tensor(first_last[:], first_last[:], take_first[:], ALU.mult)
+        last_h = [at(late_at + (4 + 2 * u) * KIB, [P, BANK], F32, f"h{LAST}_{u}") for u in range(HALVES)]
+        for u in range(HALVES):
+            cols = slice(u * BANK, (u + 1) * BANK)
+            nc.gpsimd.tensor_tensor(last_h[u][:], first_last[:, cols], second_last[:, cols], ALU.add)
         turn(2, TURN_BANKS + W1_BANKS)
         w3_rounded = at(head_at, [P, GROUPS * N, PACK], BF16, "w3_rounded")
         for g in range(GROUPS):
@@ -309,7 +338,6 @@ def tile_list_chart_tile_planes_kernel(
         page_halves = [slice(x * half, (x + 1) * half) for x in range(2)]
         woven0 = [turn_back(x) for x in range(2)]
         pairs = at(raw_at + 4 * KIB, [P, 2, T2, 2], BF16, "pairs")
-        nc.gpsimd.memset(pairs[:, 1, :, :].rearrange("p m b -> p (m b)").bitcast(I32), 0)
         for i in range(PACK, LAST):
             scatter_and_round(i)
 

@@ -28,6 +28,7 @@ HALVES = S // BANK
 CHUNKS = T2 // BANK
 NT = N // P
 KIB = 1024
+TINY = 2.0**-126
 QUADRANTS = 4
 
 W1_BANKS = (4, 5)
@@ -319,10 +320,9 @@ def tile_list_chart_tile_planes_kernel(
         take_second = at(h_places[LAST - 1], [P, S], F32, "take_second")
         take_first = at(front_at + 4 * KIB, [P, S], F32, "take_first")
         nc.gpsimd.tensor_tensor(take_second[:], second_last[:], first_last[:], ALU.subtract)
-        nc.gpsimd.tensor_scalar(take_second[:], take_second[:], 1.0, 0.0, ALU.min, ALU.max)
-        nc.gpsimd.tensor_scalar(take_second[:], take_second[:], 2.0**63, 2.0**63, ALU.mult, ALU.mult)
-        nc.gpsimd.tensor_scalar(take_second[:], take_second[:], 1.0, 0.0, ALU.min, ALU.max)
-        nc.gpsimd.tensor_scalar(take_first[:], take_second[:], -1.0, 1.0, ALU.mult, ALU.add)
+        nc.gpsimd.tensor_scalar(take_second[:], take_second[:], TINY, 0.0, ALU.min, ALU.max)
+        nc.gpsimd.tensor_scalar(take_first[:], take_second[:], -1.0 / TINY, 1.0, ALU.mult, ALU.add)
+        nc.gpsimd.tensor_scalar(take_second[:], take_second[:], 1.0 / TINY, 0.0, ALU.mult, ALU.add)
         nc.gpsimd.tensor_tensor(second_last[:], second_last[:], take_second[:], ALU.mult)
         nc.gpsimd.tensor_tensor(first_last[:], first_last[:], take_first[:], ALU.mult)
         last_h = [at(late_at + (4 + 2 * u) * KIB, [P, BANK], F32, f"h{LAST}_{u}") for u in range(HALVES)]
@@ -362,7 +362,8 @@ def tile_list_chart_tile_planes_kernel(
             return [slice(cols.start, middle), slice(middle, cols.stop)]
 
         chunks = [slice(c * BANK, (c + 1) * BANK) for c in range(CHUNKS)]
-        units = [(cols, n) for cols in chunks for n in range(NT)][:-1] + [(cols, NT - 1) for cols in halved(chunks[-1])]
+        ending = halved(chunks[-1])[:1] + halved(halved(chunks[-1])[1])
+        units = [(cols, n) for cols in chunks for n in range(NT)][:-1] + [(cols, NT - 1) for cols in ending]
         pieces = halved(chunks[0]) + chunks[1:]
         spans = [chunks[0], chunks[-1], slice(BANK, 3 * BANK)]
         places = [woven1_at, woven1_at + 4 * KIB, woven0_at]
@@ -410,7 +411,7 @@ def tile_list_chart_tile_planes_kernel(
             root = at(root_places[k % ROOT_BUFFERS], [P, width], F32, f"root{k}")
             nc.scalar.activation(scratch[:], d_of[k][:], ACT.Square)
             nc.scalar.activation(root[:], scratch[:], ACT.Abs_reciprocal_sqrt, bias=1.0)
-            if k >= len(units) - 3:
+            if k >= len(units) - 4:
                 nc.scalar.activation(scratch[:], root[:], ACT.Square)
                 store_unit(k, f_of[k], scratch)
                 return []

@@ -28,13 +28,17 @@ HALVES = S // BANK
 CHUNKS = T2 // BANK
 NT = N // P
 KIB = 1024
-TINY = 2.0**-126
+TOUCH = 64
 QUADRANTS = 4
+ON_VECTOR = 4
 
-W1_BANKS = (4, 5)
-TURN_BANKS = (6, 7)
-W2_BANKS = (2, 3, 0, 1)
-BANKS = (4, 5, 6, 7, 2, 3, 0, 1)
+OPENING_BANKS = ((0, 1), (2, 3), (4, 5))
+EARLY_A_BANKS = {1: (0, 2), 2: (4, 5), 3: (0, 2)}
+B_BANKS = {1: (1, 3), 2: (6, 7), 3: (4, 5)}
+PAIRED_BANKS = ((0, 6, 2, 7), (1, 4, 3, 5))
+BANKS = PAIRED_BANKS[0] + PAIRED_BANKS[1]
+BACK_BANKS = PAIRED_BANKS
+BYTE_OF = (0, 2, 1, 3)
 D_LEAD = 3
 COPY_BUFFERS = 8
 ROOT_BUFFERS = 8
@@ -58,30 +62,26 @@ def tile_list_chart_tile_planes_kernel(
 
         half = T2 // 2
         tab_at = 0
-        head_at = tab_at + 8 * KIB
-        h_at = head_at + 15 * KIB // 2
-        woven0_at = h_at + 33 * KIB // 4
+        ring_at = tab_at + 8 * KIB
+        woven0_at = ring_at + 20 * KIB
         woven1_at = woven0_at + 16 * KIB
-        raw_at = woven1_at + 16 * KIB
+        raw_at = woven1_at + 10 * KIB
         copies_at = raw_at + 32 * KIB
         late_at = copies_at + 16 * KIB
-        h1_at = h_at + 4 * KIB
-        w1_back_scales_at = h1_at + 9 * KIB // 2
-        w1_late_scales_at = w1_back_scales_at + KIB // 4
-        h_places = [
-            h1_at + 15 * KIB // 4, h1_at, h1_at - 15 * KIB // 4, h1_at + KIB // 4,
-            tab_at + 4 * KIB, tab_at, late_at,
-        ]
+        spare_at = late_at + 11 * KIB // 2
+        pairs_at = raw_at + 16 * KIB
+        late_w1_at = ring_at + 12 * KIB
+        value_places = [ring_at, late_w1_at - 4 * KIB + TOUCH, ring_at + 4 * KIB, spare_at]
 
         idx = held([P, S // 16], U16, "idx")
         idx2 = held([P, S // 16], U16, "idx2")
         tab_w = at(tab_at, [P, T], U32, "tab_w")
         tab_s = held([P, T], U8, "tab_s")
-        w2_w = [held([P, 2 * PASS], U8, f"w2_w{g}") for g in range(GROUPS)]
+        w2_w = held([P, 2 * H], U8, "w2_w")
         w2_s = held([P, H], U8, "w2_s")
         w4_w = held([P, GROUPS, N], U32, "w4_w")
         w4_s = held([P, GROUPS, N], U8, "w4_s")
-        gain = [held([P, S], F32, f"gain{t}") for t in range(PACK)]
+        gain = [at(late_at, [P, S], F32, "gain2") if t == 2 else held([P, S], F32, f"gain{t}") for t in range(PACK)]
         plain_gain = held([P, S], F32, "plain_gain")
         identity = held([P, P], F32, "identity")
         make_identity(nc, identity[:])
@@ -90,7 +90,7 @@ def tile_list_chart_tile_planes_kernel(
         def tile_rows(matrix, i):
             if i < PACK:
                 return matrix[i * P : (i + 1) * P, :]
-            return matrix[PASS:, :].rearrange("(p t) m -> t p m", t=PACK)[i - PACK]
+            return matrix[PASS:, :].rearrange("(p t) m -> t p m", t=PACK)[BYTE_OF[i - PACK]]
 
         wgs_rows = wgs.rearrange("(q t) j -> q t j", t=PACK)
 
@@ -100,10 +100,9 @@ def tile_list_chart_tile_planes_kernel(
         nc.vector.memset(w2_s[:].bitcast(I32), 0)
         nc.vector.memset(warm[:], 1.0)
         nc.vector.memset(w4_s[:].rearrange("p a n -> p (a n)").bitcast(I32), 0)
-        front_at = woven1_at + 8 * KIB
-        w1_front = at(front_at, [P, PACK, 2 * P], F32, "w1_front")
-        w1_back = at(raw_at, [P, PACK, 2 * P], F32, "w1_back")
-        w1_late = at(woven1_at, [P, PACK, PASS], F32, "w1_raw1")
+        w1_front = at(copies_at + 12 * KIB, [P, PACK, P], F32, "w1_front")
+        w1_back = at(raw_at, [P, PACK, 3 * P], F32, "w1_back")
+        w1_late = at(woven1_at, [P, PACK, PASS], F32, "w1_late")
         w3_raw = [at(raw_at + (20 + 6 * g) * KIB, [P, PACK, N], F32, f"w3_raw{g}") for g in range(GROUPS)]
         w1_rows = w1.rearrange("(p j) c -> p j c", j=PACK)
         w3_rows = w3.rearrange("(g p j) n -> g p j n", g=GROUPS, j=PACK)
@@ -113,30 +112,32 @@ def tile_list_chart_tile_planes_kernel(
 
         def load_gain(t):
             for q in (0, 2, 1, 3):
-                nc.sync.dma_start(gain[t][32 * q : 32 * q + 32, :], wgs_rows[:, t, :])
+                nc.sync.dma_start(gain[t][32 * q : 32 * q + 32, :], wgs_rows[:, BYTE_OF[t], :])
 
         nc.sync.dma_start(idx[:], offs)
         nc.sync.dma_start(idx2[:], offs2)
         for q in range(QUADRANTS):
             nc.sync.dma_start(tab_s[32 * q : 32 * q + 4, :].bitcast(I32), tab_scales[0, 4 * q : 4 * q + 4, :].bitcast(I32))
+        nc.sync.dma_start(w1_front[:], w1_rows[:, :, :P])
         nc.sync.dma_start(tab_w[:].bitcast(I32), tab_words[0].rearrange("p n t -> p (n t)").bitcast(I32))
         for q in range(QUADRANTS):
             nc.sync.dma_start(w2_s[32 * q : 32 * q + 4, :].bitcast(I32), w2_scales[0, 4 * q : 4 * q + 4, :].bitcast(I32))
-        nc.sync.dma_start(w2_w[0][:].bitcast(I32), w2_words[0, :, : 2 * PASS].bitcast(I32))
-        nc.sync.dma_start(w1_front[:], w1_rows[:, :, : 2 * P])
-        nc.sync.dma_start(w2_w[1][:].bitcast(I32), w2_words[0, :, 2 * PASS :].bitcast(I32))
+        nc.sync.dma_start(w2_w[:].bitcast(I32), w2_words[0].bitcast(I32))
         nc.scalar.activation(warm_out[:], warm[:], ACT.Abs_reciprocal_sqrt)
+        parts = [slice(0, 2 * P), slice(2 * P, BANK), slice(BANK, S)]
+        nc.sync.dma_start(plain_gain[:, parts[0]], wgs[:, parts[0]])
         load_page(0)
-        nc.sync.dma_start(plain_gain[:], wgs)
-        nc.sync.dma_start(w1_back[:], w1_rows[:, :, 2 * P : PASS])
+        nc.sync.dma_start(w1_back[:], w1_rows[:, :, P:PASS])
+        nc.sync.dma_start(plain_gain[:, 2 * P :], wgs[:, 2 * P :])
         nc.sync.dma_start(w1_late[:], w1_rows[:, :, PASS:])
-        for i in range(1, PACK):
-            load_page(i)
+        load_page(1)
         for g in range(GROUPS):
             nc.sync.dma_start(w3_raw[g][:], w3_rows[g])
-        for t in range(PACK):
-            load_gain(t)
-            load_page(PACK + t)
+        for i in range(2, TILES):
+            load_page(i)
+            if i < PACK:
+                load_gain(2 * i - PACK)
+                load_gain(2 * i - PACK + 1)
         nc.sync.dma_start(w4_w[:].bitcast(I32), w4_words.rearrange("a p n t -> p a (n t)").bitcast(I32))
         for q in range(QUADRANTS):
             nc.sync.dma_start(
@@ -145,81 +146,121 @@ def tile_list_chart_tile_planes_kernel(
             )
 
         v_s = held([P, S], U8, "v_s")
-        w1_c = [held([P, PASS], U32, f"w1_c{g}") for g in range(GROUPS)]
-        nc.vector.tensor_copy(v_s[:], tab_s[:].indirect(idx[:]))
-        w1_s = {}
+        v_w = [held([P, BANK], U32, f"v_w{u}") for u in range(HALVES)]
+        w1_c = held([P, H], U32, "w1_c")
+        w1_s = held([P, H], U8, "w1_s")
+        w2_dw = held([P, 2 * PASS], U8, "w2_dw")
+        w2_ds = held([P, PASS], U8, "w2_ds")
+        w2_used = [w2_w, w2_dw]
+        w2_scales_used = [w2_s, w2_ds]
+        halves = [slice(u * BANK, (u + 1) * BANK) for u in range(HALVES)]
 
-        def round_plain(rounded, raw):
-            nc.scalar.copy(rounded.rearrange("p (c i) j -> p c j i", i=4), raw.rearrange("p j (c i) -> p c j i", i=4))
+        def list_part(offsets, cols):
+            return offsets[:, cols.start // 16 : cols.stop // 16]
 
-        def quantise_w1(g, lo, hi, rounded, offset):
-            scales = at(offset, [P, (hi - lo) * P], U8, f"w1_s{g}_{lo}")
-            nc.vector.quantize_mx(w1_c[g][:, lo * P : hi * P].bitcast(FP8X4), scales[:], rounded[:].rearrange("p c j -> p (c j)"))
-            for t in range(lo, hi):
-                w1_s[PACK * g + t] = scales[:, (t - lo) * P : (t - lo + 1) * P]
+        def walk(rounded, raw):
+            return rounded.rearrange("p (c i) j -> p c j i", i=4), raw.rearrange("p j (c i) -> p c j i", i=4)
 
-        def w1_product(i, u, bank):
-            g, t = divmod(i, PACK)
-            product = psum.tile([P, BANK], F32, name="w1_product", tag=f"bank{bank}")
+        def quantise_w1(cols, rounded):
+            nc.vector.quantize_mx(w1_c[:, cols].bitcast(FP8X4), w1_s[:, cols], rounded[:].rearrange("p c j -> p (c j)"))
+
+        def stationary(i):
+            return i if i < PACK else PACK + BYTE_OF[i - PACK]
+
+        def moving(cols):
+            u = cols.start // BANK
+            return v_w[u][:, cols.start - u * BANK : cols.stop - u * BANK].bitcast(FP8X4)
+
+        def w1_product(i, cols, bank):
+            rows = slice(stationary(i) * P, (stationary(i) + 1) * P)
+            product = psum.tile([P, cols.stop - cols.start], F32, name="w1_product", tag=f"bank{bank}")
             nc.tensor.matmul_mx(
-                product[:], lhsT=w1_c[g][:, t * P : (t + 1) * P].bitcast(FP8X4), lhsT_scale=w1_s[i],
-                rhs=v_w[u][:].bitcast(FP8X4), rhs_scale=v_s[:, u * BANK : (u + 1) * BANK], start=True, stop=True,
+                product[:], lhsT=w1_c[:, rows].bitcast(FP8X4), lhsT_scale=w1_s[:, rows],
+                rhs=moving(cols), rhs_scale=v_s[:, cols], start=True, stop=True,
             )
             return product
 
-        def w2_products(i):
-            g, t = divmod(i, PACK)
-            products = []
-            for u in range(HALVES):
-                products.append(psum.tile([P, BANK], F32, name="w2_product", tag=f"bank{W2_BANKS[2 * (i % 2) + u]}"))
-                nc.tensor.matmul_mx(
-                    products[u][:], lhsT=w2_used[g][:, 2 * t * P : 2 * (t + 1) * P].bitcast(FP4X4),
-                    lhsT_scale=w2_scales_used[g][:, t * P : (t + 1) * P],
-                    rhs=v_w[u][:].bitcast(FP8X4), rhs_scale=v_s[:, u * BANK : (u + 1) * BANK], start=True, stop=True,
-                )
-            return products
+        def w2_product(i, cols, bank):
+            g, t = divmod(stationary(i), PACK)
+            product = psum.tile([P, cols.stop - cols.start], F32, name="w2_product", tag=f"bank{bank}")
+            nc.tensor.matmul_mx(
+                product[:], lhsT=w2_used[g][:, 2 * t * P : 2 * (t + 1) * P].bitcast(FP4X4),
+                lhsT_scale=w2_scales_used[g][:, t * P : (t + 1) * P],
+                rhs=moving(cols), rhs_scale=v_s[:, cols], start=True, stop=True,
+            )
+            return product
 
-        in_sbuf = {}
-        h = {}
-        scaled = {}
+        first = {}
+        second = {}
+        value = {}
 
-        def copied_w1_products(i, banks):
-            in_sbuf[i] = []
+        def one_copied(i, place):
+            first[i] = at(place, [P, S], F32, f"first{i}")
+            second[i] = []
             for u in range(HALVES):
-                product = w1_product(i, u, banks[u])
-                buffer = (HALVES * i + u) % COPY_BUFFERS
-                place = woven1_at if (i, u) == (2, 0) else copies_at + 2 * KIB * buffer
-                in_sbuf[i].append(at(place, [P, BANK], F32, f"w1_copy{i}_{u}"))
-                nc.scalar.copy(in_sbuf[i][u][:], product[:])
+                nc.scalar.copy(first[i][:, halves[u]], w1_product(i, halves[u], EARLY_A_BANKS[i][u])[:])
+                second[i].append(w2_product(i, halves[u], B_BANKS[i][u]))
 
-        def larger(i, in_psum):
-            h[i] = at(h_places[i], [P, S], F32, f"h{i}")
+        def larger(i):
+            value[i] = at(value_places[i] if i < 3 else ring_at + 16 * KIB, [P, S], F32, f"value{i}")
             for u in range(HALVES):
-                nc.vector.tensor_tensor(h[i][:, u * BANK : (u + 1) * BANK], in_psum[u][:], in_sbuf[i][u][:], ALU.max)
+                nc.vector.tensor_tensor(value[i][:, halves[u]], second[i][u][:], first[i][:, halves[u]], ALU.max)
+
+        def both_place(i):
+            return copies_at + 8 * KIB * (i % 2)
+
+        def both_copied(i):
+            if i == ON_VECTOR:
+                first[i] = at(both_place(i), [P, S], F32, f"first{i}")[:]
+                second[i] = at(spare_at, [P, S], F32, f"second{i}")[:]
+            else:
+                both = at(both_place(i), [P, 2, S], F32, f"both{i}")
+                first[i], second[i] = both[:, 0, :], both[:, 1, :]
+            for u in range(HALVES):
+                nc.scalar.copy(first[i][:, halves[u]], w1_product(i, halves[u], PAIRED_BANKS[i % 2][2 * u])[:])
+                nc.scalar.copy(second[i][:, halves[u]], w2_product(i, halves[u], PAIRED_BANKS[i % 2][2 * u + 1])[:])
+
+        def excess(i):
+            place = both_place(i + 1) if i < LAST else pairs_at
+            difference = at(place, [P, S], F32, f"difference{i}")
+            value[i] = at(value_places[i % PACK], [P, S], F32, f"value{i}")
+            nc.gpsimd.tensor_tensor(difference[:], second[i], first[i], ALU.subtract)
+            nc.scalar.activation(value[i][:], difference[:], ACT.Relu)
+
+        def add_first(i):
+            nc.gpsimd.tensor_tensor(value[i][:], value[i][:], first[i], ALU.add)
 
         def factor(i):
             return plain_gain if i < PACK else gain[i - PACK]
 
-        def scatter(i):
-            if i in scaled:
-                nc.vector.tensor_copy(page[i][:].indirect(idx2[:]), scaled[i][:])
-            else:
-                nc.vector.tensor_tensor(page[i][:].indirect(idx2[:]), h[i][:], factor(i)[:], ALU.mult)
+        def weigh(i):
+            nc.gpsimd.tensor_tensor(value[i][:], value[i][:], factor(i)[:], ALU.mult)
+
+        def store_page(i):
             nc.sync.dma_start(tile_rows(out_1, i), page[i][:])
 
-        def turn(i, banks):
+        def scatter(i):
+            nc.vector.tensor_copy(page[i][:].indirect(idx2[:]), value[i][:])
+            store_page(i)
+
+        turned = at(raw_at, [P, T2 // P, 2, P, 2], BF16, "turned")
+
+        def turn(i):
             for q in range(CHUNKS):
-                bank = psum.tile([P, PACK, P], F32, name="turned", tag=f"bank{banks[q % len(banks)]}")
+                bank = psum.tile([P, PACK, P], F32, name="turned", tag=f"bank{PAIRED_BANKS[i % 2][q]}")
                 for c in range(PACK):
                     lo = q * BANK + c * P
                     nc.tensor.transpose(bank[:, c, :], page[i][:, lo : lo + P], identity[:])
-                nc.scalar.copy(turned[:, PACK * q : PACK * (q + 1), i * P : (i + 1) * P], bank[:])
+                nc.scalar.copy(
+                    turned[:, PACK * q : PACK * (q + 1), :, 32 * i : 32 * (i + 1), :],
+                    bank[:].rearrange("p c (w u b) -> p c u w b", u=2, b=2),
+                )
 
         def turn_back(x):
             woven = at(woven0_at + 8 * KIB * x, [P, half * PACK], BF16, f"woven0_{x}")
-            words = turned[:].rearrange("p c r -> p (c r)").bitcast(F32).rearrange("p (c w u) -> p c u w", u=2, w=P)
+            words = turned[:].rearrange("p c u w b -> p (c u w b)").bitcast(F32).rearrange("p (c u w) -> p c u w", u=2, w=P)
             for q in range(half // (2 * P)):
-                bank = psum.tile([P, 2, 2, P], F32, name="turned_back", tag=f"bank{(W1_BANKS + TURN_BANKS)[q]}")
+                bank = psum.tile([P, 2, 2, P], F32, name="turned_back", tag=f"bank{BACK_BANKS[x][q]}")
                 for c in range(2):
                     for u in range(2):
                         nc.tensor.transpose(bank[:, c, u, :], words[:, 8 * x + 2 * q + c, u, :], identity[:])
@@ -229,11 +270,11 @@ def tile_list_chart_tile_planes_kernel(
                 )
             return woven
 
-        def scatter_and_round(i):
-            scatter(i)
-            t = i % PACK
-            if i == LAST - 1:
-                nc.scalar.copy(pairs[:, 1, :, :], page[i][:].unsqueeze(2).to_broadcast([P, T2, 2]))
+        def round_to_pairs(i):
+            t = BYTE_OF[i - PACK]
+            if t == 2:
+                both_places = page[i][:].unsqueeze(2).to_broadcast([P, T2, 2])
+                nc.gpsimd.tensor_scalar(pairs[:, 1, :, :], both_places, 1.0, 0.0, ALU.mult, ALU.add)
             else:
                 nc.scalar.copy(pairs[:, 0, :, t], page[i][:])
 
@@ -257,101 +298,97 @@ def tile_list_chart_tile_planes_kernel(
             for q in range(QUADRANTS):
                 nc.sync.dma_start(out_3[g, 4 * q : 4 * q + 4, :].bitcast(I32), p_s[g][32 * q : 32 * q + 4, :].bitcast(I32))
 
-        front = at(head_at + 7 * KIB // 4, [P, 2 * P, PACK], BF16, "w1_rounded0")
-        round_plain(front[:], w1_front[:])
-        v_w = [held([P, BANK], U32, f"v_w{u}") for u in range(HALVES)]
-        for u in range(HALVES):
-            nc.vector.tensor_copy(v_w[u][:], tab_w[:].indirect(idx[:, u * BANK // 16 : (u + 1) * BANK // 16]))
-        quantise_w1(0, 0, 2, front, tab_at)
-        w2_dw = at(head_at + 5 * KIB // 2, [P, 2 * PASS], U8, "w2_dw")
-        w2_ds = at(head_at + 2 * KIB, [P, PASS], U8, "w2_ds")
+        nc.vector.tensor_copy(v_s[:], tab_s[:].indirect(idx[:]))
+        front = at(ring_at + 8 * KIB, [P, P, PACK], BF16, "w1_rounded0")
+        nc.scalar.copy(*walk(front[:], w1_front[:]))
+        quantise_w1(slice(0, P), front)
+        for cols in parts:
+            u = cols.start // BANK
+            nc.vector.tensor_copy(v_w[u][:, cols.start - u * BANK : cols.stop - u * BANK], tab_w[:].indirect(list_part(idx, cols)))
         nc.vector.tensor_copy(w2_ds[:].rearrange("p (t m) -> p t m", t=PACK), w2_s[:, PASS:].rearrange("p (m t) -> p t m", t=PACK))
-        nc.vector.tensor_copy(
-            w2_dw[:].bitcast(U16).rearrange("p (t m) -> p t m", t=PACK),
-            w2_w[1][:].bitcast(U16).rearrange("p (m t) -> p t m", t=PACK),
-        )
-        w2_used = [w2_w[0], w2_dw]
-        w2_scales_used = [w2_s, w2_ds]
-        early = w2_products(0)
-        late = [w1_product(0, u, W2_BANKS[2 + u]) for u in range(HALVES)]
-        in_sbuf[0] = []
-        for u in range(HALVES):
-            in_sbuf[0].append(at(front_at + 2 * KIB * u, [P, BANK], F32, f"w2_copy{u}"))
-            nc.scalar.copy(in_sbuf[0][u][:], early[u][:])
-        larger(0, late)
-        copied_w1_products(1, W2_BANKS[0:2])
-        back = at(front_at, [P, 2 * P, PACK], BF16, "w1_rounded1")
-        round_plain(back[:], w1_back[:])
-        rounded1 = at(front_at + 2 * KIB, [P, PASS, PACK], BF16, "w1_rounded2")
-        nc.scalar.copy(
-            rounded1[:].rearrange("p (t m) j -> p m j t", t=PACK), w1_late[:].rearrange("p j (m t) -> p m j t", t=PACK)
-        )
+        back_at = ring_at + 4 * KIB - TOUCH
+        opening = []
+        for j, cols in enumerate(parts):
+            copied = at(copies_at + 4 * cols.start, [P, cols.stop - cols.start], F32, f"opening_first{j}")
+            nc.scalar.copy(copied[:], w1_product(0, cols, OPENING_BANKS[j][0])[:])
+            opening.append((cols, copied, w2_product(0, cols, OPENING_BANKS[j][1])))
 
-        scatter(0)
-        larger(1, w2_products(1))
-        quantise_w1(0, 2, PACK, back, w1_back_scales_at)
-        quantise_w1(1, 0, PACK, rounded1, w1_late_scales_at)
-        copied_w1_products(2, W1_BANKS)
-        copied_w1_products(3, TURN_BANKS)
-        for i in (4, 5):
-            copied_w1_products(i, W1_BANKS)
-        turned = at(raw_at + 4 * KIB, [P, T2 // P, PASS], BF16, "turned")
-        turn(0, TURN_BANKS)
-        scatter(1)
-        for i in range(2, PACK):
-            larger(i, w2_products(i))
-        copied_w1_products(6, W1_BANKS)
-        for i in range(PACK, LAST):
-            larger(i, w2_products(i))
-        first_last = at(copies_at + 12 * KIB, [P, S], F32, "w1_copy_last")
-        second_last = at(front_at, [P, S], F32, "w2_copy_last")
-        last_products = w2_products(LAST)
-        for u in range(HALVES):
-            cols = slice(u * BANK, (u + 1) * BANK)
-            nc.scalar.copy(first_last[:, cols], w1_product(LAST, u, W1_BANKS[u])[:])
-            nc.scalar.copy(second_last[:, cols], last_products[u][:])
-        turn(1, TURN_BANKS)
+        def opening_larger(j):
+            cols, copied, in_psum = opening[j]
+            out = at(ring_at + 4 * cols.start, [P, cols.stop - cols.start], F32, f"opening{j}")
+            nc.vector.tensor_tensor(out[:], in_psum[:], copied[:], ALU.max)
+            return out
+
+        def opening_scatter(j, values):
+            cols = parts[j]
+            nc.vector.tensor_tensor(page[0][:].indirect(list_part(idx2, cols)), values[:], plain_gain[:, cols], ALU.mult)
+
+        opening_scatter(0, opening_larger(0))
+        opening_scatter(1, opening_larger(1))
+        back = at(back_at, [P, 3 * P, PACK], BF16, "w1_rounded1")
+        nc.scalar.copy(*walk(back[:], w1_back[:]))
+        quantise_w1(slice(P, PASS), back)
+        opening_scatter(2, opening_larger(2))
+        store_page(0)
+        late = at(late_w1_at, [P, PASS, PACK], BF16, "w1_rounded2")
+        nc.scalar.copy(
+            late[:].rearrange("p (t m) j -> p m j t", t=PACK), w1_late[:].rearrange("p j (m t) -> p m j t", t=PACK)
+        )
+        for i in range(1, ON_VECTOR):
+            one_copied(i, copies_at + 4 * KIB * i)
+        nc.scalar.copy(
+            w2_dw[:].bitcast(U16).rearrange("p (t m) -> p t m", t=PACK),
+            w2_w[:, 2 * PASS :].bitcast(U16).rearrange("p (m t) -> p t m", t=PACK),
+        )
+        quantise_w1(slice(PASS, H), late)
+        for i in range(1, ON_VECTOR):
+            larger(i)
+        weighed1 = at(copies_at + 4 * KIB, [P, S], F32, "weighed1")
+        for cols in halves:
+            nc.gpsimd.tensor_tensor(weighed1[:, cols], value[1][:, cols], plain_gain[:, cols], ALU.mult)
+        for cols in halves:
+            nc.vector.tensor_copy(page[1][:].indirect(list_part(idx2, cols)), weighed1[:, cols])
+        store_page(1)
+        weigh(2)
         scatter(2)
-        scaled[3] = at(h_places[2], [P, S], F32, "scaled3")
-        nc.gpsimd.tensor_tensor(scaled[3][:], h[3][:], factor(3)[:], ALU.mult)
-        for i in range(PACK, LAST):
-            scaled[i] = h[i] if i < LAST - 1 else at(h_places[3], [P, S], F32, "scaled6")
-            nc.gpsimd.tensor_tensor(scaled[i][:], h[i][:], factor(i)[:], ALU.mult)
-        take_second = at(h_places[LAST - 1], [P, S], F32, "take_second")
-        take_first = at(front_at + 4 * KIB, [P, S], F32, "take_first")
-        nc.gpsimd.tensor_tensor(take_second[:], second_last[:], first_last[:], ALU.subtract)
-        nc.gpsimd.tensor_scalar(take_second[:], take_second[:], TINY, 0.0, ALU.min, ALU.max)
-        nc.gpsimd.tensor_scalar(take_first[:], take_second[:], -1.0 / TINY, 1.0, ALU.mult, ALU.add)
-        nc.gpsimd.tensor_scalar(take_second[:], take_second[:], 1.0 / TINY, 0.0, ALU.mult, ALU.add)
-        nc.gpsimd.tensor_tensor(second_last[:], second_last[:], take_second[:], ALU.mult)
-        nc.gpsimd.tensor_tensor(first_last[:], first_last[:], take_first[:], ALU.mult)
-        last_h = [at(late_at + (4 + 2 * u) * KIB, [P, BANK], F32, f"h{LAST}_{u}") for u in range(HALVES)]
-        for u in range(HALVES):
-            cols = slice(u * BANK, (u + 1) * BANK)
-            nc.gpsimd.tensor_tensor(last_h[u][:], first_last[:, cols], second_last[:, cols], ALU.add)
-        turn(2, TURN_BANKS + W1_BANKS)
-        w3_rounded = at(head_at, [P, GROUPS * N, PACK], BF16, "w3_rounded")
-        for g in range(GROUPS):
-            round_plain(w3_rounded[:, g * N : (g + 1) * N, :], w3_raw[g][:])
+        both_copied(ON_VECTOR)
+        excess(ON_VECTOR)
+        turn(0)
+        larger3 = value[3]
+        value[3] = at(spare_at, [P, S], F32, "weighed3")
+        nc.gpsimd.tensor_tensor(value[3][:], larger3[:], plain_gain[:], ALU.mult)
         scatter(3)
-        turn(3, TURN_BANKS + W1_BANKS)
+        for i in range(ON_VECTOR, LAST):
+            both_copied(i + 1)
+            add_first(i)
+            excess(i + 1)
+            turn(i - ON_VECTOR + 1)
+            weigh(i)
+            scatter(i)
+        w3_rounded = at(late_w1_at + 2 * TOUCH, [P, GROUPS * N, PACK], BF16, "w3_rounded")
+        for g in range(GROUPS):
+            for n in range(NT):
+                nc.scalar.copy(*walk(w3_rounded[:, g * N + n * P : g * N + (n + 1) * P, :], w3_raw[g][:, :, n * P : (n + 1) * P]))
         page_halves = [slice(x * half, (x + 1) * half) for x in range(2)]
         woven0 = [turn_back(x) for x in range(2)]
-        pairs = at(raw_at + 4 * KIB, [P, 2, T2, 2], BF16, "pairs")
+        last_sum = [at(pairs_at + 4 * KIB, [P, BANK], F32, "last_sum")[:], value[LAST][:, halves[1]]]
+        for u in range(HALVES):
+            nc.gpsimd.tensor_tensor(last_sum[u], value[LAST][:, halves[u]], first[LAST][:, halves[u]], ALU.add)
+        last_value = [at(place, [P, BANK], F32, f"last_value{u}") for u, place in enumerate((late_at + KIB, raw_at - 2 * KIB + TOUCH))]
+        for u in range(HALVES):
+            nc.gpsimd.tensor_tensor(last_value[u][:], last_sum[u], factor(LAST)[:, halves[u]], ALU.mult)
+        pairs = at(pairs_at - TOUCH, [P, 2, T2, 2], BF16, "pairs")
         for i in range(PACK, LAST):
-            scatter_and_round(i)
+            round_to_pairs(i)
 
         def scatter_half(u):
-            nc.vector.tensor_tensor(
-                page[LAST][:].indirect(idx2[:, u * BANK // 16 : (u + 1) * BANK // 16]), last_h[u][:],
-                gain[PACK - 1][:, u * BANK : (u + 1) * BANK], ALU.mult,
-            )
+            nc.vector.tensor_copy(page[LAST][:].indirect(list_part(idx2, halves[u])), last_value[u][:])
 
         scatter_half(0)
-        w3_s = at(late_at + 5 * KIB, [P, GROUPS * N], U8, "w3_s")
+        w3_s = at(late_at + 5 * KIB // 2, [P, GROUPS * N], U8, "w3_s")
         for cols in (slice(0, BANK), slice(BANK, GROUPS * N)):
             nc.vector.quantize_mx(w3_c[:, cols].bitcast(FP8X4), w3_s[:, cols], w3_rounded[:, cols, :].rearrange("p n j -> p (n j)"))
-        p_s[0] = at(late_at + 5 * KIB // 2, [P, T2], U8, "p_s0")
+        p_s[0] = at(late_at, [P, T2], U8, "p_s0")
         for x in (1, 0):
             quantise_page(0, page_halves[x], woven0[x][:])
             store_words(0, page_halves[x])
@@ -376,7 +413,7 @@ def tile_list_chart_tile_planes_kernel(
         scatter_half(1)
         nc.sync.dma_start(tile_rows(out_1, LAST), page[LAST][:])
         staged = [at(raw_at + n * 8 * KIB, [P, T2], F32, f"staged{n}") for n in range(NT)]
-        root_places = [region + 2 * KIB * j for region in (tab_at, h_at) for j in range(ROOT_BUFFERS // 2)]
+        root_places = [region + 2 * KIB * j for region in (tab_at, ring_at) for j in range(ROOT_BUFFERS // 2)]
         d_of = {}
         f_of = {}
 

@@ -35,9 +35,9 @@ ON_VECTOR = 4
 OPENING_BANKS = ((0, 1), (2, 3), (4, 5))
 EARLY_A_BANKS = {1: (0, 2), 2: (4, 5), 3: (0, 2)}
 B_BANKS = {1: (1, 3), 2: (6, 7), 3: (4, 5)}
-PAIRED_BANKS = ((0, 6, 2, 7), (1, 4, 3, 5))
-BANKS = PAIRED_BANKS[0] + PAIRED_BANKS[1]
-BACK_BANKS = PAIRED_BANKS
+PAIRED_BANKS = ((0, 6, 2, 7), (1, 0, 3, 2), (6, 1, 7, 3), (0, 6, 2, 7))
+BANKS = (4, 5, 1, 3, 0, 6, 2, 7)
+BACK_BANKS = ((4, 5, 1, 3), (0, 6, 2, 7))
 BYTE_OF = (0, 2, 1, 3)
 D_LEAD = 3
 COPY_BUFFERS = 8
@@ -69,6 +69,7 @@ def tile_list_chart_tile_planes_kernel(
         copies_at = raw_at + 32 * KIB
         late_at = copies_at + 16 * KIB
         spare_at = late_at + 11 * KIB // 2
+        head_at = spare_at + 4 * KIB
         pairs_at = raw_at + 16 * KIB
         late_w1_at = ring_at + 12 * KIB
         value_places = [ring_at, late_w1_at - 4 * KIB + TOUCH, ring_at + 4 * KIB, spare_at]
@@ -77,13 +78,14 @@ def tile_list_chart_tile_planes_kernel(
         idx2 = held([P, S // 16], U16, "idx2")
         tab_w = at(tab_at, [P, T], U32, "tab_w")
         tab_s = held([P, T], U8, "tab_s")
-        w2_w = held([P, 2 * H], U8, "w2_w")
+        w2_w = [held([P, 2 * PASS], U8, f"w2_w{g}") for g in range(GROUPS)]
         w2_s = held([P, H], U8, "w2_s")
         w4_w = held([P, GROUPS, N], U32, "w4_w")
         w4_s = held([P, GROUPS, N], U8, "w4_s")
         gain = [at(late_at, [P, S], F32, "gain2") if t == 2 else held([P, S], F32, f"gain{t}") for t in range(PACK)]
         plain_gain = held([P, S], F32, "plain_gain")
         identity = held([P, P], F32, "identity")
+        nc.gpsimd.memset(tab_s[:].bitcast(I32), 0)
         make_identity(nc, identity[:])
         page = [held([P, T2], F32, f"page{i}") for i in range(TILES)]
 
@@ -96,7 +98,6 @@ def tile_list_chart_tile_planes_kernel(
 
         warm = held([P, 1], F32, "warm")
         warm_out = held([P, 1], F32, "warm_out")
-        nc.vector.memset(tab_s[:].bitcast(I32), 0)
         nc.vector.memset(w2_s[:].bitcast(I32), 0)
         nc.vector.memset(warm[:], 1.0)
         nc.vector.memset(w4_s[:].rearrange("p a n -> p (a n)").bitcast(I32), 0)
@@ -122,13 +123,14 @@ def tile_list_chart_tile_planes_kernel(
         nc.sync.dma_start(tab_w[:].bitcast(I32), tab_words[0].rearrange("p n t -> p (n t)").bitcast(I32))
         for q in range(QUADRANTS):
             nc.sync.dma_start(w2_s[32 * q : 32 * q + 4, :].bitcast(I32), w2_scales[0, 4 * q : 4 * q + 4, :].bitcast(I32))
-        nc.sync.dma_start(w2_w[:].bitcast(I32), w2_words[0].bitcast(I32))
+        nc.sync.dma_start(w2_w[0][:].bitcast(I32), w2_words[0, :, : 2 * PASS].bitcast(I32))
         nc.scalar.activation(warm_out[:], warm[:], ACT.Abs_reciprocal_sqrt)
         parts = [slice(0, 2 * P), slice(2 * P, BANK), slice(BANK, S)]
-        nc.sync.dma_start(plain_gain[:, parts[0]], wgs[:, parts[0]])
+        nc.sync.dma_start(plain_gain[:, :BANK], wgs[:, :BANK])
         load_page(0)
         nc.sync.dma_start(w1_back[:], w1_rows[:, :, P:PASS])
-        nc.sync.dma_start(plain_gain[:, 2 * P :], wgs[:, 2 * P :])
+        nc.sync.dma_start(w2_w[1][:].bitcast(I32), w2_words[0, :, 2 * PASS :].bitcast(I32))
+        nc.sync.dma_start(plain_gain[:, BANK:], wgs[:, BANK:])
         nc.sync.dma_start(w1_late[:], w1_rows[:, :, PASS:])
         load_page(1)
         for g in range(GROUPS):
@@ -146,13 +148,13 @@ def tile_list_chart_tile_planes_kernel(
             )
 
         v_s = held([P, S], U8, "v_s")
-        v_w = [held([P, BANK], U32, f"v_w{u}") for u in range(HALVES)]
+        v_w = held([P, S], U32, "v_w")
         w1_c = held([P, H], U32, "w1_c")
         w1_s = held([P, H], U8, "w1_s")
+        w1_scales = [w1_s[:, i * P : (i + 1) * P] for i in range(TILES)]
         w2_dw = held([P, 2 * PASS], U8, "w2_dw")
-        w2_ds = held([P, PASS], U8, "w2_ds")
-        w2_used = [w2_w, w2_dw]
-        w2_scales_used = [w2_s, w2_ds]
+        w2_used = [w2_w[0], w2_dw]
+        w2_scales_used = [w2_s]
         halves = [slice(u * BANK, (u + 1) * BANK) for u in range(HALVES)]
 
         def list_part(offsets, cols):
@@ -167,16 +169,12 @@ def tile_list_chart_tile_planes_kernel(
         def stationary(i):
             return i if i < PACK else PACK + BYTE_OF[i - PACK]
 
-        def moving(cols):
-            u = cols.start // BANK
-            return v_w[u][:, cols.start - u * BANK : cols.stop - u * BANK].bitcast(FP8X4)
-
         def w1_product(i, cols, bank):
             rows = slice(stationary(i) * P, (stationary(i) + 1) * P)
             product = psum.tile([P, cols.stop - cols.start], F32, name="w1_product", tag=f"bank{bank}")
             nc.tensor.matmul_mx(
-                product[:], lhsT=w1_c[:, rows].bitcast(FP8X4), lhsT_scale=w1_s[:, rows],
-                rhs=moving(cols), rhs_scale=v_s[:, cols], start=True, stop=True,
+                product[:], lhsT=w1_c[:, rows].bitcast(FP8X4), lhsT_scale=w1_scales[stationary(i)],
+                rhs=v_w[:, cols].bitcast(FP8X4), rhs_scale=v_s[:, cols], start=True, stop=True,
             )
             return product
 
@@ -186,10 +184,11 @@ def tile_list_chart_tile_planes_kernel(
             nc.tensor.matmul_mx(
                 product[:], lhsT=w2_used[g][:, 2 * t * P : 2 * (t + 1) * P].bitcast(FP4X4),
                 lhsT_scale=w2_scales_used[g][:, t * P : (t + 1) * P],
-                rhs=moving(cols), rhs_scale=v_s[:, cols], start=True, stop=True,
+                rhs=v_w[:, cols].bitcast(FP8X4), rhs_scale=v_s[:, cols], start=True, stop=True,
             )
             return product
 
+        early_places = {1: woven1_at, 2: woven1_at + 4 * KIB, 3: copies_at + 12 * KIB}
         first = {}
         second = {}
         value = {}
@@ -217,15 +216,13 @@ def tile_list_chart_tile_planes_kernel(
                 both = at(both_place(i), [P, 2, S], F32, f"both{i}")
                 first[i], second[i] = both[:, 0, :], both[:, 1, :]
             for u in range(HALVES):
-                nc.scalar.copy(first[i][:, halves[u]], w1_product(i, halves[u], PAIRED_BANKS[i % 2][2 * u])[:])
-                nc.scalar.copy(second[i][:, halves[u]], w2_product(i, halves[u], PAIRED_BANKS[i % 2][2 * u + 1])[:])
+                nc.scalar.copy(first[i][:, halves[u]], w1_product(i, halves[u], PAIRED_BANKS[i - ON_VECTOR][2 * u])[:])
+                nc.scalar.copy(second[i][:, halves[u]], w2_product(i, halves[u], PAIRED_BANKS[i - ON_VECTOR][2 * u + 1])[:])
 
         def excess(i):
-            place = both_place(i + 1) if i < LAST else pairs_at
-            difference = at(place, [P, S], F32, f"difference{i}")
             value[i] = at(value_places[i % PACK], [P, S], F32, f"value{i}")
-            nc.gpsimd.tensor_tensor(difference[:], second[i], first[i], ALU.subtract)
-            nc.scalar.activation(value[i][:], difference[:], ACT.Relu)
+            nc.gpsimd.tensor_tensor(value[i][:], second[i], first[i], ALU.subtract)
+            nc.scalar.activation(value[i][:], value[i][:], ACT.Relu)
 
         def add_first(i):
             nc.gpsimd.tensor_tensor(value[i][:], value[i][:], first[i], ALU.add)
@@ -247,7 +244,7 @@ def tile_list_chart_tile_planes_kernel(
 
         def turn(i):
             for q in range(CHUNKS):
-                bank = psum.tile([P, PACK, P], F32, name="turned", tag=f"bank{PAIRED_BANKS[i % 2][q]}")
+                bank = psum.tile([P, PACK, P], F32, name="turned", tag=f"bank{PAIRED_BANKS[i][q]}")
                 for c in range(PACK):
                     lo = q * BANK + c * P
                     nc.tensor.transpose(bank[:, c, :], page[i][:, lo : lo + P], identity[:])
@@ -303,10 +300,9 @@ def tile_list_chart_tile_planes_kernel(
         nc.scalar.copy(*walk(front[:], w1_front[:]))
         quantise_w1(slice(0, P), front)
         for cols in parts:
-            u = cols.start // BANK
-            nc.vector.tensor_copy(v_w[u][:, cols.start - u * BANK : cols.stop - u * BANK], tab_w[:].indirect(list_part(idx, cols)))
-        nc.vector.tensor_copy(w2_ds[:].rearrange("p (t m) -> p t m", t=PACK), w2_s[:, PASS:].rearrange("p (m t) -> p t m", t=PACK))
-        back_at = ring_at + 4 * KIB - TOUCH
+            nc.vector.tensor_copy(v_w[:, cols], tab_w[:].indirect(list_part(idx, cols)))
+        back_at = head_at + PASS - TOUCH
+        opening_places = [ring_at, ring_at + KIB, back_at + KIB - TOUCH]
         opening = []
         for j, cols in enumerate(parts):
             copied = at(copies_at + 4 * cols.start, [P, cols.stop - cols.start], F32, f"opening_first{j}")
@@ -315,7 +311,7 @@ def tile_list_chart_tile_planes_kernel(
 
         def opening_larger(j):
             cols, copied, in_psum = opening[j]
-            out = at(ring_at + 4 * cols.start, [P, cols.stop - cols.start], F32, f"opening{j}")
+            out = at(opening_places[j], [P, cols.stop - cols.start], F32, f"opening{j}")
             nc.vector.tensor_tensor(out[:], in_psum[:], copied[:], ALU.max)
             return out
 
@@ -325,25 +321,35 @@ def tile_list_chart_tile_planes_kernel(
 
         opening_scatter(0, opening_larger(0))
         opening_scatter(1, opening_larger(1))
-        back = at(back_at, [P, 3 * P, PACK], BF16, "w1_rounded1")
-        nc.scalar.copy(*walk(back[:], w1_back[:]))
-        quantise_w1(slice(P, PASS), back)
-        opening_scatter(2, opening_larger(2))
+        back = [at(place, [P, (j + 1) * P, PACK], BF16, f"w1_back_rounded{j}") for j, place in enumerate((back_at, ring_at + 4 * KIB))]
+        for j in range(2):
+            nc.scalar.copy(*walk(back[j][:], w1_back[:, :, j * P : (2 * j + 1) * P]))
+        w1_scales[1] = at(raw_at, [P, P], U8, "w1_s1")[:]
+        nc.vector.quantize_mx(w1_c[:, P : 2 * P].bitcast(FP8X4), w1_scales[1], back[0][:].rearrange("p c j -> p (c j)"))
+        quantise_w1(slice(2 * P, PASS), back[1])
+        last_part = opening_larger(2)
+        w2_ds = at(head_at, [P, PASS], U8, "w2_ds")
+        w2_scales_used.append(w2_ds)
+        nc.vector.tensor_copy(w2_ds[:].rearrange("p (t m) -> p t m", t=PACK), w2_s[:, PASS:].rearrange("p (m t) -> p t m", t=PACK))
+        opening_scatter(2, last_part)
         store_page(0)
-        late = at(late_w1_at, [P, PASS, PACK], BF16, "w1_rounded2")
-        nc.scalar.copy(
-            late[:].rearrange("p (t m) j -> p m j t", t=PACK), w1_late[:].rearrange("p j (m t) -> p m j t", t=PACK)
-        )
+        late = [at(late_w1_at + 2 * KIB * j, [P, 2 * P, PACK], BF16, f"w1_late_rounded{j}") for j in range(2)]
+        for j in range(2):
+            nc.scalar.copy(
+                late[j][:].rearrange("p (t m) j -> p m j t", t=2),
+                w1_late[:].rearrange("p j (m t) -> p m j t", t=PACK)[:, :, :, 2 * j : 2 * j + 2],
+            )
         for i in range(1, ON_VECTOR):
-            one_copied(i, copies_at + 4 * KIB * i)
+            one_copied(i, early_places[i])
         nc.scalar.copy(
             w2_dw[:].bitcast(U16).rearrange("p (t m) -> p t m", t=PACK),
-            w2_w[:, 2 * PASS :].bitcast(U16).rearrange("p (m t) -> p t m", t=PACK),
+            w2_w[1][:].bitcast(U16).rearrange("p (m t) -> p t m", t=PACK),
         )
-        quantise_w1(slice(PASS, H), late)
+        for j in range(2):
+            quantise_w1(slice(PASS + 2 * P * j, PASS + 2 * P * (j + 1)), late[j])
         for i in range(1, ON_VECTOR):
             larger(i)
-        weighed1 = at(copies_at + 4 * KIB, [P, S], F32, "weighed1")
+        weighed1 = at(early_places[1], [P, S], F32, "weighed1")
         for cols in halves:
             nc.gpsimd.tensor_tensor(weighed1[:, cols], value[1][:, cols], plain_gain[:, cols], ALU.mult)
         for cols in halves:
@@ -354,15 +360,17 @@ def tile_list_chart_tile_planes_kernel(
         both_copied(ON_VECTOR)
         excess(ON_VECTOR)
         turn(0)
+        both_copied(ON_VECTOR + 1)
         larger3 = value[3]
         value[3] = at(spare_at, [P, S], F32, "weighed3")
         nc.gpsimd.tensor_tensor(value[3][:], larger3[:], plain_gain[:], ALU.mult)
         scatter(3)
         for i in range(ON_VECTOR, LAST):
-            both_copied(i + 1)
             add_first(i)
             excess(i + 1)
             turn(i - ON_VECTOR + 1)
+            if i + 2 < TILES:
+                both_copied(i + 2)
             weigh(i)
             scatter(i)
         w3_rounded = at(late_w1_at + 2 * TOUCH, [P, GROUPS * N, PACK], BF16, "w3_rounded")
@@ -386,8 +394,11 @@ def tile_list_chart_tile_planes_kernel(
 
         scatter_half(0)
         w3_s = at(late_at + 5 * KIB // 2, [P, GROUPS * N], U8, "w3_s")
-        for cols in (slice(0, BANK), slice(BANK, GROUPS * N)):
+
+        def quantise_w3(cols):
             nc.vector.quantize_mx(w3_c[:, cols].bitcast(FP8X4), w3_s[:, cols], w3_rounded[:, cols, :].rearrange("p n j -> p (n j)"))
+
+        quantise_w3(slice(0, BANK))
         p_s[0] = at(late_at, [P, T2], U8, "p_s0")
         for x in (1, 0):
             quantise_page(0, page_halves[x], woven0[x][:])
@@ -411,6 +422,7 @@ def tile_list_chart_tile_planes_kernel(
             return woven1[j][:, PACK * (cols.start - spans[j].start) : PACK * (cols.stop - spans[j].start)]
 
         scatter_half(1)
+        quantise_w3(slice(BANK, GROUPS * N))
         nc.sync.dma_start(tile_rows(out_1, LAST), page[LAST][:])
         staged = [at(raw_at + n * 8 * KIB, [P, T2], F32, f"staged{n}") for n in range(NT)]
         root_places = [region + 2 * KIB * j for region in (tab_at, ring_at) for j in range(ROOT_BUFFERS // 2)]

@@ -282,18 +282,24 @@ def tile_list_chart_tile_planes_kernel(
             return woven
 
         p_c = [held([P, T2], U32, f"p_c{g}") for g in range(GROUPS)]
-        p_s = {1: held([P, T2], U8, "p_s1")}
+        last_scales = held([P, T2], U8, "p_s1")
+        p_s = {(1, x): last_scales[:, x * half : (x + 1) * half] for x in range(2)}
+
+        def scales_of(g, cols):
+            x, lo = divmod(cols.start, half)
+            return p_s[g, x][:, lo : lo + cols.stop - cols.start]
+
         w3_c = held([P, GROUPS * N], U32, "w3_c")
 
         def quantise_page(g, cols, woven):
-            nc.vector.quantize_mx(p_c[g][:, cols].bitcast(FP8X4), p_s[g][:, cols], woven)
+            nc.vector.quantize_mx(p_c[g][:, cols].bitcast(FP8X4), scales_of(g, cols), woven)
 
         def store_words(g, cols):
             nc.sync.dma_start(out_2[g].rearrange("p m t -> p (m t)").bitcast(I32)[:, cols], p_c[g][:, cols].bitcast(I32))
 
-        def store_scales(g):
+        def store_scales(g, cols, scales):
             for q in range(QUADRANTS):
-                nc.sync.dma_start(out_3[g, 4 * q : 4 * q + 4, :].bitcast(I32), p_s[g][32 * q : 32 * q + 4, :].bitcast(I32))
+                nc.sync.dma_start(out_3[g, 4 * q : 4 * q + 4, cols].bitcast(I32), scales[32 * q : 32 * q + 4, :].bitcast(I32))
 
         nc.vector.tensor_copy(v_s[:], tab_s[:].indirect(idx[:]))
         front = at(ring_at + 8 * KIB, [P, P, PACK], BF16, "w1_rounded0")
@@ -399,11 +405,10 @@ def tile_list_chart_tile_planes_kernel(
             nc.vector.quantize_mx(w3_c[:, cols].bitcast(FP8X4), w3_s[:, cols], w3_rounded[:, cols, :].rearrange("p n j -> p (n j)"))
 
         quantise_w3(slice(0, BANK))
-        p_s[0] = at(late_at, [P, T2], U8, "p_s0")
-        for x in (1, 0):
-            quantise_page(0, page_halves[x], woven0[x][:])
-            store_words(0, page_halves[x])
-        store_scales(0)
+        p_s[0, 0] = at(late_at + KIB // 2, [P, half], U8, "p_s00")[:]
+        quantise_page(0, page_halves[0], woven0[0][:])
+        store_words(0, page_halves[0])
+        store_scales(0, page_halves[0], p_s[0, 0])
 
         def halved(cols):
             middle = (cols.start + cols.stop) // 2
@@ -435,7 +440,7 @@ def tile_list_chart_tile_planes_kernel(
                 d_of[k] = psum.tile([P, cols.stop - cols.start], F32, name="d", tag=f"bank{BANKS[sums.index((d_pass, k)) % len(BANKS)]}")
             nc.tensor.matmul_mx(
                 d_of[k][:], lhsT=w4_w[:, g, n * P : (n + 1) * P].bitcast(FP8X4), lhsT_scale=w4_s[:, g, n * P : (n + 1) * P],
-                rhs=p_c[g][:, cols].bitcast(FP8X4), rhs_scale=p_s[g][:, cols], start=(g == 0), stop=(g == GROUPS - 1),
+                rhs=p_c[g][:, cols].bitcast(FP8X4), rhs_scale=scales_of(g, cols), start=(g == 0), stop=(g == GROUPS - 1),
             )
 
         def f_pass(k, g):
@@ -445,12 +450,13 @@ def tile_list_chart_tile_planes_kernel(
             wcols = slice(g * N + n * P, g * N + (n + 1) * P)
             nc.tensor.matmul_mx(
                 f_of[k][:], lhsT=w3_c[:, wcols].bitcast(FP8X4), lhsT_scale=w3_s[:, wcols],
-                rhs=p_c[g][:, cols].bitcast(FP8X4), rhs_scale=p_s[g][:, cols], start=(g == 0), stop=(g == GROUPS - 1),
+                rhs=p_c[g][:, cols].bitcast(FP8X4), rhs_scale=scales_of(g, cols), start=(g == 0), stop=(g == GROUPS - 1),
             )
 
         def store_unit(k, left, right):
             cols, n = units[k]
-            nc.vector.tensor_tensor(staged[n][:, cols], left[:], right[:], ALU.mult)
+            engine = nc.gpsimd if k % 2 == 1 and k < len(units) - 3 else nc.vector
+            engine.tensor_tensor(staged[n][:, cols], left[:], right[:], ALU.mult)
             nc.sync.dma_start(out_0[n * P : (n + 1) * P, cols], staged[n][:, cols])
 
         def damp(k):
@@ -460,7 +466,7 @@ def tile_list_chart_tile_planes_kernel(
             root = at(root_places[k % ROOT_BUFFERS], [P, width], F32, f"root{k}")
             nc.scalar.activation(scratch[:], d_of[k][:], ACT.Square)
             nc.scalar.activation(root[:], scratch[:], ACT.Abs_reciprocal_sqrt, bias=1.0)
-            if k >= len(units) - 4:
+            if k >= len(units) - 2:
                 nc.scalar.activation(scratch[:], root[:], ACT.Square)
                 store_unit(k, f_of[k], scratch)
                 return []
@@ -493,9 +499,13 @@ def tile_list_chart_tile_planes_kernel(
         fill(pieces[2], nc.vector.tensor_copy)
         fill(slice(2 * BANK, shared), nc.vector.tensor_copy)
         quantise_piece(2)
+        p_s[0, 1] = at(woven1_at, [P, half], U8, "p_s01")[:]
+        quantise_page(0, page_halves[1], woven0[1][:])
+        store_words(0, page_halves[1])
+        store_scales(0, page_halves[1], p_s[0, 1])
         quantise_piece(3)
         quantise_piece(4)
-        store_scales(1)
+        store_scales(1, slice(0, T2), last_scales[:])
         waiting = []
         for place, (one_pass, k) in enumerate(sums):
             if place >= len(BANKS):

@@ -499,12 +499,12 @@ def tile_list_chart_tile_planes_kernel(
         fill(pieces[2], nc.vector.tensor_copy)
         fill(slice(2 * BANK, shared), nc.vector.tensor_copy)
         quantise_piece(2)
-        p_s[0, 1] = at(woven1_at, [P, half], U8, "p_s01")[:]
+        quantise_piece(4)
+        quantise_piece(3)
+        p_s[0, 1] = at(woven0_at, [P, half], U8, "p_s01")[:]
         quantise_page(0, page_halves[1], woven0[1][:])
         store_words(0, page_halves[1])
         store_scales(0, page_halves[1], p_s[0, 1])
-        quantise_piece(3)
-        quantise_piece(4)
         store_scales(1, slice(0, T2), last_scales[:])
         waiting = []
         for place, (one_pass, k) in enumerate(sums):

@@ -85,7 +85,6 @@ def tile_list_chart_tile_planes_kernel(
         gain = [at(late_at, [P, S], F32, "gain2") if t == 2 else held([P, S], F32, f"gain{t}") for t in range(PACK)]
         plain_gain = held([P, S], F32, "plain_gain")
         identity = held([P, P], F32, "identity")
-        nc.gpsimd.memset(tab_s[:].bitcast(I32), 0)
         make_identity(nc, identity[:])
         page = [held([P, T2], F32, f"page{i}") for i in range(TILES)]
 
@@ -98,6 +97,7 @@ def tile_list_chart_tile_planes_kernel(
 
         warm = held([P, 1], F32, "warm")
         warm_out = held([P, 1], F32, "warm_out")
+        nc.vector.memset(tab_s[:].bitcast(I32), 0)
         nc.vector.memset(w2_s[:].bitcast(I32), 0)
         nc.vector.memset(warm[:], 1.0)
         nc.vector.memset(w4_s[:].rearrange("p a n -> p (a n)").bitcast(I32), 0)

from contextlib import ExitStack

import concourse.mybir as mybir
from concourse.masks import make_identity

K, T, S, T2, H, N = 512, 2048, 1024, 2048, 1024, 384
FLOPS = 2 * (2 * K * H * S + 2 * H * N * T2)

F32 = mybir.dt.float32
BF16 = mybir.dt.bfloat16
I32 = mybir.dt.int32
U32 = mybir.dt.uint32
U16 = mybir.dt.uint16
U8 = mybir.dt.uint8
FP8X4 = mybir.dt.float8_e4m3fn_x4
FP4X4 = mybir.dt.float4_e2m1fn_x4
ALU = mybir.AluOpType
ACT = mybir.ActivationFunctionType

P = 128
PACK = 4
PASS = P * PACK
BANK = 512
GROUPS = H // PASS
TILES = GROUPS * PACK
LAST = TILES - 1
HALVES = S // BANK
CHUNKS = T2 // BANK
NT = N // P
KIB = 1024
TOUCH = 64
QUADRANTS = 4
ON_VECTOR = 4

OPENING_BANKS = ((0, 1), (2, 3), (4, 5))
EARLY_A_BANKS = {1: (0, 2), 2: (4, 5), 3: (0, 2)}
B_BANKS = {1: (1, 3), 2: (6, 7), 3: (4, 5)}
PAIRED_BANKS = ((0, 6, 2, 7), (1, 0, 3, 2), (6, 1, 7, 3), (0, 6, 2, 7))
BANKS = (4, 5, 1, 3, 0, 6, 2, 7)
BACK_BANKS = ((4, 5, 1, 3), (0, 6, 2, 7))
BYTE_OF = (0, 2, 1, 3)
D_LEAD = 3
COPY_BUFFERS = 8
ROOT_BUFFERS = 8


def tile_list_chart_tile_planes_kernel(
    tc, tab_words, tab_scales, offs, offs2, w1, w2_words, w2_scales, page0, wgs, w3, w4_words, w4_scales,
    out_0, out_1, out_2, out_3,
):
    nc = tc.nc
    with ExitStack() as ctx:
        keep = ctx.enter_context(tc.tile_pool(name="keep", bufs=1))
        placed = ctx.enter_context(tc.tile_pool(name="placed", bufs=1))
        psum = ctx.enter_context(tc.psum_pool(name="psum", bufs=1))

        def held(shape, dtype, name):
            return keep.tile(shape, dtype, name=name, align_bytes=64)

        def at(offset, shape, dtype, name):
            return placed.tile(shape, dtype, name=name, offset=offset, align_bytes=64)

        half = T2 // 2
        tab_at = 0
        ring_at = tab_at + 8 * KIB
        woven0_at = ring_at + 20 * KIB
        woven1_at = woven0_at + 16 * KIB
        raw_at = woven1_at + 10 * KIB
        copies_at = raw_at + 32 * KIB
        late_at = copies_at + 16 * KIB
        spare_at = late_at + 11 * KIB // 2
        head_at = spare_at + 4 * KIB
        pairs_at = raw_at + 16 * KIB
        late_w1_at = ring_at + 12 * KIB
        value_places = [ring_at, late_w1_at - 4 * KIB + TOUCH, ring_at + 4 * KIB, spare_at]

        idx = held([P, S // 16], U16, "idx")
        idx2 = held([P, S // 16], U16, "idx2")
        tab_w = at(tab_at, [P, T], U32, "tab_w")
        tab_s = held([P, T], U8, "tab_s")
        w2_w = [held([P, 2 * PASS], U8, f"w2_w{g}") for g in range(GROUPS)]
        w2_s = held([P, H], U8, "w2_s")
        w4_w = held([P, GROUPS, N], U32, "w4_w")
        w4_s = held([P, GROUPS, N], U8, "w4_s")
        gain = [at(late_at, [P, S], F32, "gain2") if t == 2 else held([P, S], F32, f"gain{t}") for t in range(PACK)]
        plain_gain = held([P, S], F32, "plain_gain")
        identity = held([P, P], F32, "identity")
        make_identity(nc, identity[:])
        page = [held([P, T2], F32, f"page{i}") for i in range(TILES)]

        def tile_rows(matrix, i):
            if i < PACK:
                return matrix[i * P : (i + 1) * P, :]
            return matrix[PASS:, :].rearrange("(p t) m -> t p m", t=PACK)[BYTE_OF[i - PACK]]

        wgs_rows = wgs.rearrange("(q t) j -> q t j", t=PACK)

        warm = held([P, 1], F32, "warm")
        warm_out = held([P, 1], F32, "warm_out")
        nc.vector.memset(tab_s[:].bitcast(I32), 0)
        nc.vector.memset(w2_s[:].bitcast(I32), 0)
        nc.vector.memset(warm[:], 1.0)
        nc.vector.memset(w4_s[:].rearrange("p a n -> p (a n)").bitcast(I32), 0)
        w1_front = at(copies_at + 12 * KIB, [P, PACK, P], F32, "w1_front")
        w1_back = at(raw_at, [P, PACK, 3 * P], F32, "w1_back")
        w1_late = at(woven1_at, [P, PACK, PASS], F32, "w1_late")
        w3_raw = [at(raw_at + (20 + 6 * g) * KIB, [P, PACK, N], F32, f"w3_raw{g}") for g in range(GROUPS)]
        w1_rows = w1.rearrange("(p j) c -> p j c", j=PACK)
        w3_rows = w3.rearrange("(g p j) n -> g p j n", g=GROUPS, j=PACK)

        def load_page(i):
            nc.sync.dma_start(page[i][:], tile_rows(page0, i))

        def load_gain(t):
            for q in (0, 2, 1, 3):
                nc.sync.dma_start(gain[t][32 * q : 32 * q + 32, :], wgs_rows[:, BYTE_OF[t], :])

        nc.sync.dma_start(idx[:], offs)
        nc.sync.dma_start(idx2[:], offs2)
        for q in range(QUADRANTS):
            nc.sync.dma_start(tab_s[32 * q : 32 * q + 4, :].bitcast(I32), tab_scales[0, 4 * q : 4 * q + 4, :].bitcast(I32))
        nc.sync.dma_start(w1_front[:], w1_rows[:, :, :P])
        nc.sync.dma_start(tab_w[:].bitcast(I32), tab_words[0].rearrange("p n t -> p (n t)").bitcast(I32))
        for q in range(QUADRANTS):
            nc.sync.dma_start(w2_s[32 * q : 32 * q + 4, :].bitcast(I32), w2_scales[0, 4 * q : 4 * q + 4, :].bitcast(I32))
        nc.sync.dma_start(w2_w[0][:].bitcast(I32), w2_words[0, :, : 2 * PASS].bitcast(I32))
        nc.scalar.activation(warm_out[:], warm[:], ACT.Abs_reciprocal_sqrt)
        parts = [slice(0, 2 * P), slice(2 * P, BANK), slice(BANK, S)]
        nc.sync.dma_start(plain_gain[:, :BANK], wgs[:, :BANK])
        load_page(0)
        nc.sync.dma_start(w1_back[:], w1_rows[:, :, P:PASS])
        nc.sync.dma_start(w2_w[1][:].bitcast(I32), w2_words[0, :, 2 * PASS :].bitcast(I32))
        nc.sync.dma_start(plain_gain[:, BANK:], wgs[:, BANK:])
        nc.sync.dma_start(w1_late[:], w1_rows[:, :, PASS:])
        load_page(1)
        for g in range(GROUPS):
            nc.sync.dma_start(w3_raw[g][:], w3_rows[g])
        for i in range(2, TILES):
            load_page(i)
            if i < PACK:
                load_gain(2 * i - PACK)
                load_gain(2 * i - PACK + 1)
        nc.sync.dma_start(w4_w[:].bitcast(I32), w4_words.rearrange("a p n t -> p a (n t)").bitcast(I32))
        for q in range(QUADRANTS):
            nc.sync.dma_start(
                w4_s[32 * q : 32 * q + 4, :, :].bitcast(I32),
                w4_scales[:, 4 * q : 4 * q + 4, :].rearrange("a r n -> r a n").bitcast(I32),
            )

        v_s = held([P, S], U8, "v_s")
        v_w = held([P, S], U32, "v_w")
        w1_c = held([P, H], U32, "w1_c")
        w1_s = held([P, H], U8, "w1_s")
        w1_scales = [w1_s[:, i * P : (i + 1) * P] for i in range(TILES)]
        w2_dw = held([P, 2 * PASS], U8, "w2_dw")
        w2_used = [w2_w[0], w2_dw]
        w2_scales_used = [w2_s]
        halves = [slice(u * BANK, (u + 1) * BANK) for u in range(HALVES)]

        def list_part(offsets, cols):
            return offsets[:, cols.start // 16 : cols.stop // 16]

        def walk(rounded, raw):
            return rounded.rearrange("p (c i) j -> p c j i", i=4), raw.rearrange("p j (c i) -> p c j i", i=4)

        def quantise_w1(cols, rounded):
            nc.vector.quantize_mx(w1_c[:, cols].bitcast(FP8X4), w1_s[:, cols], rounded[:].rearrange("p c j -> p (c j)"))

        def stationary(i):
            return i if i < PACK else PACK + BYTE_OF[i - PACK]

        def w1_product(i, cols, bank):
            rows = slice(stationary(i) * P, (stationary(i) + 1) * P)
            product = psum.tile([P, cols.stop - cols.start], F32, name="w1_product", tag=f"bank{bank}")
            nc.tensor.matmul_mx(
                product[:], lhsT=w1_c[:, rows].bitcast(FP8X4), lhsT_scale=w1_scales[stationary(i)],
                rhs=v_w[:, cols].bitcast(FP8X4), rhs_scale=v_s[:, cols], start=True, stop=True,
            )
            return product

        def w2_product(i, cols, bank):
            g, t = divmod(stationary(i), PACK)
            product = psum.tile([P, cols.stop - cols.start], F32, name="w2_product", tag=f"bank{bank}")
            nc.tensor.matmul_mx(
                product[:], lhsT=w2_used[g][:, 2 * t * P : 2 * (t + 1) * P].bitcast(FP4X4),
                lhsT_scale=w2_scales_used[g][:, t * P : (t + 1) * P],
                rhs=v_w[:, cols].bitcast(FP8X4), rhs_scale=v_s[:, cols], start=True, stop=True,
            )
            return product

        early_places = {1: woven1_at, 2: woven1_at + 4 * KIB, 3: copies_at + 12 * KIB}
        first = {}
        second = {}
        value = {}

        def one_copied(i, place):
            first[i] = at(place, [P, S], F32, f"first{i}")
            second[i] = []
            for u in range(HALVES):
                nc.scalar.copy(first[i][:, halves[u]], w1_product(i, halves[u], EARLY_A_BANKS[i][u])[:])
                second[i].append(w2_product(i, halves[u], B_BANKS[i][u]))

        def larger(i):
            value[i] = at(value_places[i] if i < 3 else ring_at + 16 * KIB, [P, S], F32, f"value{i}")
            for u in range(HALVES):
                nc.vector.tensor_tensor(value[i][:, halves[u]], second[i][u][:], first[i][:, halves[u]], ALU.max)

        def both_place(i):
            return copies_at + 8 * KIB * (i % 2)

        def both_copied(i):
            if i == ON_VECTOR:
                first[i] = at(both_place(i), [P, S], F32, f"first{i}")[:]
                second[i] = at(spare_at, [P, S], F32, f"second{i}")[:]
            else:
                both = at(both_place(i), [P, 2, S], F32, f"both{i}")
                first[i], second[i] = both[:, 0, :], both[:, 1, :]
            for u in range(HALVES):
                nc.scalar.copy(first[i][:, halves[u]], w1_product(i, halves[u], PAIRED_BANKS[i - ON_VECTOR][2 * u])[:])
                nc.scalar.copy(second[i][:, halves[u]], w2_product(i, halves[u], PAIRED_BANKS[i - ON_VECTOR][2 * u + 1])[:])

        def excess(i):
            value[i] = at(value_places[i % PACK], [P, S], F32, f"value{i}")
            nc.gpsimd.tensor_tensor(value[i][:], second[i], first[i], ALU.subtract)
            nc.scalar.activation(value[i][:], value[i][:], ACT.Relu)

        def add_first(i):
            nc.gpsimd.tensor_tensor(value[i][:], value[i][:], first[i], ALU.add)

        def factor(i):
            return plain_gain if i < PACK else gain[i - PACK]

        def weigh(i):
            nc.gpsimd.tensor_tensor(value[i][:], value[i][:], factor(i)[:], ALU.mult)

        def store_page(i):
            nc.sync.dma_start(tile_rows(out_1, i), page[i][:])

        def scatter(i):
            nc.vector.tensor_copy(page[i][:].indirect(idx2[:]), value[i][:])
            store_page(i)

        turned = at(raw_at, [P, T2 // P, 2, P, 2], BF16, "turned")

        def turn(i):
            for q in range(CHUNKS):
                bank = psum.tile([P, PACK, P], F32, name="turned", tag=f"bank{PAIRED_BANKS[i][q]}")
                for c in range(PACK):
                    lo = q * BANK + c * P
                    nc.tensor.transpose(bank[:, c, :], page[i][:, lo : lo + P], identity[:])
                nc.scalar.copy(
                    turned[:, PACK * q : PACK * (q + 1), :, 32 * i : 32 * (i + 1), :],
                    bank[:].rearrange("p c (w u b) -> p c u w b", u=2, b=2),
                )

        def turn_back(x):
            woven = at(woven0_at + 8 * KIB * x, [P, half * PACK], BF16, f"woven0_{x}")
            words = turned[:].rearrange("p c u w b -> p (c u w b)").bitcast(F32).rearrange("p (c u w) -> p c u w", u=2, w=P)
            for q in range(half // (2 * P)):
                bank = psum.tile([P, 2, 2, P], F32, name="turned_back", tag=f"bank{BACK_BANKS[x][q]}")
                for c in range(2):
                    for u in range(2):
                        nc.tensor.transpose(bank[:, c, u, :], words[:, 8 * x + 2 * q + c, u, :], identity[:])
                nc.scalar.copy(
                    woven[:].bitcast(F32)[:, q * BANK : (q + 1) * BANK].rearrange("p (c m u) -> p c m u", c=2, u=2),
                    bank[:].rearrange("p c u m -> p c m u"),
                )
            return woven

        def round_to_pairs(i):
            t = BYTE_OF[i - PACK]
            if t == 2:
                both_places = page[i][:].unsqueeze(2).to_broadcast([P, T2, 2])
                nc.gpsimd.tensor_scalar(pairs[:, 1, :, :], both_places, 1.0, 0.0, ALU.mult, ALU.add)
            else:
                nc.scalar.copy(pairs[:, 0, :, t], page[i][:])

        def weave(cols, offset, name):
            woven = at(offset, [P, (cols.stop - cols.start) * PACK], BF16, name)
            words = pairs[:].rearrange("p u m b -> p (u m b)").bitcast(U32).rearrange("p (u m) -> p m u", u=2)
            nc.scalar.copy(woven[:].bitcast(U32).rearrange("p (m u) -> p m u", u=2), words[:, cols, :])
            return woven

        p_c = [held([P, T2], U32, f"p_c{g}") for g in range(GROUPS)]
        last_scales = held([P, T2], U8, "p_s1")
        p_s = {(1, x): last_scales[:, x * half : (x + 1) * half] for x in range(2)}

        def scales_of(g, cols):
            x, lo = divmod(cols.start, half)
            return p_s[g, x][:, lo : lo + cols.stop - cols.start]

        w3_c = held([P, GROUPS * N], U32, "w3_c")

        def quantise_page(g, cols, woven):
            nc.vector.quantize_mx(p_c[g][:, cols].bitcast(FP8X4), scales_of(g, cols), woven)

        def store_words(g, cols):
            nc.sync.dma_start(out_2[g].rearrange("p m t -> p (m t)").bitcast(I32)[:, cols], p_c[g][:, cols].bitcast(I32))

        def store_scales(g, cols, scales):
            for q in range(QUADRANTS):
                nc.sync.dma_start(out_3[g, 4 * q : 4 * q + 4, cols].bitcast(I32), scales[32 * q : 32 * q + 4, :].bitcast(I32))

        nc.vector.tensor_copy(v_s[:], tab_s[:].indirect(idx[:]))
        front = at(ring_at + 8 * KIB, [P, P, PACK], BF16, "w1_rounded0")
        nc.scalar.copy(*walk(front[:], w1_front[:]))
        quantise_w1(slice(0, P), front)
        for cols in parts:
            nc.vector.tensor_copy(v_w[:, cols], tab_w[:].indirect(list_part(idx, cols)))
        back_at = head_at + PASS - TOUCH
        opening_places = [ring_at, ring_at + KIB, back_at + KIB - TOUCH]
        opening = []
        for j, cols in enumerate(parts):
            copied = at(copies_at + 4 * cols.start, [P, cols.stop - cols.start], F32, f"opening_first{j}")
            nc.scalar.copy(copied[:], w1_product(0, cols, OPENING_BANKS[j][0])[:])
            opening.append((cols, copied, w2_product(0, cols, OPENING_BANKS[j][1])))

        def opening_larger(j):
            cols, copied, in_psum = opening[j]
            out = at(opening_places[j], [P, cols.stop - cols.start], F32, f"opening{j}")
            nc.vector.tensor_tensor(out[:], in_psum[:], copied[:], ALU.max)
            return out

        def opening_scatter(j, values):
            cols = parts[j]
            nc.vector.tensor_tensor(page[0][:].indirect(list_part(idx2, cols)), values[:], plain_gain[:, cols], ALU.mult)

        opening_scatter(0, opening_larger(0))
        opening_scatter(1, opening_larger(1))
        back = [at(place, [P, (j + 1) * P, PACK], BF16, f"w1_back_rounded{j}") for j, place in enumerate((back_at, ring_at + 4 * KIB))]
        for j in range(2):
            nc.scalar.copy(*walk(back[j][:], w1_back[:, :, j * P : (2 * j + 1) * P]))
        w1_scales[1] = at(raw_at, [P, P], U8, "w1_s1")[:]
        nc.vector.quantize_mx(w1_c[:, P : 2 * P].bitcast(FP8X4), w1_scales[1], back[0][:].rearrange("p c j -> p (c j)"))
        quantise_w1(slice(2 * P, PASS), back[1])
        last_part = opening_larger(2)
        w2_ds = at(head_at, [P, PASS], U8, "w2_ds")
        w2_scales_used.append(w2_ds)
        nc.vector.tensor_copy(w2_ds[:].rearrange("p (t m) -> p t m", t=PACK), w2_s[:, PASS:].rearrange("p (m t) -> p t m", t=PACK))
        opening_scatter(2, last_part)
        store_page(0)
        late = [at(late_w1_at + 2 * KIB * j, [P, 2 * P, PACK], BF16, f"w1_late_rounded{j}") for j in range(2)]
        for j in range(2):
            nc.scalar.copy(
                late[j][:].rearrange("p (t m) j -> p m j t", t=2),
                w1_late[:].rearrange("p j (m t) -> p m j t", t=PACK)[:, :, :, 2 * j : 2 * j + 2],
            )
        for i in range(1, ON_VECTOR):
            one_copied(i, early_places[i])
        nc.scalar.copy(
            w2_dw[:].bitcast(U16).rearrange("p (t m) -> p t m", t=PACK),
            w2_w[1][:].bitcast(U16).rearrange("p (m t) -> p t m", t=PACK),
        )
        for j in range(2):
            quantise_w1(slice(PASS + 2 * P * j, PASS + 2 * P * (j + 1)), late[j])
        for i in range(1, ON_VECTOR):
            larger(i)
        weighed1 = at(early_places[1], [P, S], F32, "weighed1")
        for cols in halves:
            nc.gpsimd.tensor_tensor(weighed1[:, cols], value[1][:, cols], plain_gain[:, cols], ALU.mult)
        for cols in halves:
            nc.vector.tensor_copy(page[1][:].indirect(list_part(idx2, cols)), weighed1[:, cols])
        store_page(1)
        weigh(2)
        scatter(2)
        both_copied(ON_VECTOR)
        excess(ON_VECTOR)
        turn(0)
        both_copied(ON_VECTOR + 1)
        larger3 = value[3]
        value[3] = at(spare_at, [P, S], F32, "weighed3")
        nc.gpsimd.tensor_tensor(value[3][:], larger3[:], plain_gain[:], ALU.mult)
        scatter(3)
        for i in range(ON_VECTOR, LAST):
            add_first(i)
            excess(i + 1)
            turn(i - ON_VECTOR + 1)
            if i + 2 < TILES:
                both_copied(i + 2)
            weigh(i)
            scatter(i)
        w3_rounded = at(late_w1_at + 2 * TOUCH, [P, GROUPS * N, PACK], BF16, "w3_rounded")
        for g in range(GROUPS):
            for n in range(NT):
                nc.scalar.copy(*walk(w3_rounded[:, g * N + n * P : g * N + (n + 1) * P, :], w3_raw[g][:, :, n * P : (n + 1) * P]))
        page_halves = [slice(x * half, (x + 1) * half) for x in range(2)]
        woven0 = [turn_back(x) for x in range(2)]
        last_sum = [at(pairs_at + 4 * KIB, [P, BANK], F32, "last_sum")[:], value[LAST][:, halves[1]]]
        for u in range(HALVES):
            nc.gpsimd.tensor_tensor(last_sum[u], value[LAST][:, halves[u]], first[LAST][:, halves[u]], ALU.add)
        last_value = [at(place, [P, BANK], F32, f"last_value{u}") for u, place in enumerate((late_at + KIB, raw_at - 2 * KIB + TOUCH))]
        for u in range(HALVES):
            nc.gpsimd.tensor_tensor(last_value[u][:], last_sum[u], factor(LAST)[:, halves[u]], ALU.mult)
        pairs = at(pairs_at - TOUCH, [P, 2, T2, 2], BF16, "pairs")
        for i in range(PACK, LAST):
            round_to_pairs(i)

        def scatter_half(u):
            nc.vector.tensor_copy(page[LAST][:].indirect(list_part(idx2, halves[u])), last_value[u][:])

        scatter_half(0)
        w3_s = at(late_at + 5 * KIB // 2, [P, GROUPS * N], U8, "w3_s")

        def quantise_w3(cols):
            nc.vector.quantize_mx(w3_c[:, cols].bitcast(FP8X4), w3_s[:, cols], w3_rounded[:, cols, :].rearrange("p n j -> p (n j)"))

        quantise_w3(slice(0, BANK))
        p_s[0, 0] = at(late_at + KIB // 2, [P, half], U8, "p_s00")[:]
        quantise_page(0, page_halves[0], woven0[0][:])
        store_words(0, page_halves[0])
        store_scales(0, page_halves[0], p_s[0, 0])

        def halved(cols):
            middle = (cols.start + cols.stop) // 2
            return [slice(cols.start, middle), slice(middle, cols.stop)]

        chunks = [slice(c * BANK, (c + 1) * BANK) for c in range(CHUNKS)]
        ending = halved(chunks[-1])[:1] + halved(halved(chunks[-1])[1])
        units = [(cols, n) for cols in chunks for n in range(NT)][:-1] + [(cols, NT - 1) for cols in ending]
        pieces = halved(chunks[0]) + chunks[1:]
        spans = [chunks[0], chunks[-1], slice(BANK, 3 * BANK)]
        places = [woven1_at, woven1_at + 4 * KIB, woven0_at]
        woven1 = [weave(cols, place, f"woven1_{cols.start}") for cols, place in zip(spans, places)]

        def woven_part(cols):
            j = [span.start <= cols.start < span.stop for span in spans].index(True)
            return woven1[j][:, PACK * (cols.start - spans[j].start) : PACK * (cols.stop - spans[j].start)]

        scatter_half(1)
        quantise_w3(slice(BANK, GROUPS * N))
        nc.sync.dma_start(tile_rows(out_1, LAST), page[LAST][:])
        staged = [at(raw_at + n * 8 * KIB, [P, T2], F32, f"staged{n}") for n in range(NT)]
        root_places = [region + 2 * KIB * j for region in (tab_at, ring_at) for j in range(ROOT_BUFFERS // 2)]
        d_of = {}
        f_of = {}

        def d_pass(k, g):
            cols, n = units[k]
            if g == 0:
                d_of[k] = psum.tile([P, cols.stop - cols.start], F32, name="d", tag=f"bank{BANKS[sums.index((d_pass, k)) % len(BANKS)]}")
            nc.tensor.matmul_mx(
                d_of[k][:], lhsT=w4_w[:, g, n * P : (n + 1) * P].bitcast(FP8X4), lhsT_scale=w4_s[:, g, n * P : (n + 1) * P],
                rhs=p_c[g][:, cols].bitcast(FP8X4), rhs_scale=scales_of(g, cols), start=(g == 0), stop=(g == GROUPS - 1),
            )

        def f_pass(k, g):
            cols, n = units[k]
            if g == 0:
                f_of[k] = psum.tile([P, cols.stop - cols.start], F32, name="f", tag=f"bank{BANKS[sums.index((f_pass, k)) % len(BANKS)]}")
            wcols = slice(g * N + n * P, g * N + (n + 1) * P)
            nc.tensor.matmul_mx(
                f_of[k][:], lhsT=w3_c[:, wcols].bitcast(FP8X4), lhsT_scale=w3_s[:, wcols],
                rhs=p_c[g][:, cols].bitcast(FP8X4), rhs_scale=scales_of(g, cols), start=(g == 0), stop=(g == GROUPS - 1),
            )

        def store_unit(k, left, right):
            cols, n = units[k]
            engine = nc.gpsimd if k % 2 == 1 and k < len(units) - 3 else nc.vector
            engine.tensor_tensor(staged[n][:, cols], left[:], right[:], ALU.mult)
            nc.sync.dma_start(out_0[n * P : (n + 1) * P, cols], staged[n][:, cols])

        def damp(k):
            cols, n = units[k]
            width = cols.stop - cols.start
            scratch = at(copies_at + 2 * KIB * (k % COPY_BUFFERS), [P, width], F32, f"scratch{k}")
            root = at(root_places[k % ROOT_BUFFERS], [P, width], F32, f"root{k}")
            nc.scalar.activation(scratch[:], d_of[k][:], ACT.Square)
            nc.scalar.activation(root[:], scratch[:], ACT.Abs_reciprocal_sqrt, bias=1.0)
            if k >= len(units) - 2:
                nc.scalar.activation(scratch[:], root[:], ACT.Square)
                store_unit(k, f_of[k], scratch)
                return []
            nc.vector.tensor_tensor(scratch[:], f_of[k][:], root[:], ALU.mult)
            return [(k, scratch, root)]

        def fill(cols, copy):
            copy(woven_part(cols).rearrange("p (m t) -> p m t", t=PACK)[:, :, PACK - 1], page[LAST][:, cols])

        def quantise_piece(j):
            cols = pieces[j]
            quantise_page(1, cols, woven_part(cols))
            if cols.stop % BANK == 0:
                store_words(1, slice(cols.stop - BANK, cols.stop))

        sums = [(d_pass, k) for k in range(D_LEAD)]
        for k in range(len(units)):
            sums.append((f_pass, k))
            if k + D_LEAD < len(units):
                sums.append((d_pass, k + D_LEAD))
        for one_pass, k in sums[: len(BANKS)]:
            one_pass(k, 0)
        shared = 3 * BANK - P
        fill(pieces[0], nc.vector.tensor_copy)
        fill(pieces[1], nc.vector.tensor_copy)
        fill(pieces[4], nc.scalar.copy)
        fill(slice(shared, 3 * BANK), nc.scalar.copy)
        quantise_piece(0)
        quantise_piece(1)
        fill(pieces[2], nc.vector.tensor_copy)
        fill(slice(2 * BANK, shared), nc.vector.tensor_copy)
        quantise_piece(2)
        quantise_piece(4)
        quantise_piece(3)
        p_s[0, 1] = at(woven0_at, [P, half], U8, "p_s01")[:]
        quantise_page(0, page_halves[1], woven0[1][:])
        store_words(0, page_halves[1])
        store_scales(0, page_halves[1], p_s[0, 1])
        store_scales(1, slice(0, T2), last_scales[:])
        waiting = []
        for place, (one_pass, k) in enumerate(sums):
            if place >= len(BANKS):
                one_pass(k, 0)
            one_pass(k, 1)
            if one_pass != f_pass:
                continue
            following = damp(k)
            for earlier, part, root in waiting:
                store_unit(earlier, part, root)
            waiting = following
